import numpy as np, ml_dtypes
CORES = [48,51,52,55]
N = 4
BF = ml_dtypes.bfloat16
def gentries(a):
    return np.ascontiguousarray(a.reshape(8, 16, -1).transpose(0, 2, 1)).reshape(8, -1)
def gtable(e):
    e = np.asarray(e); return np.ascontiguousarray(e.reshape(8, -1, 16).transpose(0, 2, 1)).reshape(128, -1).astype(np.int32)
M, NC, R, L, S, D = 3072, 1024, 64, 192, 3, 1
def mag(rng, shape, lo, hi):
    return lo + (hi - lo) * rng.random(shape)
def thin(rng, y):
    k = rng.integers(0, 16, y.shape); low = mag(rng, y.shape, 1.0, 2.0) * np.exp2(rng.choice(np.array([-20.0, -12.0, -10.0, -8.0, -7.0, -6.0, -5.0]), y.shape))
    return np.where(k == 0, 0.0, np.where(k < 4, low, y))
def parts(rng):
    return {"X": rng.integers(-7, 8, (N, 8, 16, M)), "E": mag(rng, (N, 8, 16, M), 0.5, 2.0), "XR": rng.integers(-7, 8, (N, 8, 16, R)), "ER": mag(rng, (N, 8, 16, R), 0.5, 1.0),
            "HC": rng.integers(0, M, (N, 8, 16, NC)), "TC": rng.integers(0, M, (N, 8, 16, NC)), "NH": rng.integers(0, M, (N, 8, 16, S, L)), "NT": rng.integers(0, M, (N, 8, 16, S, L)),
            "h": rng.integers(0, M, (N, 8, L)), "p": rng.integers(0, R, (N, 8, L)), "t": rng.integers(0, M, (N, 8, L))}
def pack(d):
    b = lambda v: np.ascontiguousarray(v.reshape(N, 128, -1)).astype(np.float32).astype(BF)
    i = lambda v: np.ascontiguousarray(v.reshape(N, 128, -1)).astype(np.int32)
    l = lambda v: np.stack([gtable(a) for a in v])
    return {"xe": b(d["X"]), "ee": b(d["E"]), "xr": b(d["XR"]), "er": b(d["ER"]), "hc": i(d["HC"]), "tc": i(d["TC"]), "nh": i(d["NH"]), "nt": i(d["NT"]), "hl": l(d["h"]), "rl": l(d["p"]), "tl": l(d["t"])}
def setup_inputs(rng):
    return pack(parts(rng))
def setup_inputs_spread(rng):
    d = parts(rng)
    full = mag(rng, (N, 8, 16, M), 0.25, 1.0) * np.exp2(rng.choice(np.array([-1.0, -1.0, -1.0, -1.0, -1.0, -1.0, 0.0, 1.0]), (N, 8, 1, M)))
    d["E"] = thin(rng, full); d["E"][:, :, 0] = full[:, :, 0]; d["ER"] = thin(rng, d["ER"])
    amp = rng.choice(np.array([1, 2, 4, 7]), (N, 8, 1, M)); d["X"] = rng.integers(0, 2 ** 20, (N, 8, 16, M)) % (2 * amp + 1) - amp
    low = lambda n, shape: np.minimum((n * rng.random(shape) ** 2).astype(np.int64), n - 1)
    for k in ("HC", "TC", "NH", "NT", "h", "t"): d[k] = low(M, d[k].shape)
    d["p"] = low(R, d["p"].shape)
    g = int(rng.integers(0, 8)); o = rng.permutation(M)
    cold = np.zeros(M, bool); cold[o[:2 * NC]] = True
    d["E"][:, g] = np.where(cold, mag(rng, (N, 16, M), 0.1875, 0.3125), mag(rng, (N, 16, M), 1.75, 2.0)); d["ER"][:, g] = mag(rng, (N, 16, R), 0.875, 1.0)
    h = o[rng.integers(2 * NC, M, (N, L))]; t = o[rng.integers(2 * NC, M, (N, L))]; p = rng.integers(0, R, (N, L))
    d["h"][:, g] = h; d["t"][:, g] = t; d["p"][:, g] = p
    d["HC"][:, g] = o[:NC]; d["TC"][:, g] = o[NC:2 * NC]
    d["NH"][:, g] = o[(37 * p + t) & (NC - 1)][:, None, None, :]
    d["NT"][:, g] = np.roll(o[NC + ((37 * h + p) & (NC - 1))], D, axis=0)[:, None, None, :]
    return pack(d)
def setup_inputs_ends(rng):
    d = parts(rng); sign = lambda shape: 2 * rng.integers(0, 2, shape) - 1
    v = 7 * sign((2, 8, 16)); X = 7 * sign((N, 8, 16, M)); z = rng.integers(0, 8, (N, 8, 1, M))
    for j in range(4): X = np.where(z == j, (1 - 2 * (j & 1)) * v[j >> 1][None, :, :, None], X)
    for c, w in ((0, v[0]), (1, v[1]), (2, v[1]), (3, v[0]), (4, -v[0]), (5, -v[1]), (M - 4, v[0]), (M - 3, v[1]), (M - 2, v[0]), (M - 1, v[1])): X[..., c] = w
    both = np.sign(v[0] * v[1]) * 7; XR = 7 * sign((N, 8, 16, R)); XR[..., 0] = both; XR[..., R - 1] = -both
    twin = np.array([1, 2, 3, 4, 5, M - 2, M - 3, M // 2])
    ent = lambda shape: np.where(rng.random(shape) < 0.8, (M - 1) * rng.integers(0, 2, shape), twin[rng.integers(0, 8, shape)])
    for k in ("HC", "TC", "NH", "NT", "h", "t"): d[k] = ent(d[k].shape)
    p = np.where(rng.random((N, 8, L)) < 0.8, (R - 1) * rng.integers(0, 2, (N, 8, L)), rng.integers(0, R, (N, 8, L)))
    d["h"][..., L - 2:] = 0; d["t"][..., L - 2:] = M - 1; p[..., L - 1] = 0; p[..., L - 2] = R - 1
    kh = (37 * (R - 1) + M - 1) & (NC - 1); kt = (R - 1) & (NC - 1); kx = (M - 1) & (NC - 1)
    d["HC"][:, ::7, :, kh] = M - 4; d["NH"][:, ::7, :, 0, L - 2] = M - 4; d["TC"][:, ::7, :, kt] = M - 1; d["NT"][:, ::7, :, 0, L - 2] = M - 1
    d["HC"][:, 7, :14, kx] = 4; d["HC"][:, 7, 14, kx] = 3; d["HC"][:, 7, 15, kx] = 0; d["NH"][:, 7, :, 0, L - 1] = 4
    g = int(rng.integers(1, 7))
    d["E"][:, g] = mag(rng, (N, 16, M), 1.5, 2.0); d["E"][:, g, :, M - 1] = 2.0; d["ER"][:, g] = mag(rng, (N, 16, R), 0.75, 1.0); d["ER"][:, g, :, R - 1] = 1.0
    d["X"], d["XR"], d["p"] = X, XR, p
    return pack(d)
def setup_inputs_crowd(rng):
    d = parts(rng); o = rng.permutation(8); h, p, t = d["h"], d["p"], d["t"]; one = int(rng.integers(0, L))
    for g in (o[0], o[1]):
        for a in (h, p, t): a[:, g] = a[:, g, :1].copy()
    h[:, o[1], one] = (h[:, o[1], one] + 1 + rng.integers(0, M - 1, N)) % M; t[:, o[1], one] = (t[:, o[1], one] + 1 + rng.integers(0, NC - 1, N)) % M; p[:, o[1], one] = rng.integers(0, R, N)
    p[:, o[2]] = p[:, o[2], :1].copy(); t[:, o[2]] = t[:, o[2], :1] % NC + NC * rng.integers(0, M // NC, (N, L))
    for g in (o[3], o[4]):
        c = rng.choice(np.array([0, M - 1, M // 2, 17]), N)
        for k in ("HC", "TC"): d[k][:, g] = c[:, None, None]
        for k in ("NH", "NT"):
            keep = d[k][:, g, :, :, one].copy(); d[k][:, g] = c[:, None, None, None]
            if g == o[4]: d[k][:, g, :, :, one] = keep
    j = np.arange(L) & 1
    for a in (h, p, t): a[:, o[5]] = a[:, o[5]][:, j].copy()
    b = rng.integers(0, NC, (2, N, 1)); inv = pow(37, -1, NC)
    t[:, o[6]] = (b[0] - 37 * p[:, o[6]]) & (NC - 1); h[:, o[6]] = ((b[1] - p[:, o[6]]) * inv) & (NC - 1)
    return pack(d)
def setup_inputs_ties(rng):
    d = parts(rng); o = rng.permutation(8); X, XR = d["X"], d["XR"]
    X[:, o[:2]] = rng.integers(-1, 2, (N, 2, 16, M)); XR[:, o[:2]] = rng.integers(-1, 2, (N, 2, 16, R))
    XR[:, o[2]] = XR[:, o[2]] * (rng.random((N, 1, R)) < 0.5)
    g = o[3]; H = M // 2; X[:, g, :, H:] = X[:, g, :, :H].copy()
    for r in range(N):
        q = (r + D) % N; kh = (37 * d["p"][r, g] + d["t"][r, g]) & (NC - 1); kt = (37 * d["h"][r, g] + d["p"][r, g]) & (NC - 1)
        d["NH"][r, g, ::2, 0] = (d["HC"][r, g][:, kh][::2] + H) % M; d["NT"][q, g, ::2, 0] = (d["TC"][q, g][:, kt][::2] + H) % M
    for g in (o[4], o[5]):
        v = 2 * rng.integers(0, 2, (15, 1)) - 1
        X[:, g, :15] = 7 * v; XR[:, g, :15] = 7; XR[:, g, 15] = 2 * rng.integers(0, 2, (N, R)) - 1
    for k in ("HC", "TC"): d[k][:, o[6]] = d[k][:, o[6], :1].copy()
    return pack(d)
def setup_inputs_full(rng):
    d = parts(rng); kind = rng.permutation(8); sign = lambda shape: 2 * rng.integers(0, 2, shape) - 1; take = lambda a, i: np.take_along_axis(a, i, 2)
    w = 1 - 2 * (kind & 1); run = (kind >> 2) == 1; head = ((np.arange(N)[:, None] + ((kind >> 1) & 1)) & 1) == 0
    F = M - NC; dp = F + np.argsort(rng.random((N, 8, NC)), axis=-1); fp = np.argsort(rng.random((N, 8, F)), axis=-1)
    sg = np.ones((N, 8, M), np.int64); np.put_along_axis(sg, dp[..., NC // 2:], -1, 2); np.put_along_axis(sg, fp[..., F // 2:], -1, 2)
    v = sign((N, 8, 16)); X = 7 * v[..., None] * sg[:, :, None, :]; dent = np.arange(16)[:, None] == rng.integers(0, 16, (N, 8, 1, NC))
    X[..., F:] = np.where(dent, 6 * v[..., None] * sg[:, :, None, F:], X[..., F:])
    sp = sign((N, 8, R)); XR = 7 * (v * np.roll(v, -D, axis=0))[..., None] * sp[:, :, None, :]
    p = d["p"]; keys = np.argsort(rng.random((2, N, 8, NC)), axis=-1)[..., :L]; block = NC * rng.integers(0, M // NC - 1, (2, N, 8, L)); inv = pow(37, -1, NC)
    t = ((keys[0] - 37 * p) & (NC - 1)) + block[0]; h = (((keys[1] - p) * inv) & (NC - 1)) + block[1]
    cut = rng.random((N, 8, L)) < 0.3; cut[..., 0] = True
    first = np.maximum.accumulate(np.where(cut, np.arange(L), 0), axis=-1); own = np.where(run[None, :, None], first, np.arange(L)); up = (w > 0)[None, :, None]
    for tail in (0, 1):
        need = w[None, :, None] * take(sp, p) * take(np.roll(sg, -D * (1 - tail), axis=0), h if tail else t); neg = (need < 0).astype(np.int64); slot = own + L * tail
        dented = take(np.roll(dp, -D * tail, axis=0), slot + (NC // 2) * neg)
        whole = [take(np.roll(fp, -D * tail, axis=0), slot + 2 * L * e + (F // 2) * neg) for e in (0, 1)]
        good = [np.where(up, y, dented)[:, :, None, :] for y in whole]; poor = [np.where(up, dented, y)[:, :, None, :] for y in whole]
        star = np.arange(16)[:, None] == rng.integers(1, 16, (N, 8, 1, L)); m = rng.random((2, N, 8, 16, L)) < 0.2
        m[:, :, :, 0] = False; m[0] &= ~star; m[1] |= star; m &= (head == (tail == 0))[None, :, :, None, None]
        z = rng.integers(0, 2, (2, N, 8, 16, L)) == 1
        c = np.roll(np.where(m, np.where(z, good[1], good[0]), np.where(z, poor[1], poor[0])), D * tail, axis=1)
        k = np.roll(keys[tail], D * tail, axis=0)
        np.put_along_axis(d["TC" if tail else "HC"], np.broadcast_to(k[:, :, None, :], (N, 8, 16, L)), c[0], 3)
        d["NT" if tail else "NH"][:, :, :, 0] = c[1]
    d["X"], d["XR"], d["h"], d["t"] = X, XR, h, t
    return pack(d)
def check_ranges(d):
    bad = []
    for k, lo, hi in (("xe", -7, 7), ("xr", -7, 7), ("hc", 0, M - 1), ("tc", 0, M - 1), ("nh", 0, M - 1), ("nt", 0, M - 1), ("hl", 0, M - 1), ("rl", 0, R - 1), ("tl", 0, M - 1)):
        v = np.asarray(d[k]).astype(np.float64)
        if not np.all((v >= lo) & (v <= hi) & (v == np.rint(v))): bad.append("range of " + k)
    for k, hi in (("ee", 2.0), ("er", 1.0)):
        v = np.asarray(d[k]).astype(np.float64)
        if not np.all((v == 0) | ((v >= 2.0 ** -20) & (v <= hi))): bad.append("range of " + k)
        if k == "ee" and not np.all(v[:, ::16] >= 0.125): bad.append("least value of feature 0 in ee")
    return bad
def pick(tab, ix):
    return np.take_along_axis(tab, ix.reshape(8, 1, -1), 2)
def side(x, e, c, key, n, u, v):
    a = pick(c, key)
    score = lambda m: np.add.reduce(pick(x, m).reshape(8, 16, 16, L) * u[:, :, None, :], axis=1)
    sa, sn = score(a), score(n); won = sn > sa; a = np.where(won, n, a); s = np.where(won, sn, sa)
    ea = pick(e, a).reshape(8, 16, 16, L)
    w = np.reciprocal(1.0 + np.exp(-0.0625 * np.add.reduce(ea * v[:, :, None, :], axis=1))); G = np.add.reduce(w[:, None] * ea, axis=2)
    k = np.argmax(s, axis=1)[:, None, :]; best = lambda y: np.take_along_axis(y, k, 1)[:, 0]
    b = best(a); nx = np.clip(pick(x, b) - np.sign(u), -7, 7); ne = 0.875 * pick(e, b) + 0.125 * best(w)[:, None] * v
    return a, G, best(s), b, nx, ne
def put(tab, key, live, new):
    for g in range(8):
        lanes = np.nonzero(live[g])[0]; names, i = np.unique(key[g][lanes], return_index=True)
        tab[g][:, names] = new[g][:, lanes[i]]
def reference(xe, ee, xr, er, hc, tc, nh, nt, hl, rl, tl):
    whole = lambda y: y.astype(np.float32).astype(np.int64).reshape(N, 8, 16, -1)
    X, XR = whole(xe), whole(xr); E = ee.astype(np.float64).reshape(N, 8, 16, M); ER = er.astype(np.float64).reshape(N, 8, 16, R)
    HC = hc.astype(np.int64).reshape(N, 8, 16, NC); TC = tc.astype(np.int64).reshape(N, 8, 16, NC)
    NH = nh.astype(np.int64).reshape(N, 8, 16, S, L); NT = nt.astype(np.int64).reshape(N, 8, 16, S, L)
    h, p, t = [np.stack([gentries(a) for a in y]).astype(np.int64) for y in (hl, rl, tl)]
    yh = np.zeros((N, 8, 16, L)); yt = np.zeros((N, 8, 16, L)); every = np.ones((8, L), bool)
    for s in range(S):
        kh = (37 * p + t) & (NC - 1); kt = (37 * h + p) & (NC - 1); hs, ts = [], []
        for r in range(N):
            q = (r + D) % N
            xp, ep = pick(XR[r], p[r]), pick(ER[r], p[r])
            hs.append(side(X[r], E[r], HC[r], kh[r], NH[r][:, :, s], xp * pick(X[q], t[r]), ep * pick(E[q], t[r])))
            ts.append(side(X[q], E[q], TC[q], kt[r], NT[q][:, :, s], pick(X[r], h[r]) * xp, pick(E[r], h[r]) * ep))
            yh[r] += hs[r][1]; yt[q] += ts[r][1]
        if s == S - 1: break
        head = [hs[r][2] >= ts[r][2] for r in range(N)]
        for r in range(N):
            put(HC[r], kh[r], every, hs[r][0]); put(X[r], hs[r][3], head[r], hs[r][4]); put(E[r], hs[r][3], head[r], hs[r][5])
        for r in range(N):
            q = (r + D) % N
            put(TC[q], kt[r], every, ts[r][0]); put(X[q], ts[r][3], ~head[r], ts[r][4]); put(E[q], ts[r][3], ~head[r], ts[r][5])
            h[r] = np.where(head[r], hs[r][3], h[r]); t[r] = np.where(head[r], t[r], ts[r][3])
    return {"yh": yh.reshape(N, 128, L).astype(np.float32), "yt": yt.reshape(N, 128, L).astype(np.float32)}

def check_inputs(d):
    bad = list(check_ranges(d))
    if not bad:
        for name, y in reference(**d).items():
            for q in range(N):
                v = np.abs(np.asarray(y[q], np.float64)); s = np.sqrt(np.mean(v * v))
                if v.max() > 4 * s or s < 2.0 ** 2: bad.append('%s of rank %d is uneven or too small' % (name, q))
    return bad

@@ -1,0 +1,649 @@
+from concourse.bass import DstId, RemoteDMATransfer
+from concourse.mybir import AluOpType as A, ActivationFunctionType as F
+
+M, L, S, NC = 3072, 192, 3, 1024
+EO = M + 32
+NW = NC + 16
+BIG = float(1 << 20)
+UPA = 8192
+f32, bf, i32, u16, f16 = "float32", "bfloat16", "int32", "uint16", "float16"
+
+
+def _sb(n, d):
+    return ("sbuf", [128, n], d)
+
+
+SCRATCH = {
+    "XB": _sb(EO, bf), "TB": _sb(EO, f32), "CT": _sb(2 * NW, i32), "EN": ("sbuf", [128, 3, 384], i32),
+    "ENO": _sb(1152, u16), "LN": _sb(36, i32), "RL": _sb(36, i32), "XR": _sb(64, bf), "ER": _sb(64, bf),
+    "XP": _sb(384, bf), "EP": _sb(384, bf), "OW": _sb(72, f32), "OT": _sb(72, f32), "KA": _sb(24, f32), "KB": _sb(24, f32),
+    "KC": _sb(24, f32), "K1": _sb(24, f32), "K2": _sb(24, i32), "K3": _sb(24, i32), "KF": _sb(24, f32), "KO": _sb(24, u16),
+    "K16": _sb(24, f16), "PO": _sb(12, u16), "OO": _sb(24, u16), "CO": _sb(384, u16), "DF": _sb(384, f32),
+    "XG0": ("sbuf", [128, 2, M], bf), "XG1": ("sbuf", [128, 2, M], bf), "UP": _sb(12304, bf),
+    "EG0": _sb(6144, f32), "EG1": _sb(6144, f32), "PE": _sb(6144, f32), "ENS": _sb(1152, f16),
+    "HA": ("sbuf", [128, 24, 16], f32), "SV": ("sbuf", [128, 24, 16], f32), "MX": _sb(192, f32), "LB": _sb(384, bf),
+    "LT": ("sbuf", [128, 24, 16], bf), "AL": _sb(384, f16), "AO": _sb(384, u16), "YB": _sb(384, f16), "ZS": _sb(384, f32),
+    "SK": _sb(384, f32), "BO": _sb(24, u16), "SG": _sb(384, bf), "CI": _sb(64, f32), "CZ": ("sbuf", [128, 4, 16], bf),
+    "MG": _sb(8, f32), "IDB": _sb(128, bf), "IDF": _sb(128, f32), "SC": ("psum", [128, 48, 2, 16], f32),
+    "XS": _sb(384, bf), "EV": _sb(384, f32), "E7": _sb(384, f32),
+    "MI": _sb(24, f32), "BD": _sb(24, f32), "DO": _sb(24, f32), "T1": _sb(24, f32),
+    "T2": _sb(24, f32), "T3": _sb(24, f32), "T4": _sb(24, f32), "T5": _sb(24, f32), "B16": _sb(24, f16), "SD": _sb(384, f32),
+    "ND": _sb(24, f32), "SO": _sb(48, u16), "NE": _sb(24, f32), "C1": _sb(24, f32), "C2": _sb(24, f32),
+    "CSO": _sb(48, u16), "QX": _sb(384, f32), "R": _sb(408, f32), "RH0": _sb(408, bf), "RO0": _sb(408, f16),
+    "RH1": _sb(408, bf), "RO1": _sb(408, f16), "GS": _sb(768, f32), "GT": _sb(384, f32),
+    "ACC": _sb(384, f32),
+    "PI": _sb(8, i32), "PJ": _sb(8, i32), "PC": _sb(16, f32), "IC": _sb(160, f32), "IG": _sb(128, f32), "PRI": _sb(384, bf),
+    "EXI": _sb(24, i32), "EXO": _sb(24, u16), "W": _sb(160, bf), "PW0": _sb(160, bf), "PW1": _sb(160, bf),
+    "ONE": _sb(128, f32), "RM": _sb(384, f32), "DM": _sb(384, f32), "SEL": _sb(2048, bf), "DD": _sb(2048, bf),
+}
+for _s in range(S):
+    SCRATCH["U%d" % _s] = _sb(384, bf)
+    SCRATCH["V%d" % _s] = _sb(384, f32)
+    SCRATCH["UO%d" % _s] = _sb(384, bf)
+    SCRATCH["VO%d" % _s] = _sb(384, f32)
+for _s in range(S - 1):
+    SCRATCH["MS%d" % _s] = _sb(48, i32)
+    SCRATCH["RX%d" % _s] = _sb(48, i32)
+for _s in (2, 4, 5, 6, 7):
+    SCRATCH["P%d" % _s] = ("psum", [128, 512], f32)
+
+SEMAPHORES = ["cg", "cv", "ca", "cp", "sent", "ldL", "ldR", "ldX", "ldC", "ldN", "ldTE", "out0", "out1",
+              "arL", "arP", "arU0h", "arU0t", "arU1", "arU2", "arV0", "arV1", "arV2", "arM0", "arM1"]
+CNT = {"g": "cg", "v": "cv", "a": "ca", "p": "cp"}
+PEC, HOP = 0.6, 70
+TUNE = {'bias': 20000, 'patience': 1.0, 'turns': 3, 'shy': 1000}
+TUNE.update((k + s, 20) for s in "01" for k in ("EV", "z3p", "z3a", "z3v", "E"))
+TUNE.update((k + s, 30) for s in "01" for k in ("ZS", "QX", "z5a", "RH", "z5p", "R", "Rl", "RO", "vp"))
+TUNE.update((k + "s", 30) for k in ("PO", "OO", "XP", "EP", "UO", "K", "KF", "KO", "CO", "ENO", "OT", "OT0a", "KB", "KA", "KC", "d", "-"))
+TUNE.update({'PE0': -10, 'PE0h': -20, 'PE1': -10, 'PE1h': -10, 'rb0': 10, 'rb1': 10, 'GS2t': -20, 'GS2h': -20, 'GS0': -10,
+             'E1': 10, 'UP1h': 2, 'G1': 1, 'cv0': 5, 'AO1h': 2, 'TBE1': -15, 'cv1': 5, 'G2h': -20, 'UP2t': 10,
+             'UPas': 100, 'QX1': 31, 'POs': 25, 'T0': 25, 'LT2h': 2, 'OT1': -5, 'G0': 2, 'PE2h': -10, 'RH2h': 1})
+KEEP = set(['EG0h', 'EG0t', 'EG1t', 'RH1', 'UP0h', 'UP2h', 'XG2h', 'ZS0', 'vp0', 'vp1'])
+_ORDER = {}
+BASE = {"v": 84, "a": 450, "g": 900, "s": 100, "p": 40}
+COST = {"vUPa": 4100, "vUPb": 2100, "vSEL": 1050, "vENO": 404, "vENS": 404, "vXP": 350, "vEP": 350, "vUO": 650, "vVO": 650, "vCO": 650,
+        "vDF": 650, "vW": 180, "vIDF": 150, "vIDB": 150, "vPW": 180, "vONE": 150, "vRM": 404, "vDM": 404, "vHA": 404, "aHA": 450,
+        "vSV": 404, "vLB": 404, "vMX": 404, "vLT": 116, "vSK": 212, "vlo": 212, "vAL": 212, "vYB": 212, "vAO": 116, "vXS": 650,
+        "vEV": 650, "vz": 404, "vE": 404, "aE": 665, "vSD": 404, "vCT": 111, "vTBX": 111, "vTBE": 111, "vR": 404, "vRH": 430, "aRH": 475,
+        "vRO": 836, "vGS": 404, "vGT": 404, "vACC": 788, "aUP": 161, "vZS": 404, "aZS": 450, "vvp": 404, "avp": 450, "vQX": 404,
+        "aQX": 450, "vW8": 404, "aEN": 100, "aXR": 100, "gTBE": 700, "gPI": 140, "gIG": 390, "gIC": 450, "gCI": 260, "gEXI": 180,
+        "gSEL": 4300, "gDD": 4300}
+LATE = {"ldL": 2200, "ldN": 3500, "ldX": 4200, "ldR": 2500, "ldC": 6000, "ldTE": 6500}
+
+
+def _order(ops, raised):
+    n = len(ops)
+    pre = []
+    for e, fs, deps, dma, soft, cost, tag in ops:
+        p = []
+        for d in list(deps) + list(soft):
+            if d[0] == "e":
+                p.append((d[1], 0 if d in soft else HOP))
+            elif d[2]:
+                p += [(j, LATE.get(d[1], 2300)) for j in raised[d[1]]]
+        pre.append(p)
+    post = [[] for _ in ops]
+    for i in range(n):
+        for j, lag in pre[i]:
+            post[j].append((i, lag))
+    left = [len(p) for p in post]
+    prio = [0.0] * n
+    todo = [i for i in range(n) if not left[i]]
+    while todo:
+        i = todo.pop()
+        prio[i] = min(ops[i][5].values()) + max([prio[k] + lag for k, lag in post[i]] or [0])
+        for j, lag in pre[i]:
+            left[j] -= 1
+            if not left[j]:
+                todo.append(j)
+    for i in range(n):
+        if ops[i][3] and not pre[i]:
+            prio[i] = 1e9 - i
+        tag = ops[i][6]
+        prio[i] += 1000.0 * (TUNE.get(tag, 0) + (TUNE.get(tag[:-1], 0) if tag[-1] in "ht" else 0))
+    left = [len(p) for p in pre]
+    ready = {i: 0.0 for i in range(n) if not left[i]}
+    free = {e: 0.0 for e in BASE}
+    out, at, begin = [], [0.0] * n, [0.0] * n
+    while ready:
+        pick = None
+        for e in free:
+            cand = [i for i in ready if e in ops[i][5]]
+            if not cand:
+                continue
+            t = max(free[e], min(ready[i] for i in cand))
+            pr = {i: prio[i] - (TUNE["bias"] if e == "v" and len(ops[i][5]) > 1 else 0) for i in cand}
+            if e == "v":
+                cand = [i for i in cand if len(ops[i][5]) == 1 or ops[i][6] not in KEEP]
+                if not cand:
+                    continue
+                t = max(free[e], min(ready[i] for i in cand))
+            top = max(cand, key=lambda i: (pr[i] - max(0.0, ready[i] - t), -i))
+            if ready[top] > t:
+                gap = ready[top] - t
+                now = [i for i in cand if ready[i] <= t]
+                fits = [i for i in now if ops[i][5][e] <= gap + HOP]
+                if fits:
+                    top = max(fits, key=lambda i: (pr[i], -i))
+                else:
+                    b = max(now, key=lambda i: (pr[i], -i))
+                    if gap > TUNE["patience"] * (ops[b][5][e] - gap) or pr[top] - pr[b] < ops[b][5][e]:
+                        top = b
+            t = max(t, ready[top])
+            if pick is None or (t, ops[top][5][e]) < pick[0]:
+                pick = ((t, ops[top][5][e]), e, top)
+        (t, c), e, i = pick
+        del ready[i]
+        free[e] = t + c
+        out.append((i, e))
+        begin[i] = t
+        for k, lag in post[i]:
+            left[k] -= 1
+            at[k] = max(at[k], t + c + lag)
+            if not left[k]:
+                ready[k] = at[k]
+    best = (max(free.values()), out)
+
+    def pack(seq, before, on, choose):
+        busy, end, res = {e: [] for e in BASE}, [0.0] * n, {}
+        for i in seq:
+            t0, pick = max([end[j] + lag for j, lag in before[i]] or [0.0]), None
+            for e in (sorted(ops[i][5]) if choose else [on[i]]):
+                c, t, k, b = ops[i][5][e], t0, len(busy[e]), busy[e]
+                while k and b[k - 1][1] > t0:
+                    k -= 1
+                while k < len(b) and b[k][0] < t + c:
+                    t = max(t, b[k][1])
+                    k += 1
+                late = t + c + (TUNE["shy"] if e == "v" else 0)
+                if pick is None or late < pick[0]:
+                    pick = (late, t, c, e, k)
+            late, t, c, e, k = pick
+            busy[e].insert(k, (t, t + c))
+            end[i], res[i] = t + c, (t, e)
+        return end, res
+
+    on = dict(out)
+    end = [begin[i] + ops[i][5][on[i]] for i in range(n)]
+    for turn in range(TUNE["turns"]):
+        end, res = pack(sorted(range(n), key=lambda i: (-end[i], -i)), post, on, False)
+        end, res = pack(sorted(range(n), key=lambda i: (prio[i] < 5e8, -end[i], i)), pre, on, True)
+        on = {i: res[i][1] for i in res}
+        if max(end) < best[0]:
+            best = (max(end), [(i, on[i]) for i in sorted(range(n), key=lambda i: (res[i][0], i))])
+    return best[1], best[0]
+
+
+def rank_program(g, core, T, topo):
+    rank = T.rank_of(core)
+    if rank is None:
+        return
+    n = len(T.cores)
+    nxt, prv = T.cores[(rank + 1) % n], T.cores[(rank - 1) % n]
+    Q = {"g": g, "v": g.vector, "a": g.scalar, "p": g.tensor, "s": g.sync}
+    ops, wr, rd, bank, sent, raised, step = [], {}, {}, {}, [0], {}, ["s"]
+
+    def op(e, f, r="", w="", b="", dma=None, free=False, alt=None, c=None):
+        i = len(ops)
+        me = ("s",) + dma if dma else ("e", i)
+        deps, soft = set(), set()
+        for x in r.split():
+            deps.add(wr[x])
+        for x in w.split():
+            for d in [wr.get(x)] + rd.get(x, []):
+                if d:
+                    (soft if free else deps).add(d)
+        eng = "?%d" % i if alt else e
+        for x in b.split():
+            st = bank.setdefault(x, [None, [], []])
+            if st[0] != eng:
+                st[:] = [eng, [], st[1]]
+            deps.update(st[2])
+            if e == "p":
+                soft.update(st[1][-1:])
+            st[1].append(me)
+        deps.discard(me)
+        if e == "p":
+            soft.update(d for d in deps if d[0] == "e" and ops[d[1]][0] == "p")
+            deps -= soft
+        for x in r.split():
+            rd.setdefault(x, []).append(me)
+        for x in w.split():
+            wr[x] = me
+            rd[x] = []
+        if dma and dma[1]:
+            raised.setdefault(dma[0], []).append(i)
+        name = (w.split() or ["-"])[0].rstrip("0123456789_")
+        cost = {e: c or COST.get(e + name, BASE[e])}
+        fs = {e: f}
+        if alt:
+            fs["a"], cost["a"] = alt, COST["a" + name] if c is None else c + 15
+        ops.append((e, fs, deps, dma, soft, cost, (w[:2] + e if name == "z" else name) + step[0]))
+
+    def mask(dst, a, b):
+        return sum(1 << e for e in topo.engines(core, dst)[a:b])
+
+    def send(r, parts):
+        trs = []
+        for dst, src_ap, dst_ap, sem, a, b in parts:
+            rid, pid = topo.addr(dst)[:2]
+            trs.append(RemoteDMATransfer(dst_ids=[DstId(rid=rid, pnc=pid)], dma_engine_mask=mask(dst, a, b),
+                                         remote_sem=T.sem[sem], src=src_ap, dst=dst_ap))
+            sent[0] += b - a
+            raised.setdefault(sem, []).append(len(ops))
+        op("g", lambda q: q.remote_dma_fused(trs, local_sem=T.sem.sent), r=r, dma=("sent", 0))
+
+    def tt(out, a, b, o, r, w, bk="", c=None):
+        op("v", lambda q: q.tensor_tensor(out, a, b, o), r, w, bk, c=c)
+
+    def ts(out, a, s1, o0, r, w, bk="", s2=None, o1=None, c=None, alt=None):
+        if o1 is None:
+            op("v", lambda q: q.tensor_scalar(out, a, s1, None, o0), r, w, bk, c=c, alt=alt)
+        else:
+            op("v", lambda q: q.tensor_scalar(out, a, s1, s2, o0, o1), r, w, bk, c=c, alt=alt)
+
+    def cp(out, a, r, w, bk="", free=False, either=False, c=None):
+        op("v", lambda q: q.tensor_copy(out, a), r, w, bk, free=free, c=c,
+           alt=(lambda q: q.activation(out, a, F.Copy)) if either else None)
+
+    def ms(out, c, w):
+        op("v", lambda q: q.memset(out, c), "", w)
+
+    def scan(out, a, b, o0, o1, r, w, bk=""):
+        op("v", lambda q: q.tensor_tensor_scan(out, a, b, 0.0, o0, o1), r, w, bk)
+
+    def act(out, a, fn, r, w, bk="", bias=0.0, scale=1.0, c=None):
+        op("a", lambda q: q.activation(out, a, fn, bias=bias, scale=scale), r, w, bk, c=c)
+
+    def mm(out, l, m, st, sp, r, w, bk, c=64):
+        op("p", lambda q: q.matmul(out, l, m, st, sp), r, w, bk, c=c * PEC)
+
+    def dma(e, out, a, r, w, sem, val):
+        op(e, lambda q: q.dma_start(out, a), r, w, dma=(sem, val))
+
+    PS = {i: T["P%d" % i] for i in (2, 4, 5, 6, 7)}
+    TX_, TE_ = T.XB[:, 0:M], T.TB[:, 0:M]
+    for x, sem, val in (("RL", "arL", 8), ("XP1", "arP", 8), ("EP1", "arP", 8), ("U0_0", "arU0h", 16), ("U0_1", "arU0t", 8)):
+        wr[x] = ("s", sem, val)
+    for s in range(S):
+        wr["V%d" % s] = ("s", "arV%d" % s, 16)
+        if s:
+            wr["U%d_0" % s] = wr["U%d_1" % s] = ("s", "arU%d" % s, 16)
+            wr["RX%d" % (s - 1)] = ("s", "arM%d" % (s - 1), 16)
+
+    dma("g", TE_, T.ee[:], "", "TBE", "ldTE", 16)
+    dma("s", T.LN[:, 0:12], T.tl[:], "", "LN", "ldL", 48)
+    dma("s", T.LN[:, 12:24], T.hl[:], "", "LN", "ldL", 48)
+    dma("s", T.LN[:, 24:36], T.rl[:], "", "LN", "ldL", 48)
+    dma("a", T.EN[:, :, 192:384], T.nt[:], "", "EN", "ldN", 32)
+    dma("s", TX_, T.xe[:], "", "TBX", "ldX", 16)
+    dma("a", T.XR[:], T.xr[:], "", "XR", "ldR", 32)
+    dma("a", T.ER[:], T.er[:], "", "XR", "ldR", 32)
+    dma("a", T.EN[:, :, 0:192], T.nh[:], "", "EN", "ldN", 32)
+    dma("s", T.CT[:, NW:NW + NC], T.tc[:], "", "CT0 CT1", "ldC", 32)
+    dma("s", T.CT[:, 0:NC], T.hc[:], "", "CT0 CT1", "ldC", 32)
+    op("g", lambda q: q.iota(T.PI[:, 0:1], [[0, 1]], 0, 1), w="PI")
+    op("g", lambda q: q.iota(T.IG[:], [[16, 8], [0, 16]], 0, 0, allow_small_or_imprecise_dtypes=True), w="IG")
+    op("g", lambda q: q.iota(T.IC[:], [[1, 160]], 0, 0, allow_small_or_imprecise_dtypes=True), w="IC")
+    send("LN", [(nxt, T.LN[:], T.RL[:], "arL", 0, 8)])
+    op("g", lambda q: q.iota(T.CI[:], [[-1, 2], [0, 2], [-2, 16]], 31, 0, allow_small_or_imprecise_dtypes=True), w="CI")
+
+    ms(T.UP[:, 0:UPA], 0.0, "UPa")
+    ms(T.KA[:, 0:12], 1.0, "KA0"); ms(T.KA[:, 12:24], 37.0, "KA1"); ms(T.KC[:, 0:12], 0.0, "KC0"); ms(T.KC[:, 12:24], float(NW), "KC1")
+    ms(T.TB[:, M:EO], 0.0, "d0"); ms(T.XB[:, M:EO], 0.0, "d1"); ms(T.CT[:, NC:NW], 0, "d2"); ms(T.CT[:, NW + NC:2 * NW], 0, "d3")
+    ts(T.PJ[:, 0:1], T.PI[:, 0:1], 15, A.bitwise_and, "PI", "PJ0")
+    ts(T.PJ[:, 1:2], T.PI[:, 0:1], 4, A.arith_shift_right, "PI", "PJ1", s2=1, o1=A.bitwise_and)
+    cp(T.ENO[:, 0:384], T.EN[:, 0, :], "EN", "ENO0")
+    cp(T.PO[:], T.LN[:, 24:36], "LN", "PO")
+    cp(T.OO[:, 0:12], T.LN[:, 12:24], "LN", "OO0")
+    cp(T.XP[:, 0:L], T.XR[:, 0:64].indirect(T.PO[:, 0:12]), "XR PO", "XP0")
+    cp(T.EP[:, 0:L], T.ER[:, 0:64].indirect(T.PO[:, 0:12]), "XR PO", "EP0")
+    tt(T.UO0[:, 0:L], T.XB[:, 0:M].indirect(T.OO[:, 0:12]), T.XP[:, 0:L], A.mult, "TBX OO0 XP0", "UO0_0")
+    send("XP0 EP0 UO0_0", [(nxt, T.XP[:, 0:L], T.XP[:, L:384], "arP", 0, 4), (nxt, T.EP[:, 0:L], T.EP[:, L:384], "arP", 4, 8),
+                           (nxt, T.UO0[:, 0:L], T.U0[:, L:384], "arU0t", 8, 16)])
+    cp(T.PC[:, 0:1], T.PJ[:, 0:1], "PJ0", "PC0")
+    tt(T.PC[:, 1:2], T.PI[:, 0:1], T.PJ[:, 0:1], A.subtract, "PI PJ0", "PC1")
+    ts(T.PC[:, 2:3], T.PC[:, 1:2], 15.0, A.add, "PC1", "PC2")
+    ts(T.PC[:, 3:4], T.PI[:, 0:1], 16.0, A.add, "PI", "PC3")
+    cp(T.PC[:, 4:5], T.PJ[:, 1:2], "PJ1", "PC4")
+    ts(T.PC[:, 5:6], T.PJ[:, 1:2], -1.0, A.mult, "PJ1", "PC5", s2=1.0, o1=A.add)
+    ts(T.PC[:, 6:7], T.PJ[:, 0:1], float(M), A.add, "PJ0", "PC6")
+    ts(T.PC[:, 8:9], T.PJ[:, 0:1], float(M - 1568), A.add, "PJ0", "PC8")
+    ts(T.PC[:, 9:10], T.PJ[:, 0:1], float(NC), A.add, "PJ0", "PC9")
+    cp(T.OW[:, 0:12], T.LN[:, 12:24], "LN", "OW0a"); cp(T.OT[:, 0:12], T.LN[:, 0:12], "LN", "OT0a")
+    ts(T.KB[:, 0:12], T.LN[:, 24:36], 37.0, A.mult, "LN", "KB0")
+    ts(T.ONE[:], T.IG[:], T.PC[:, 1:2], A.is_equal, "IG PC1", "ONE")
+    ts(T.MG[:], T.ONE[:, 0:128:16], 32.0, A.mult, "ONE", "MG")
+    cp(T.OO[:, 12:24], T.RL[:, 0:12], "RL", "OO1")
+    cp(T.OT[:, 12:24], T.RL[:, 12:24], "RL OT0a", "OT0")
+    cp(T.KB[:, 12:24], T.RL[:, 24:36], "RL", "KB1")
+
+    def keys(s):
+        tt(T.K1[:], T.OT[:, 24 * s:24 * s + 24], T.KA[:], A.mult, "OT%d KA0 KA1" % s, "K1")
+        tt(T.K2[:], T.K1[:], T.KB[:], A.add, "K1 KB0 KB1", "K2")
+        ts(T.K3[:], T.K2[:], NC - 1, A.bitwise_and, "K2", "K3")
+        tt(T.KF[:], T.K3[:], T.KC[:], A.add, "K3 KC0 KC1", "KF")
+        cp(T.KO[:], T.KF[:], "KF", "KO")
+
+    def cands(s):
+        win = T.CT[:, 0:2 * NW].indirect(T.KO[:, 0:24])
+        cp(T.CO[:], win, "CT0 CT1 d2 d3 KO", "CO")
+        tt(T.DF[:], win, T.EN[:, s, :], A.subtract, "CT0 CT1 d2 d3 KO EN", "DF")
+
+    keys(0)
+    cands(0)
+    tt(T.UO0[:, L:384], T.XB[:, 0:M].indirect(T.OO[:, 12:24]), T.XP[:, L:384], A.mult, "TBX OO1 XP1", "UO0_1")
+    send("UO0_1", [(prv, T.UO0[:, L:384], T.U0[:, 0:L], "arU0h", 0, 16)])
+
+    def vsend(s):
+        tt(T["VO%d" % s][:], TE_.indirect(T.OO[:, 0:24]), T.EP[:], A.mult, "TBE OO0 OO1 EP0 EP1", "VO%d" % s)
+        send("VO%d" % s, [(nxt, T["VO%d" % s][:, 0:L], T["V%d" % s][:, L:384], "arV%d" % s, 0, 8),
+                          (prv, T["VO%d" % s][:, L:384], T["V%d" % s][:, 0:L], "arV%d" % s, 8, 16)])
+
+    vsend(0)
+    ms(T.UP[:, UPA:12304], 0.0, "UPb")
+    ms(T.SEL[:], 1.0, "SEL")
+    cp(T.OW[:, 12:24], T.RL[:, 0:12], "RL OW0a", "OW0")
+    op("g", lambda q: q.iota(T.PRI[:], [[0, 24], [-1, 16]], 15, 0, allow_small_or_imprecise_dtypes=True), w="PRI")
+    op("g", lambda q: q.iota(T.EXI[:], [[16, 24]], 15, 0), w="EXI")
+    op("g", lambda q: q.affine_select(T.SEL[:], T.SEL[:], [[-1, 16], [-16, 8], [0, 16]], A.is_equal, 0.0, 0, 1), "SEL", "SEL")
+    op("g", lambda q: q.affine_select(T.DD[:], T.SEL[:], [[0, 16], [-16, 8], [-1, 16]], A.not_equal, -1.0, 0, 1), "SEL", "DD")
+    op("g", lambda q: q.affine_select(T.DD[:], T.DD[:], [[-1, 16], [0, 8], [1, 16]], A.not_equal, 0.0, 0, 0), "DD", "DD")
+
+    def consts():
+        ts(T.PJ[:, 2:3], T.PI[:, 0:1], 1, A.bitwise_and, "PI", "PJ2")
+        ts(T.IDB[:], T.IC[:, 16:144], T.PC[:, 3:4], A.is_equal, "IC PC3", "IDB")
+        ts(T.PC[:, 10:11], T.PJ[:, 2:3], -BIG, A.mult, "PJ2", "PC10")
+        ts(T.PC[:, 11:12], T.PJ[:, 2:3], BIG, A.mult, "PJ2", "PC11", s2=-BIG, o1=A.add)
+        ts(T.ENS[:, 0:384], T.EN[:, 0, :], -1536.0, A.add, "EN", "ENS0")
+        for x in range(4):
+            ts(T.CZ[:, x, :], T.CI[:, 16 * x:16 * x + 16], T.PC[:, 10 + x % 2:11 + x % 2], A.add, "CI PC10 PC11", "CZ%d" % x)
+
+    def consts2():
+        ts(T.W[:], T.IC[:], T.PC[:, 2:3], A.is_equal, "IC PC2", "W")
+        ts(T.IDF[:], T.IC[:, 16:144], T.PC[:, 3:4], A.is_equal, "IC PC3", "IDF")
+        ts(T.PW0[:], T.IC[:], T.PC[:, 3:4], A.is_equal, "IC PC3 PC5", "PW0", s2=T.PC[:, 5:6], o1=A.mult)
+        ts(T.PW1[:], T.IC[:], T.PC[:, 3:4], A.is_equal, "IC PC3 PC4", "PW1", s2=T.PC[:, 4:5], o1=A.mult)
+        ts(T.RM[:], T.PRI[:], 15.0, A.is_equal, "PRI", "RM", s2=-1.0e9, o1=A.mult)
+        ts(T.DM[:], T.PRI[:], T.PC[:, 0:1], A.is_equal, "PRI PC0", "DM")
+        cp(T.EXO[:], T.EXI[:], "EXI", "EXO")
+
+    def entrants(s):
+        c = slice(384 * s, 384 * s + 384)
+        ts(T.ENS[:, c], T.EN[:, s, :], -1536.0, A.add, "EN", "ENS%d" % s)
+        ts(T.ENO[:, c], T.ENS[:, c], 1536.0, A.add, "ENS%d" % s, "ENO%d" % s, c=212)
+
+    def xgather(s, d):
+        for h in range(3):
+            for ent in (1, 0):
+                a, o = 64 * h, 384 * s + L * d
+                off, on = (T.ENO[:, o + a:o + a + 64], "ENO%d" % s) if ent else (T.CO[:, L * d + a:L * d + a + 64], "CO")
+                cp(T["XG%d" % d][:, ent, 16 * a:16 * a + 1024], TX_.indirect(off), "TBX " + on, "XG%d_%d_%d" % (d, ent, h),
+                   either=True, c=1650)
+
+    UPN = " ".join("UP%d" % x for x in range(16))
+
+    def spread(s, d):
+        for x in range(16):
+            gg, h = divmod(x, 2)
+            o = 16 * gg + 14 + h
+            out, src, m = T.UP[:, o:o + 128 * 95 + 1:128], T["U%d" % s][:, L * d + h:L * d + L:2], T.MG[:, gg:gg + 1]
+            ts(out, src, m, A.mult, "U%d_%d MG UPa UPb" % (s, d), "UP%d" % x,
+               alt=lambda q, out=out, src=src, m=m: q.activation(out, src, F.Copy, scale=m))
+
+    def scores(d):
+        for c in range(12):
+            row = 24 * (1 - d) + 2 * c
+            out, bk = T.SC[:, row:row + 2, :, :], "s%d" % (row // 16)
+            mm(out, T.IDB[:], T.CZ[:], True, False, "IDB CZ0 CZ1 CZ2 CZ3", "sc%d" % d, bk)
+            for t in range(8):
+                q = 8 * c + t
+                o = 128 * q + 14 - 2 * t
+                mm(out, T.UP[:, o:o + 128], T["XG%d" % d][:, :, 32 * q:32 * q + 32], False, t == 7,
+                   "%s XG%d_0_%d XG%d_1_%d" % (UPN, d, c // 4, d, c // 4), "sc%d" % d, bk)
+
+    def turn(a, row, r, w):
+        op("v", lambda q: q.transpose(T.LT[:, a // 16:a // 16 + 12, :], T.LB[:, a:a + L]), r, "LT%d" % a)
+        for h in range(2):
+            for g2 in range(2):
+                o = 16 + 16 * (h - g2)
+                mm(T.SC[:, row:row + 6, h, :], T["PW%d" % h][:, o:o + 128], T.LT[:, a // 16 + g2:a // 16 + 12:2, :], g2 == 0, g2 == 1,
+                   "PW0 PW1 LT%d" % a, w, "s%d" % (row // 16), 96)
+
+    def contest(s, d):
+        c = slice(L * d, L * d + L)
+        r0, r1, both, bk = 24 * (1 - d), 32 * (1 - d), ("s1 s2", "s0 s1")[d], ("s2", "s0")[d]
+        oh, lo = T.SC[:, r1:r1 + 6, :, :], T.SC[:, r1 + 6:r1 + 12, :, :]
+        cp(T.HA[:], T.SC[:, r0:r0 + 24, 0, :], "sc%d" % d, "HA", both, either=True)
+        tt(T.SV[:], T.SC[:, r0:r0 + 24, 1, :], T.HA[:], A.max, "sc%d HA" % d, "SV", both)
+        tt(T.LB[:, 0:L], T.SV[:, 0:24:2, :], T.SV[:, 1:24:2, :], A.is_gt, "SV", "LB0")
+        if s < S - 1:
+            tt(T.MX[:], T.SV[:, 0:24:2, :], T.SV[:, 1:24:2, :], A.max, "SV", "MX")
+        turn(0, r1 + 6, "LB0", "lo%d" % d)
+        if s < S - 1:
+            scan(T.SK[:, c], T.RM[:, 0:L], T.MX[:], A.add, A.max, "RM MX", "SK%d" % d)
+            tt(T.LB[:, L:384], T.SK[:, c].indirect(T.EXO[:, 0:12]), T.MX[:], A.is_equal, "SK%d EXO MX" % d, "LB1")
+            turn(L, r1, "LB1", "oh%d" % d)
+        tt(lo, lo, T.DF[:, c], A.mult, "lo%d DF" % d, "lo%d" % d, bk)
+        tt(T.AL[:, c], lo, T.ENS[:, 384 * s + L * d:384 * s + L * d + L], A.add, "lo%d ENS%d" % (d, s), "AL%d" % d, bk)
+        if s < S - 1:
+            tt(T.YB[:, c], oh, T.AL[:, c], A.mult, "oh%d AL%d" % (d, d), "YB%d" % d, bk)
+        ts(T.AO[:, c], T.AL[:, c], 1536.0, A.add, "AL%d" % d, "AO%d" % d)
+
+    def egather(s, d):
+        for h in range(2):
+            a = L * d + 96 * h
+            cp(T["EG%d" % (s & 1)][:, 16 * a:16 * a + 1536], TE_.indirect(T.AO[:, a:a + 96]), "TBE AO%d" % d,
+               "EG%d_%d" % (s & 1, 2 * d + h), either=True, c=2450)
+
+    def best(s):
+        MS = T["MS%d" % s]
+        for j in range(16):
+            mm(PS[4][:, 384:408], T.W[:, 15 - j:143 - j], T.YB[:, j:384:16], j == 0, j == 15, "W YB0 YB1", "cv", "b4")
+        ts(MS[:, 0:48:2], T.SK[:, 15:384:16], 1.0 / 32, A.mult, "SK0 SK1", "MSa%d" % s, s2=-15.5 / 32, o1=A.add)
+        ts(MS[:, 1:48:2], PS[4][:, 384:408], 1536.0, A.add, "cv", "MSb%d" % s, "b4")
+        send("MSa%d MSb%d" % (s, s), [(nxt, MS[:, 0:24], T["RX%d" % s][:, 24:48], "arM%d" % s, 0, 8),
+                                      (prv, MS[:, 24:48], T["RX%d" % s][:, 0:24], "arM%d" % s, 8, 16)])
+        ts(T.BO[:], PS[4][:, 384:408], 1536.0, A.add, "cv", "BO", "b4")
+
+    WZ = T.SC[:, 0:12, :, :]
+
+    def propose1(s):
+        V = T["V%d" % s]
+        tt(T.XS[:], TX_.indirect(T.BO[:, 0:24]), T.SG[:], A.subtract, "TBX BO SG", "XS")
+        tt(T.EV[:], TE_.indirect(T.BO[:, 0:24]), V[:], A.mult, "TBE BO V%d" % s, "EV")
+        mm(WZ, T.ONE[:], T.EV[:], True, True, "ONE EV", "z3", "s0", 1536)
+        act(T.E7[:], TE_.indirect(T.BO[:, 0:24]), F.Copy, "TBE BO", "E7", scale=0.875)
+        act(WZ, WZ, F.Sigmoid, "z3", "z3", "s0", scale=0.0625)
+        act(WZ, WZ, F.Copy, "z3", "z3", "s0", scale=0.125)
+        ts(T.XS[:], T.XS[:], -7.0, A.max, "XS", "XS", s2=7.0, o1=A.min, c=212)
+        ts(T.BD[:], T["MS%d" % s][:, 1:48:2], T.PC[:, 6:7], A.subtract, "MSb%d PC6" % s, "BD")
+        tt(T.DO[:], T["MS%d" % s][:, 1:48:2], T.OW[:, 24 * s:24 * s + 24], A.subtract, "MSb%d OW%d" % (s, s), "DO")
+
+    def propose2(s):
+        tt(WZ, WZ, T["V%d" % s][:], A.mult, "V%d z3" % s, "z3", "s0")
+        tt(T.E7[:], WZ, T.E7[:], A.add, "z3 E7", "E7", "s0")
+
+    def firsts(src, nm, p, bk, out, on):
+        for j in range(16):
+            mm(PS[p][:, 15 - j:384:16], T.DD[:, 128 * j:128 * j + 128], src, True, True, "DD " + nm, "dd" + on, bk)
+        scan(out, PS[p][:, 0:384], T.DM[:], A.mult, A.add, "dd%s DM" % on, on, bk)
+
+    def cache1():
+        ts(T.K16[:], T.K3[:], 1.0 / 64, A.mult, "K3", "K16")
+        ts(T.C1[:], T.K3[:], T.PC[:, 9:10], A.subtract, "K3 PC9", "C1")
+
+    def cache2(p):
+        firsts(T.K16[:], "K16", p, "b%d" % p, T.SD[:], "SD")
+        ts(T.NE[:], T.SD[:, 15:384:16], 0.0, A.not_equal, "SD", "NE")
+        tt(T.C2[:], T.NE[:], T.C1[:], A.mult, "NE C1", "C2")
+        ts(T.CSO[:, 0:48:2], T.C2[:], T.PC[:, 9:10], A.add, "C2 PC9", "CSO")
+
+    def cache3():
+        for c in range(23, -1, -1):
+            d = c // 12
+            cp(T.CT[:, NW * d:NW * d + NW].indirect(T.CSO[:, 2 * c:2 * c + 1]), T.AO[:, 16 * c:16 * c + 16], "CSO AO%d d2 d3" % d, "CT%d" % d)
+
+    def decide(s):
+        MS, RX, a, b = T["MS%d" % s], T["RX%d" % s], slice(24 * s, 24 * s + 24), slice(24 * s + 24, 24 * s + 48)
+        tt(T.MI[:, 0:12], MS[:, 0:24:2], RX[:, 0:24:2], A.is_ge, "MSa%d RX%d" % (s, s), "MI0")
+        tt(T.MI[:, 12:24], MS[:, 24:48:2], RX[:, 24:48:2], A.is_gt, "MSa%d RX%d" % (s, s), "MI1")
+        tt(T.T3[:], T.OT[:, a], RX[:, 1:48:2], A.subtract, "OT%d RX%d" % (s, s), "T3")
+        tt(T.T1[:], T.MI[:], T.BD[:], A.mult, "MI0 MI1 BD", "T1")
+        tt(T.T4[:], T.MI[:], T.T3[:], A.mult, "MI0 MI1 T3", "T4")
+        ts(T.B16[:], T.T1[:], T.PC[:, 8:9], A.add, "T1 PC8", "B16", s2=1.0 / 64, o1=A.mult)
+        tt(T.OT[:, b], T.T4[:], RX[:, 1:48:2], A.add, "T4 RX%d" % s, "OT%d" % (s + 1))
+        tt(T.T5[:], T.MI[:], T.DO[:], A.mult, "MI0 MI1 DO", "T5")
+        keys(s + 1)
+        tt(T.OW[:, b], T.T5[:], T.OW[:, a], A.add, "T5 OW%d" % s, "OW%d" % (s + 1))
+        firsts(T.B16[:], "B16", 4, "b4", T.SD[:], "SD")
+        cp(T.OO[:], T.OW[:, b], "OW%d" % (s + 1), "OO0 OO1")
+        ts(T.ND[:], T.SD[:, 15:384:16], 0.0, A.not_equal, "SD", "ND")
+        tt(T.T2[:], T.ND[:], T.T1[:], A.mult, "ND T1", "T2")
+        ts(T.SO[:, 0:48:2], T.T2[:], T.PC[:, 6:7], A.add, "T2 PC6", "SO")
+
+    def write(e):
+        src, nm = ((T.XS, "XS"), (T.E7, "E7"))[e]
+        for i, c in enumerate(list(range(11, -1, -1)) + list(range(23, 11, -1))):
+            cp((T.XB, T.TB)[e][:, 0:EO].indirect(T.SO[:, 2 * c:2 * c + 1]), src[:, 16 * c:16 * c + 16], "SO d0 d1 " + nm,
+               ("TBX", "TBE")[e])
+
+    def usend(s):
+        tt(T["UO%d" % s][:], TX_.indirect(T.OO[:, 0:24]), T.XP[:], A.mult, "TBX OO0 OO1 XP0 XP1", "UO%d" % s)
+        send("UO%d" % s, [(nxt, T["UO%d" % s][:, 0:L], T["U%d" % s][:, L:384], "arU%d" % s, 0, 8),
+                          (prv, T["UO%d" % s][:, L:384], T["U%d" % s][:, 0:L], "arU%d" % s, 8, 16)])
+
+    def vcopy(s):
+        cp(PS[2][:, 0:384], T["V%d" % s][:], "V%d" % s, "vp", "b2", either=True)
+
+    def sign(s):
+        act(T.SG[:], T["U%d" % s][:], F.Sign, "U%d_0 U%d_1" % (s, s), "SG")
+
+    def ev(s, ks, ds):
+        a, b = ds[0], ds[-1] + 1
+        for k in ks:
+            tt(T.PE[:, 1536 * a + k:1536 * b:16], T["EG%d" % (s & 1)][:, 1536 * a + k:1536 * b:16], PS[2][:, 96 * a:96 * b], A.mult,
+               "vp " + " ".join("EG%d_%d" % (s & 1, x) for x in ds), " ".join("PE%d_%d" % (d, k) for d in ds), "b2",
+               c=20 + 96 * len(ds))
+
+    def pen(ds):
+        return " ".join("PE%d_%d" % (d, k) for d in ds for k in range(16))
+
+    def zsum(js, p):
+        for j in js:
+            for x in range(3):
+                b = 3 * j + x
+                mm(PS[p][:, 128 * x + j:128 * x + 128:16], T.PE[:, 128 * b:128 * b + 128], T.ONE[:, 0:128:16], True, True,
+                   "ONE " + pen([j // 4]), "z%d" % p, "b%d" % p, 256)
+
+    def zturn(p):
+        cp(T.ZS[:], PS[p][:, 0:384], "z%d" % p, "ZS", "b%d" % p, either=True)
+        for x in range(3):
+            mm(PS[p][:, 128 * x:128 * x + 128], T.ZS[:, 128 * x:128 * x + 128], T.IDF[:], True, True, "ZS IDF", "z%d" % p, "b%d" % p, 512)
+
+    def weights(p, y, exp_first=False):
+        bk, z, P = "b%d" % p, "z%d" % p, PS[p][:, 0:384]
+        if exp_first:
+            act(T.QX[:], P, F.Exp, z, "QX", bk, scale=-0.0625)
+            act(P, P, F.Sigmoid, z, z, bk, scale=0.0625, c=1950)
+            ts(T.QX[:], T.QX[:], 1.0, A.add, "QX", "QX", alt=lambda q: q.activation(T.QX[:], T.QX[:], F.Identity, bias=1.0))
+            w, q1, wn = PS[p], T.QX, z
+        else:
+            act(T.QX[:], P, F.Sigmoid, z, "QX", bk, scale=0.0625)
+            act(P, P, F.Exp, z, z, bk, scale=-0.0625, c=1950)
+            act(P, P, F.Identity, z, z, bk, bias=1.0)
+            w, q1, wn = T.QX, PS[p], "QX"
+        cp(T.R[:, 384:408], w[:, 15:384:16], wn, "Rl", bk if exp_first else "")
+        tt(T.R[:, 1:384], w[:, 0:383], q1[:, 1:384], A.mult, z + " QX", "R", bk)
+        op("v", lambda q: q.memset(T.R[:, 0:384:16], 0.0), "", "R", c=84)
+        cp(T["RH%d" % y][:], T.R[:], "R Rl", "RH%d" % y, either=True)
+        tt(T["RO%d" % y][:], T.R[:], T["RH%d" % y][:], A.subtract, "R Rl RH%d" % y, "RO%d" % y)
+
+    def gscan(s, js, y):
+        def fin(j):
+            p = 6 + (j & 1)
+            tt((T.GT if s else T.ACC)[:, 24 * j:24 * j + 24], PS[p][:, 384:408], T.GS[:, 384 * (j & 1) + 15:384 * (j & 1) + 384:16], A.mult,
+               "rb%d GS%d" % (p, p), "G%d_%d" % (min(s, 1), j), "b%d" % p)
+        for j in js:
+            p = 6 + (j & 1)
+            for i, x in enumerate(("RH%d" % y, "RO%d" % y)):
+                mm(PS[p][:, 0:408], T.SEL[:, 128 * j:128 * j + 128], T[x][:], i == 0, i == 1, "SEL " + x, "rb%d" % p, "b%d" % p, 408)
+            scan(T.GS[:, 384 * (j & 1):384 * (j & 1) + 384], PS[p][:, 0:384], T["EG%d" % (s & 1)][:, 384 * j:384 * j + 384], A.mult, A.add,
+                 "rb%d EG%d_%d" % (p, s & 1, j // 4), "GS%d" % p, "b%d" % p)
+            fin(j)
+        if s:
+            a, b = 24 * js[0], 24 * js[-1] + 24
+            acc = " ".join(sorted(set("ACC%d" % (j // 8) for j in js)))
+            tt(T.ACC[:, a:b], T.GT[:, a:b], T.ACC[:, a:b], A.add, " ".join("G0_%d G1_%d" % (j, j) for j in js), acc, c=20 + 2 * (b - a))
+
+    ALL, KS = list(range(16)), list(range(16))
+    for s in range(S):
+        last = s == S - 1
+        step[0] = str(s)
+        H, TL = ALL[:8], ALL[8:]
+        if s == 0:
+            consts(); consts2(); entrants(1); entrants(2)
+        if not last:
+            cache1(); cache2(4); sign(s)
+        for d in (1, 0):
+            step[0] = str(s) + "ht"[d]
+            xgather(s, d); spread(s, d); scores(d); contest(s, d); egather(s, d)
+        step[0] = str(s)
+        if not last:
+            best(s); propose1(s); cache3(); decide(s); cands(s + 1)
+            write(0); usend(s + 1)
+            propose2(s); write(1); vsend(s + 1)
+            vcopy(s); ev(s, KS, (2, 3)); step[0] = str(s) + "h"; ev(s, KS, (0, 1)); step[0] = str(s); zsum(TL + H, 5); zturn(5); weights(5, s & 1)
+            gscan(s, ALL, s & 1)
+        else:
+            vcopy(s)
+            step[0] = "2t"
+            ev(s, KS, (2, 3)); zsum(TL, 4); zturn(4); weights(4, 0, True)
+            step[0] = "2h"
+            ev(s, KS, (0,)); ev(s, KS, (1,)); zsum(H, 5); zturn(5); weights(5, 1)
+            step[0] = "2t"
+            gscan(s, TL, 0)
+            dma("s", T.yt[:], T.ACC[:, L:384], "ACC1", "yt", "out1", 16)
+            step[0] = "2h"
+            gscan(s, H, 1)
+            dma("s", T.yh[:], T.ACC[:, 0:L], "ACC0", "yh", "out0", 16)
+
+    if "order" not in _ORDER:
+        _ORDER["order"] = _order(ops, raised)[0]
+        _ORDER["ops"] = (ops, raised)
+    order = _ORDER["order"]
+    on = dict(order)
+    place = {i: k for k, (i, e) in enumerate(order)}
+    need, seen = set(), {e: {} for e in Q}
+    for i, e in order:
+        last_of = {}
+        for x in ops[i][2]:
+            if x[0] == "e":
+                last_of[on[x[1]]] = max(last_of.get(on[x[1]], -1), place[x[1]])
+        for e2, k in last_of.items():
+            if k > seen[e].get(e2, -1):
+                seen[e][e2] = k
+                need.add(order[k][0])
+    num, tot = {}, {e: 0 for e in Q}
+    for i, e in order:
+        tot[e] += i in need
+        num[i] = tot[e] if i in need else 0
+    seen = {e: {} for e in Q}
+    for i, e in order:
+        f, deps, d = ops[i][1][e], ops[i][2], ops[i][3]
+        want = {}
+        for x in deps:
+            sem, val = (CNT[on[x[1]]], num[x[1]]) if x[0] == "e" else (x[1], x[2])
+            want[sem] = max(want.get(sem, 0), val)
+        for sem in sorted(want):
+            if want[sem] > seen[e].get(sem, 0):
+                seen[e][sem] = want[sem]
+                Q[e].wait_ge(T.sem[sem], want[sem])
+        ins = f(Q[e])
+        if d and d[1]:
+            ins.then_inc(T.sem[d[0]], 16)
+        elif i in need:
+            ins.then_inc(T.sem[CNT[e]], 1)
+    g.wait_ge(T.sem.sent, sent[0])
+    g.wait_ge(T.sem.out1, 16)
+    g.wait_ge(T.sem.out0, 16)

@@ -30,7 +30,7 @@ SCRATCH = {
     "T2": _sb(24, f32), "T3": _sb(24, f32), "T4": _sb(24, f32), "T5": _sb(24, f32), "B16": _sb(24, f16), "SD": _sb(384, f32),
     "ND": _sb(24, f32), "SO": _sb(48, u16), "NE": _sb(24, f32), "C1": _sb(24, f32), "C2": _sb(24, f32),
     "CSO": _sb(48, u16), "QX": _sb(384, f32), "R": _sb(408, f32), "RH0": _sb(408, bf), "RO0": _sb(408, f16),
-    "RH1": _sb(408, bf), "RO1": _sb(408, f16), "GS": _sb(768, f32), "GT": _sb(384, f32),
+    "RH1": _sb(408, bf), "RO1": _sb(408, f16), "GS": _sb(3072, f32),
     "ACC": _sb(384, f32),
     "PI": _sb(8, i32), "PJ": _sb(8, i32), "PC": _sb(16, f32), "IC": _sb(160, f32), "IG": _sb(128, f32), "PRI": _sb(384, bf),
     "EXI": _sb(24, i32), "EXO": _sb(24, u16), "W": _sb(160, bf), "PW0": _sb(160, bf), "PW1": _sb(160, bf),
@@ -50,7 +50,7 @@ for _s in (2, 4, 5, 6, 7):
 SEMAPHORES = ["cg", "cv", "ca", "cp", "sent", "ldL", "ldR", "ldX", "ldC", "ldN", "ldTE", "out0", "out1",
               "arL", "arP", "arU0h", "arU0t", "arU1", "arU2", "arV0", "arV1", "arV2", "arM0", "arM1"]
 CNT = {"g": "cg", "v": "cv", "a": "ca", "p": "cp"}
-PEC, HOP = 0.6, 70
+PEC, HOP = 0.5, 200
 TUNE = {'bias': 20000, 'patience': 1.0, 'turns': 3, 'shy': 1000}
 TUNE.update((k + s, 20) for s in "01" for k in ("EV", "z3p", "z3a", "z3v", "E"))
 TUNE.update((k + s, 30) for s in "01" for k in ("ZS", "QX", "z5a", "RH", "z5p", "R", "Rl", "RO", "vp"))
@@ -58,7 +58,11 @@ TUNE.update((k + "s", 30) for k in ("PO", "OO", "XP", "EP", "UO", "K", "KF", "KO
 TUNE.update({'PE0': -10, 'PE0h': -20, 'PE1': -10, 'PE1h': -10, 'rb0': 10, 'rb1': 10, 'GS2t': -20, 'GS2h': -20, 'GS0': -10,
              'E1': 10, 'UP1h': 2, 'G1': 1, 'cv0': 5, 'AO1h': 2, 'TBE1': -15, 'cv1': 5, 'G2h': -20, 'UP2t': 10,
              'UPas': 100, 'QX1': 31, 'POs': 25, 'T0': 25, 'LT2h': 2, 'OT1': -5, 'G0': 2, 'PE2h': -10, 'RH2h': 1})
-KEEP = set(['EG0h', 'EG0t', 'EG1t', 'RH1', 'UP0h', 'UP2h', 'XG2h', 'ZS0', 'vp0', 'vp1'])
+TUNE.update({'wl0': 30, 'wl1': 30, 'bias': 2000, 'ENOs': 50, 'TBE1': -25, 'EG0t': 20, 'EG2t': -20, 'sc2t': 20, 'z5a2h': -10, 'OWs': 20,
+             'LB0t': -10, 'RH0': 10, 'z5a1': 29, 'Ks': 40, 'EG2h': -15, 'SV2h': -20, 'sc1h': -20, 'DF0': -5, 'ddSD1': 5, 'LNs': 10,
+             'W0': 20, 'EG0h': 2, 'XG1t': -2, 'PE2t': -11, 'UO0': 5, 'DO1': -2, 'CT1': 5, 'sc2h': 20, 'SK0t': -5, 'XS1': -10, 'ddSD0': 2})
+KEEP = set(['EG0h', 'EG0t', 'EG1t', 'EG2t', 'HA2t', 'QX2t', 'RH1', 'RH2h', 'UP0h', 'UP1t', 'UP2h', 'XG2h', 'ZS0', 'ZS1', 'ZS2h', 'vp0',
+            'vp1'])
 _ORDER = {}
 BASE = {"v": 84, "a": 450, "g": 900, "s": 100, "p": 40}
 COST = {"vUPa": 4100, "vUPb": 2100, "vSEL": 1050, "vENO": 404, "vENS": 404, "vXP": 350, "vEP": 350, "vUO": 650, "vVO": 650, "vCO": 650,
@@ -559,22 +563,26 @@ def rank_program(g, core, T, topo):
         cp(T["RH%d" % y][:], T.R[:], "R Rl", "RH%d" % y, either=True)
         tt(T["RO%d" % y][:], T.R[:], T["RH%d" % y][:], A.subtract, "R Rl RH%d" % y, "RO%d" % y)
 
-    def gscan(s, js, y):
-        def fin(j):
-            p = 6 + (j & 1)
-            tt((T.GT if s else T.ACC)[:, 24 * j:24 * j + 24], PS[p][:, 384:408], T.GS[:, 384 * (j & 1) + 15:384 * (j & 1) + 384:16], A.mult,
-               "rb%d GS%d" % (p, p), "G%d_%d" % (min(s, 1), j), "b%d" % p)
+    def gscan(s, js, y, pz):
+        z, zb = "wl%d" % pz, "b%d" % pz
         for j in js:
-            p = 6 + (j & 1)
             for i, x in enumerate(("RH%d" % y, "RO%d" % y)):
-                mm(PS[p][:, 0:408], T.SEL[:, 128 * j:128 * j + 128], T[x][:], i == 0, i == 1, "SEL " + x, "rb%d" % p, "b%d" % p, 408)
-            scan(T.GS[:, 384 * (j & 1):384 * (j & 1) + 384], PS[p][:, 0:384], T["EG%d" % (s & 1)][:, 384 * j:384 * j + 384], A.mult, A.add,
-                 "rb%d EG%d_%d" % (p, s & 1, j // 4), "GS%d" % p, "b%d" % p)
-            fin(j)
+                mm(PS[pz][:, 24 * j:24 * j + 24], T.SEL[:, 128 * j:128 * j + 128], T[x][:, 384:408], i == 0, i == 1, "SEL " + x, z, zb)
+        for j in js:
+            p, x8 = 6 + (j & 1), j % 8
+            for i, x in enumerate(("RH%d" % y, "RO%d" % y)):
+                mm(PS[p][:, 0:384], T.SEL[:, 128 * j:128 * j + 128], T[x][:, 0:384], i == 0, i == 1, "SEL " + x, "rb%d" % p, "b%d" % p, 384)
+            scan(T.GS[:, 384 * x8:384 * x8 + 384], PS[p][:, 0:384], T["EG%d" % (s & 1)][:, 384 * j:384 * j + 384], A.mult, A.add,
+                 "rb%d EG%d_%d" % (p, s & 1, j // 4), "GS%d" % x8, "b%d" % p)
+            if j % 4 == 3:
+                a, o = 24 * (j - 3), 384 * (x8 - 3)
+                tt((PS[pz] if s else T.ACC)[:, a:a + 96], PS[pz][:, a:a + 96], T.GS[:, o + 15:o + 1536:16], A.mult,
+                   z + "".join(" GS%d" % k for k in range(x8 - 3, x8 + 1)), "G%d_%d" % (min(s, 1), j // 4), zb, c=116)
         if s:
             a, b = 24 * js[0], 24 * js[-1] + 24
             acc = " ".join(sorted(set("ACC%d" % (j // 8) for j in js)))
-            tt(T.ACC[:, a:b], T.GT[:, a:b], T.ACC[:, a:b], A.add, " ".join("G0_%d G1_%d" % (j, j) for j in js), acc, c=20 + 2 * (b - a))
+            tt(T.ACC[:, a:b], PS[pz][:, a:b], T.ACC[:, a:b], A.add, " ".join("G0_%d G1_%d" % (j // 4, j // 4) for j in js[::4]), acc, zb,
+               c=20 + b - a)
 
     ALL, KS = list(range(16)), list(range(16))
     for s in range(S):
@@ -594,7 +602,7 @@ def rank_program(g, core, T, topo):
             write(0); usend(s + 1)
             propose2(s); write(1); vsend(s + 1)
             vcopy(s); ev(s, KS, (2, 3)); step[0] = str(s) + "h"; ev(s, KS, (0, 1)); step[0] = str(s); zsum(TL + H, 5); zturn(5); weights(5, s & 1)
-            gscan(s, ALL, s & 1)
+            gscan(s, ALL, s & 1, 5)
         else:
             vcopy(s)
             step[0] = "2t"
@@ -602,10 +610,10 @@ def rank_program(g, core, T, topo):
             step[0] = "2h"
             ev(s, KS, (0,)); ev(s, KS, (1,)); zsum(H, 5); zturn(5); weights(5, 1)
             step[0] = "2t"
-            gscan(s, TL, 0)
+            gscan(s, TL, 0, 4)
             dma("s", T.yt[:], T.ACC[:, L:384], "ACC1", "yt", "out1", 16)
             step[0] = "2h"
-            gscan(s, H, 1)
+            gscan(s, H, 1, 5)
             dma("s", T.yh[:], T.ACC[:, 0:L], "ACC0", "yh", "out0", 16)
 
     if "order" not in _ORDER:

@@ -4,37 +4,37 @@ from concourse.mybir import AluOpType as A, ActivationFunctionType as F
 M, L, S, NC = 3072, 192, 3, 1024
 EO = M + 32
 NW = NC + 16
-BIG = float(1 << 20)
-UPA = 8192
+KEY0 = 1 << 18
 f32, bf, i32, u16, f16 = "float32", "bfloat16", "int32", "uint16", "float16"
 
 
 def _sb(n, d):
-    return ("sbuf", [128, n], d)
+    return ("sbuf", [128] + (n if isinstance(n, list) else [n]), d)
 
 
 SCRATCH = {
-    "XB": _sb(EO, bf), "TB": _sb(EO, f32), "CT": _sb(2 * NW, i32), "EN": ("sbuf", [128, 3, 384], i32),
-    "ENO": _sb(1152, u16), "LN": _sb(36, i32), "RL": _sb(36, i32), "XR": _sb(64, bf), "ER": _sb(64, bf),
+    "XB": _sb(EO, bf), "TB": _sb(EO, f32), "CT": _sb(2 * NW, i32), "EN": _sb([3, 384], i32),
+    "ENO": _sb(1152, u16), "ENS": _sb(1152, f16), "LN": _sb(36, i32), "RL": _sb(36, i32), "XR": _sb(64, bf), "ER": _sb(64, bf),
     "XP": _sb(384, bf), "EP": _sb(384, bf), "OW": _sb(72, f32), "OT": _sb(72, f32), "KA": _sb(24, f32), "KB": _sb(24, f32),
-    "KC": _sb(24, f32), "K1": _sb(24, f32), "K2": _sb(24, i32), "K3": _sb(24, i32), "KF": _sb(24, f32), "KO": _sb(24, u16),
+    "K1": _sb(24, f32), "K2": _sb(24, i32), "K3": _sb(24, i32), "KO": _sb(24, u16),
     "K16": _sb(24, f16), "PO": _sb(12, u16), "OO": _sb(24, u16), "CO": _sb(384, u16), "DF": _sb(384, f32),
-    "XG0": ("sbuf", [128, 2, M], bf), "XG1": ("sbuf", [128, 2, M], bf), "UP": _sb(12304, bf),
-    "EG0": _sb(6144, f32), "EG1": _sb(6144, f32), "PE": _sb(6144, f32), "ENS": _sb(1152, f16),
-    "HA": ("sbuf", [128, 24, 16], f32), "SV": ("sbuf", [128, 24, 16], f32), "MX": _sb(192, f32), "LB": _sb(384, bf),
-    "LT": ("sbuf", [128, 24, 16], bf), "AL": _sb(384, f16), "AO": _sb(384, u16), "YB": _sb(384, f16), "ZS": _sb(384, f32),
-    "SK": _sb(384, f32), "BO": _sb(24, u16), "SG": _sb(384, bf), "CI": _sb(64, f32), "CZ": ("sbuf", [128, 4, 16], bf),
-    "MG": _sb(8, f32), "IDB": _sb(128, bf), "IDF": _sb(128, f32), "SC": ("psum", [128, 48, 2, 16], f32),
-    "XS": _sb(384, bf), "EV": _sb(384, f32), "E7": _sb(384, f32),
-    "MI": _sb(24, f32), "BD": _sb(24, f32), "DO": _sb(24, f32), "T1": _sb(24, f32),
-    "T2": _sb(24, f32), "T3": _sb(24, f32), "T4": _sb(24, f32), "T5": _sb(24, f32), "B16": _sb(24, f16), "SD": _sb(384, f32),
-    "ND": _sb(24, f32), "SO": _sb(48, u16), "NE": _sb(24, f32), "C1": _sb(24, f32), "C2": _sb(24, f32),
-    "CSO": _sb(48, u16), "QX": _sb(384, f32), "R": _sb(408, f32), "RH0": _sb(408, bf), "RO0": _sb(408, f16),
-    "RH1": _sb(408, bf), "RO1": _sb(408, f16), "GS": _sb(3072, f32),
-    "ACC": _sb(384, f32),
+    "XG": _sb(12288, bf), "UM": _sb([8, 384], bf), "VM": _sb([8, 384], f32),
+    "EG0": _sb(6144, f32), "EG1": _sb(6144, f32), "GS": _sb(6144, f32),
+    "SCP": _sb(768, f32), "SK": _sb(768, f32), "LB": _sb(384, bf), "LT": _sb([24, 16], bf), "KI": _sb(12, i32),
+    "KL": _sb(24, i32), "KS": _sb(24, u16), "AL": _sb(384, f16), "AO": _sb(384, u16), "YB": _sb(384, f16),
+    "BO": _sb(24, u16), "SG": _sb(384, bf), "XS": _sb(384, bf), "EV": _sb(384, f32), "E7": _sb(384, f32), "WV": _sb(384, f32),
+    "MI": _sb(24, f32), "LM": _sb(12, f32), "CP": _sb(12, f32), "BD": _sb(24, f32), "BM": _sb(24, f32), "DO": _sb(24, f32),
+    "T1": _sb(24, f32), "T2": _sb(24, f32), "T3": _sb(24, f32), "T4": _sb(24, f32), "T5": _sb(24, f32), "B16": _sb(24, f16),
+    "SD": _sb(384, f32), "SE": _sb(384, f32), "ND": _sb(24, f32), "SO": _sb(48, u16), "NE": _sb(24, f32), "C1": _sb(24, f32),
+    "C2": _sb(24, f32), "CSO": _sb(48, u16), "WS0": _sb(256, f32), "WS1": _sb(256, f32),
+    "RW": _sb([24, 17], f32), "RH": _sb([24, 17], bf), "RO": _sb([24, 17], f16), "ACC": _sb(384, f32),
     "PI": _sb(8, i32), "PJ": _sb(8, i32), "PC": _sb(16, f32), "IC": _sb(160, f32), "IG": _sb(128, f32), "PRI": _sb(384, bf),
-    "EXI": _sb(24, i32), "EXO": _sb(24, u16), "W": _sb(160, bf), "PW0": _sb(160, bf), "PW1": _sb(160, bf),
-    "ONE": _sb(128, f32), "RM": _sb(384, f32), "DM": _sb(384, f32), "SEL": _sb(2048, bf), "DD": _sb(2048, bf),
+    "VI": _sb(32, f32), "IT": _sb(32, bf), "W": _sb(160, bf), "PW0": _sb(160, bf), "PW1": _sb(160, bf),
+    "IDF": _sb([4, 2, 16], f32), "IDD": _sb(64, f32), "ONE": _sb(128, f32), "RM": _sb(384, f32), "DM": _sb(384, f32),
+    "ONES": _sb(512, bf), "SEL": _sb(2048, bf), "DD": _sb(2048, bf),
+    "S0": ("psum", [128, 512], f32), "WL": ("psum", [128, 4, 128], f32), "KP": ("psum", [128, 512], f32),
+    "B3": ("psum", [128, 16, 2, 16], f32), "WP": ("psum", [128, 16, 2, 16], f32), "ZP": ("psum", [128, 16, 32], f32),
+    "RB0": ("psum", [128, 512], f32), "RB1": ("psum", [128, 512], f32),
 }
 for _s in range(S):
     SCRATCH["U%d" % _s] = _sb(384, bf)
@@ -42,37 +42,19 @@ for _s in range(S):
     SCRATCH["UO%d" % _s] = _sb(384, bf)
     SCRATCH["VO%d" % _s] = _sb(384, f32)
 for _s in range(S - 1):
-    SCRATCH["MS%d" % _s] = _sb(48, i32)
-    SCRATCH["RX%d" % _s] = _sb(48, i32)
-for _s in (2, 4, 5, 6, 7):
-    SCRATCH["P%d" % _s] = ("psum", [128, 512], f32)
+    SCRATCH["MS%d" % _s] = _sb([4, 12], i32)
+    SCRATCH["RX%d" % _s] = _sb([4, 12], i32)
 
-SEMAPHORES = ["cg", "cv", "ca", "cp", "sent", "ldL", "ldR", "ldX", "ldC", "ldN", "ldTE", "out0", "out1",
-              "arL", "arP", "arU0h", "arU0t", "arU1", "arU2", "arV0", "arV1", "arV2", "arM0", "arM1"]
+SEMAPHORES = ["cg", "cv", "ca", "cp", "sent", "ldL", "ldR", "ldX", "ldC0", "ldC1", "ldN0", "ldN1", "ldTE", "out0", "out1", "out2",
+              "arL", "arP", "arU0h", "arU0t", "arU1", "arU2", "arV0", "arV1", "arV2", "arT0", "arT1", "arK0", "arK1", "arB0", "arB1",
+              "spU0h", "spU0t", "spU1", "spU2", "spV0", "spV1", "spV2"]
 CNT = {"g": "cg", "v": "cv", "a": "ca", "p": "cp"}
-PEC, HOP = 0.5, 200
-TUNE = {'bias': 20000, 'patience': 1.0, 'turns': 3, 'shy': 1000}
-TUNE.update((k + s, 20) for s in "01" for k in ("EV", "z3p", "z3a", "z3v", "E"))
-TUNE.update((k + s, 30) for s in "01" for k in ("ZS", "QX", "z5a", "RH", "z5p", "R", "Rl", "RO", "vp"))
-TUNE.update((k + "s", 30) for k in ("PO", "OO", "XP", "EP", "UO", "K", "KF", "KO", "CO", "ENO", "OT", "OT0a", "KB", "KA", "KC", "d", "-"))
-TUNE.update({'PE0': -10, 'PE0h': -20, 'PE1': -10, 'PE1h': -10, 'rb0': 10, 'rb1': 10, 'GS2t': -20, 'GS2h': -20, 'GS0': -10,
-             'E1': 10, 'UP1h': 2, 'G1': 1, 'cv0': 5, 'AO1h': 2, 'TBE1': -15, 'cv1': 5, 'G2h': -20, 'UP2t': 10,
-             'UPas': 100, 'QX1': 31, 'POs': 25, 'T0': 25, 'LT2h': 2, 'OT1': -5, 'G0': 2, 'PE2h': -10, 'RH2h': 1})
-TUNE.update({'wl0': 30, 'wl1': 30, 'bias': 2000, 'ENOs': 50, 'TBE1': -25, 'EG0t': 20, 'EG2t': -20, 'sc2t': 20, 'z5a2h': -10, 'OWs': 20,
-             'LB0t': -10, 'RH0': 10, 'z5a1': 29, 'Ks': 40, 'EG2h': -15, 'SV2h': -20, 'sc1h': -20, 'DF0': -5, 'ddSD1': 5, 'LNs': 10,
-             'W0': 20, 'EG0h': 2, 'XG1t': -2, 'PE2t': -11, 'UO0': 5, 'DO1': -2, 'CT1': 5, 'sc2h': 20, 'SK0t': -5, 'XS1': -10, 'ddSD0': 2})
-KEEP = set(['EG0h', 'EG0t', 'EG1t', 'EG2t', 'HA2t', 'QX2t', 'RH1', 'RH2h', 'UP0h', 'UP1t', 'UP2h', 'XG2h', 'ZS0', 'ZS1', 'ZS2h', 'vp0',
-            'vp1'])
+CYC, PEC, HOP, GAT, SCA = 0.85, 0.43, 140, 1.56, 3.8
+LATE = {"ldL": 2200, "ldN1": 2800, "ldN0": 4500, "ldX": 3600, "ldR": 2500, "ldC1": 4600, "ldC0": 5200, "ldTE": 6500}
+TUNE = {"bias": 2000, "patience": 1.0, "turns": 3, "shy": 600}
+LASTUNITS = [(4, 5), (2, 3), (0, 1)]
 _ORDER = {}
-BASE = {"v": 84, "a": 450, "g": 900, "s": 100, "p": 40}
-COST = {"vUPa": 4100, "vUPb": 2100, "vSEL": 1050, "vENO": 404, "vENS": 404, "vXP": 350, "vEP": 350, "vUO": 650, "vVO": 650, "vCO": 650,
-        "vDF": 650, "vW": 180, "vIDF": 150, "vIDB": 150, "vPW": 180, "vONE": 150, "vRM": 404, "vDM": 404, "vHA": 404, "aHA": 450,
-        "vSV": 404, "vLB": 404, "vMX": 404, "vLT": 116, "vSK": 212, "vlo": 212, "vAL": 212, "vYB": 212, "vAO": 116, "vXS": 650,
-        "vEV": 650, "vz": 404, "vE": 404, "aE": 665, "vSD": 404, "vCT": 111, "vTBX": 111, "vTBE": 111, "vR": 404, "vRH": 430, "aRH": 475,
-        "vRO": 836, "vGS": 404, "vGT": 404, "vACC": 788, "aUP": 161, "vZS": 404, "aZS": 450, "vvp": 404, "avp": 450, "vQX": 404,
-        "aQX": 450, "vW8": 404, "aEN": 100, "aXR": 100, "gTBE": 700, "gPI": 140, "gIG": 390, "gIC": 450, "gCI": 260, "gEXI": 180,
-        "gSEL": 4300, "gDD": 4300}
-LATE = {"ldL": 2200, "ldN": 3500, "ldX": 4200, "ldR": 2500, "ldC": 6000, "ldTE": 6500}
+QS = "vagsp"
 
 
 def _order(ops, raised):
@@ -84,7 +66,7 @@ def _order(ops, raised):
             if d[0] == "e":
                 p.append((d[1], 0 if d in soft else HOP))
             elif d[2]:
-                p += [(j, LATE.get(d[1], 2300)) for j in raised[d[1]]]
+                p += [(j, LATE.get(d[1], 2400)) for j in raised[d[1]]]
         pre.append(p)
     post = [[] for _ in ops]
     for i in range(n):
@@ -103,29 +85,27 @@ def _order(ops, raised):
     for i in range(n):
         if ops[i][3] and not pre[i]:
             prio[i] = 1e9 - i
-        tag = ops[i][6]
-        prio[i] += 1000.0 * (TUNE.get(tag, 0) + (TUNE.get(tag[:-1], 0) if tag[-1] in "ht" else 0))
+        prio[i] += 1000.0 * TUNE.get(ops[i][6], 0)
     left = [len(p) for p in pre]
-    ready = {i: 0.0 for i in range(n) if not left[i]}
-    free = {e: 0.0 for e in BASE}
+    ready = {e: {} for e in QS}
+    for i in range(n):
+        if not left[i]:
+            for e in ops[i][5]:
+                ready[e][i] = 0.0
+    free = {e: 0.0 for e in QS}
     out, at, begin = [], [0.0] * n, [0.0] * n
-    while ready:
+    while len(out) < n:
         pick = None
-        for e in free:
-            cand = [i for i in ready if e in ops[i][5]]
+        for e in QS:
+            cand = ready[e]
             if not cand:
                 continue
-            t = max(free[e], min(ready[i] for i in cand))
+            t = max(free[e], min(cand.values()))
             pr = {i: prio[i] - (TUNE["bias"] if e == "v" and len(ops[i][5]) > 1 else 0) for i in cand}
-            if e == "v":
-                cand = [i for i in cand if len(ops[i][5]) == 1 or ops[i][6] not in KEEP]
-                if not cand:
-                    continue
-                t = max(free[e], min(ready[i] for i in cand))
-            top = max(cand, key=lambda i: (pr[i] - max(0.0, ready[i] - t), -i))
-            if ready[top] > t:
-                gap = ready[top] - t
-                now = [i for i in cand if ready[i] <= t]
+            top = max(cand, key=lambda i: (pr[i] - max(0.0, cand[i] - t), -i))
+            if cand[top] > t:
+                gap = cand[top] - t
+                now = [i for i in cand if cand[i] <= t]
                 fits = [i for i in now if ops[i][5][e] <= gap + HOP]
                 if fits:
                     top = max(fits, key=lambda i: (pr[i], -i))
@@ -133,11 +113,12 @@ def _order(ops, raised):
                     b = max(now, key=lambda i: (pr[i], -i))
                     if gap > TUNE["patience"] * (ops[b][5][e] - gap) or pr[top] - pr[b] < ops[b][5][e]:
                         top = b
-            t = max(t, ready[top])
+            t = max(t, cand[top])
             if pick is None or (t, ops[top][5][e]) < pick[0]:
                 pick = ((t, ops[top][5][e]), e, top)
         (t, c), e, i = pick
-        del ready[i]
+        for e2 in ops[i][5]:
+            del ready[e2][i]
         free[e] = t + c
         out.append((i, e))
         begin[i] = t
@@ -145,11 +126,12 @@ def _order(ops, raised):
             left[k] -= 1
             at[k] = max(at[k], t + c + lag)
             if not left[k]:
-                ready[k] = at[k]
+                for e2 in ops[k][5]:
+                    ready[e2][k] = at[k]
     best = (max(free.values()), out)
 
     def pack(seq, before, on, choose):
-        busy, end, res = {e: [] for e in BASE}, [0.0] * n, {}
+        busy, end, res = {e: [] for e in QS}, [0.0] * n, {}
         for i in seq:
             t0, pick = max([end[j] + lag for j, lag in before[i]] or [0.0]), None
             for e in (sorted(ops[i][5]) if choose else [on[i]]):
@@ -187,16 +169,14 @@ def rank_program(g, core, T, topo):
     Q = {"g": g, "v": g.vector, "a": g.scalar, "p": g.tensor, "s": g.sync}
     ops, wr, rd, bank, sent, raised, step = [], {}, {}, {}, [0], {}, ["s"]
 
-    def op(e, f, r="", w="", b="", dma=None, free=False, alt=None, c=None):
+    def op(e, f, r, w, b, c, dma=None, alt=None):
         i = len(ops)
         me = ("s",) + dma if dma else ("e", i)
         deps, soft = set(), set()
         for x in r.split():
             deps.add(wr[x])
         for x in w.split():
-            for d in [wr.get(x)] + rd.get(x, []):
-                if d:
-                    (soft if free else deps).add(d)
+            deps.update(d for d in [wr.get(x)] + rd.get(x, []) if d)
         eng = "?%d" % i if alt else e
         for x in b.split():
             st = bank.setdefault(x, [None, [], []])
@@ -217,12 +197,10 @@ def rank_program(g, core, T, topo):
             rd[x] = []
         if dma and dma[1]:
             raised.setdefault(dma[0], []).append(i)
-        name = (w.split() or ["-"])[0].rstrip("0123456789_")
-        cost = {e: c or COST.get(e + name, BASE[e])}
-        fs = {e: f}
+        fs, cost = {e: f}, {e: c}
         if alt:
-            fs["a"], cost["a"] = alt, COST["a" + name] if c is None else c + 15
-        ops.append((e, fs, deps, dma, soft, cost, (w[:2] + e if name == "z" else name) + step[0]))
+            fs["a"], cost["a"] = alt
+        ops.append((e, fs, deps, dma, soft, cost, (w.split() or ["-"])[0].rstrip("0123456789_") + step[0]))
 
     def mask(dst, a, b):
         return sum(1 << e for e in topo.engines(core, dst)[a:b])
@@ -235,76 +213,93 @@ def rank_program(g, core, T, topo):
                                          remote_sem=T.sem[sem], src=src_ap, dst=dst_ap))
             sent[0] += b - a
             raised.setdefault(sem, []).append(len(ops))
-        op("g", lambda q: q.remote_dma_fused(trs, local_sem=T.sem.sent), r=r, dma=("sent", 0))
+        op("g", lambda q: q.remote_dma_fused(trs, local_sem=T.sem.sent), r, "", "", 900, dma=("sent", 0))
 
-    def tt(out, a, b, o, r, w, bk="", c=None):
-        op("v", lambda q: q.tensor_tensor(out, a, b, o), r, w, bk, c=c)
+    def vns(c, k):
+        return 50 + CYC * (GAT * k if k > 0 else -SCA * k) if k else 20 + CYC * max(64, c)
 
-    def ts(out, a, s1, o0, r, w, bk="", s2=None, o1=None, c=None, alt=None):
+    def ans(c, k):
+        return 65 + CYC * (GAT * k if k else c)
+
+    def tt(out, a, b, o, r, w, bk="", c=0, k=0):
+        op("v", lambda q: q.tensor_tensor(out, a, b, o), r, w, bk, vns(c, k))
+
+    def ts(out, a, s1, o0, r, w, bk="", s2=None, o1=None, c=0, k=0, alt=None):
+        alt = alt and (alt, ans(c, k))
         if o1 is None:
-            op("v", lambda q: q.tensor_scalar(out, a, s1, None, o0), r, w, bk, c=c, alt=alt)
+            op("v", lambda q: q.tensor_scalar(out, a, s1, None, o0), r, w, bk, vns(c, k), alt=alt)
         else:
-            op("v", lambda q: q.tensor_scalar(out, a, s1, s2, o0, o1), r, w, bk, c=c, alt=alt)
+            op("v", lambda q: q.tensor_scalar(out, a, s1, s2, o0, o1), r, w, bk, vns(c, k), alt=alt)
 
-    def cp(out, a, r, w, bk="", free=False, either=False, c=None):
-        op("v", lambda q: q.tensor_copy(out, a), r, w, bk, free=free, c=c,
-           alt=(lambda q: q.activation(out, a, F.Copy)) if either else None)
+    def cp(out, a, r, w, bk="", either=False, c=0, k=0):
+        op("v", lambda q: q.tensor_copy(out, a), r, w, bk, vns(c, k),
+           alt=((lambda q: q.activation(out, a, F.Copy)), ans(c, k)) if either else None)
 
-    def ms(out, c, w):
-        op("v", lambda q: q.memset(out, c), "", w)
+    def ms(out, v, w, c=0, r=""):
+        op("v", lambda q: q.memset(out, v), r, w, "", vns(c, 0))
 
-    def scan(out, a, b, o0, o1, r, w, bk=""):
-        op("v", lambda q: q.tensor_tensor_scan(out, a, b, 0.0, o0, o1), r, w, bk)
+    def scan(out, a, b, o0, o1, r, w, bk, c):
+        op("v", lambda q: q.tensor_tensor_scan(out, a, b, 0.0, o0, o1), r, w, bk, vns(c, 0))
 
-    def act(out, a, fn, r, w, bk="", bias=0.0, scale=1.0, c=None):
-        op("a", lambda q: q.activation(out, a, fn, bias=bias, scale=scale), r, w, bk, c=c)
+    def act(out, a, fn, r, w, bk="", bias=0.0, scale=1.0, c=0, k=0):
+        op("a", lambda q: q.activation(out, a, fn, bias=bias, scale=scale), r, w, bk, ans(c, k))
 
-    def mm(out, l, m, st, sp, r, w, bk, c=64):
-        op("p", lambda q: q.matmul(out, l, m, st, sp), r, w, bk, c=c * PEC)
+    def mms(calls, r, w, bk, c):
+        op("p", lambda q: [q.matmul(*x) for x in calls][-1], r, w, bk, c * PEC * len(calls))
 
     def dma(e, out, a, r, w, sem, val):
-        op(e, lambda q: q.dma_start(out, a), r, w, dma=(sem, val))
+        op(e, lambda q: q.dma_start(out, a), r, w, "", 900 if e == "g" else 100, dma=(sem, val))
 
-    PS = {i: T["P%d" % i] for i in (2, 4, 5, 6, 7)}
+    def pool(f, r, w, c):
+        op("g", f, r, w, "", 150 + 2 * CYC * c)
+
     TX_, TE_ = T.XB[:, 0:M], T.TB[:, 0:M]
-    for x, sem, val in (("RL", "arL", 8), ("XP1", "arP", 8), ("EP1", "arP", 8), ("U0_0", "arU0h", 16), ("U0_1", "arU0t", 8)):
+    for x, sem, val in (("RL", "arL", 16), ("XP1", "arP", 8), ("EP1", "arP", 8), ("U0_0", "arU0h", 16), ("U0_1", "arU0t", 8)):
         wr[x] = ("s", sem, val)
     for s in range(S):
         wr["V%d" % s] = ("s", "arV%d" % s, 16)
         if s:
             wr["U%d_0" % s] = wr["U%d_1" % s] = ("s", "arU%d" % s, 16)
-            wr["RX%d" % (s - 1)] = ("s", "arM%d" % (s - 1), 16)
+            for x in "TKB":
+                wr["RX%s%d" % (x, s - 1)] = ("s", "ar%s%d" % (x, s - 1), 16)
 
     dma("g", TE_, T.ee[:], "", "TBE", "ldTE", 16)
     dma("s", T.LN[:, 0:12], T.tl[:], "", "LN", "ldL", 48)
     dma("s", T.LN[:, 12:24], T.hl[:], "", "LN", "ldL", 48)
     dma("s", T.LN[:, 24:36], T.rl[:], "", "LN", "ldL", 48)
-    dma("a", T.EN[:, :, 192:384], T.nt[:], "", "EN", "ldN", 32)
-    dma("s", TX_, T.xe[:], "", "TBX", "ldX", 16)
     dma("a", T.XR[:], T.xr[:], "", "XR", "ldR", 32)
     dma("a", T.ER[:], T.er[:], "", "XR", "ldR", 32)
-    dma("a", T.EN[:, :, 0:192], T.nh[:], "", "EN", "ldN", 32)
-    dma("s", T.CT[:, NW:NW + NC], T.tc[:], "", "CT0 CT1", "ldC", 32)
-    dma("s", T.CT[:, 0:NC], T.hc[:], "", "CT0 CT1", "ldC", 32)
-    op("g", lambda q: q.iota(T.PI[:, 0:1], [[0, 1]], 0, 1), w="PI")
-    op("g", lambda q: q.iota(T.IG[:], [[16, 8], [0, 16]], 0, 0, allow_small_or_imprecise_dtypes=True), w="IG")
-    op("g", lambda q: q.iota(T.IC[:], [[1, 160]], 0, 0, allow_small_or_imprecise_dtypes=True), w="IC")
-    send("LN", [(nxt, T.LN[:], T.RL[:], "arL", 0, 8)])
-    op("g", lambda q: q.iota(T.CI[:], [[-1, 2], [0, 2], [-2, 16]], 31, 0, allow_small_or_imprecise_dtypes=True), w="CI")
+    dma("a", T.EN[:, :, 192:384], T.nt[:], "", "EN1", "ldN1", 16)
+    dma("s", TX_, T.xe[:], "", "TBX", "ldX", 16)
+    dma("s", T.CT[:, NW:NW + NC], T.tc[:], "", "CT1", "ldC1", 16)
+    dma("a", T.EN[:, :, 0:192], T.nh[:], "", "EN0", "ldN0", 16)
+    dma("s", T.CT[:, 0:NC], T.hc[:], "", "CT0", "ldC0", 16)
+    pool(lambda q: q.iota(T.PI[:, 0:1], [[0, 1]], 0, 1), "", "PI", 1)
+    pool(lambda q: q.iota(T.IC[:], [[1, 160]], 0, 0, allow_small_or_imprecise_dtypes=True), "", "IC", 160)
+    pool(lambda q: q.iota(T.IG[:], [[16, 8], [0, 16]], 0, 0, allow_small_or_imprecise_dtypes=True), "", "IG", 128)
+    pool(lambda q: q.iota(T.VI[:], [[-1, 16], [0, 2]], 15, 0, allow_small_or_imprecise_dtypes=True), "", "VI", 32)
+    pool(lambda q: q.iota(T.PRI[:], [[0, 24], [-1, 16]], 15, 0, allow_small_or_imprecise_dtypes=True), "", "PRI", 384)
+    send("LN", [(nxt, T.LN[:], T.RL[:], "arL", 0, 16)])
 
-    ms(T.UP[:, 0:UPA], 0.0, "UPa")
-    ms(T.KA[:, 0:12], 1.0, "KA0"); ms(T.KA[:, 12:24], 37.0, "KA1"); ms(T.KC[:, 0:12], 0.0, "KC0"); ms(T.KC[:, 12:24], float(NW), "KC1")
+    ms(T.UM[:], 0.0, "UMz", 1536)
+    act(T.VM[:], T.UM[:], F.Copy, "UMz", "VMz", c=3072)
+    ms(T.KA[:, 0:12], 1.0, "KA0"); ms(T.KA[:, 12:24], 37.0, "KA1")
     ms(T.TB[:, M:EO], 0.0, "d0"); ms(T.XB[:, M:EO], 0.0, "d1"); ms(T.CT[:, NC:NW], 0, "d2"); ms(T.CT[:, NW + NC:2 * NW], 0, "d3")
-    ts(T.PJ[:, 0:1], T.PI[:, 0:1], 15, A.bitwise_and, "PI", "PJ0")
-    ts(T.PJ[:, 1:2], T.PI[:, 0:1], 4, A.arith_shift_right, "PI", "PJ1", s2=1, o1=A.bitwise_and)
-    cp(T.ENO[:, 0:384], T.EN[:, 0, :], "EN", "ENO0")
+    ms(T.ONES[:], 1.0, "ONES", 256)
+    ms(T.RM[:], 0.0, "RM", 384); ms(T.RM[:, 0:384:32], -1.0e9, "RM")
+    ms(T.RW[:, :, 16], 1.0, "RWc"); ms(T.RH[:, :, 0], 0.0, "RHc"); ms(T.RO[:, :, 0], 0.0, "ROc")
     cp(T.PO[:], T.LN[:, 24:36], "LN", "PO")
     cp(T.OO[:, 0:12], T.LN[:, 12:24], "LN", "OO0")
-    cp(T.XP[:, 0:L], T.XR[:, 0:64].indirect(T.PO[:, 0:12]), "XR PO", "XP0")
-    cp(T.EP[:, 0:L], T.ER[:, 0:64].indirect(T.PO[:, 0:12]), "XR PO", "EP0")
-    tt(T.UO0[:, 0:L], T.XB[:, 0:M].indirect(T.OO[:, 0:12]), T.XP[:, 0:L], A.mult, "TBX OO0 XP0", "UO0_0")
+    cp(T.XP[:, 0:L], T.XR[:, 0:64].indirect(T.PO[:, 0:12]), "XR PO", "XP0", k=L)
+    ts(T.EP[:, 0:L], T.ER[:, 0:64].indirect(T.PO[:, 0:12]), 0.125, A.mult, "XR PO", "EP0", k=L)
+    tt(T.UO0[:, 0:L], TX_.indirect(T.OO[:, 0:12]), T.XP[:, 0:L], A.mult, "TBX OO0 XP0", "UO0_0", k=L)
     send("XP0 EP0 UO0_0", [(nxt, T.XP[:, 0:L], T.XP[:, L:384], "arP", 0, 4), (nxt, T.EP[:, 0:L], T.EP[:, L:384], "arP", 4, 8),
                            (nxt, T.UO0[:, 0:L], T.U0[:, L:384], "arU0t", 8, 16)])
+    ts(T.PJ[:, 0:1], T.PI[:, 0:1], 15, A.bitwise_and, "PI", "PJ0")
+    ts(T.PJ[:, 1:2], T.PI[:, 0:1], 4, A.arith_shift_right, "PI", "PJ1", s2=1, o1=A.bitwise_and)
+    ts(T.PJ[:, 2:3], T.PI[:, 0:1], 1, A.arith_shift_right, "PI", "PJ2")
+    ts(T.PJ[:, 3:4], T.PI[:, 0:1], 1, A.bitwise_and, "PI", "PJ3")
+    ts(T.PJ[:, 4:5], T.PI[:, 0:1], 31, A.bitwise_and, "PI", "PJ4")
     cp(T.PC[:, 0:1], T.PJ[:, 0:1], "PJ0", "PC0")
     tt(T.PC[:, 1:2], T.PI[:, 0:1], T.PJ[:, 0:1], A.subtract, "PI PJ0", "PC1")
     ts(T.PC[:, 2:3], T.PC[:, 1:2], 15.0, A.add, "PC1", "PC2")
@@ -312,312 +307,296 @@ def rank_program(g, core, T, topo):
     cp(T.PC[:, 4:5], T.PJ[:, 1:2], "PJ1", "PC4")
     ts(T.PC[:, 5:6], T.PJ[:, 1:2], -1.0, A.mult, "PJ1", "PC5", s2=1.0, o1=A.add)
     ts(T.PC[:, 6:7], T.PJ[:, 0:1], float(M), A.add, "PJ0", "PC6")
-    ts(T.PC[:, 8:9], T.PJ[:, 0:1], float(M - 1568), A.add, "PJ0", "PC8")
+    ts(T.PC[:, 12:13], T.PJ[:, 3:4], 2.0, A.mult, "PJ3", "PC12", s2=float(30 + KEY0), o1=A.add)
+    tt(T.PC[:, 8:9], T.PC[:, 12:13], T.PJ[:, 4:5], A.subtract, "PC12 PJ4", "PC8")
     ts(T.PC[:, 9:10], T.PJ[:, 0:1], float(NC), A.add, "PJ0", "PC9")
+    cp(T.PC[:, 10:11], T.PJ[:, 2:3], "PJ2", "PC10")
+    ts(T.PC[:, 11:12], T.PJ[:, 3:4], 2.0, A.mult, "PJ3", "PC11", s2=-1.0, o1=A.add)
     cp(T.OW[:, 0:12], T.LN[:, 12:24], "LN", "OW0a"); cp(T.OT[:, 0:12], T.LN[:, 0:12], "LN", "OT0a")
     ts(T.KB[:, 0:12], T.LN[:, 24:36], 37.0, A.mult, "LN", "KB0")
-    ts(T.ONE[:], T.IG[:], T.PC[:, 1:2], A.is_equal, "IG PC1", "ONE")
-    ts(T.MG[:], T.ONE[:, 0:128:16], 32.0, A.mult, "ONE", "MG")
     cp(T.OO[:, 12:24], T.RL[:, 0:12], "RL", "OO1")
     cp(T.OT[:, 12:24], T.RL[:, 12:24], "RL OT0a", "OT0")
     cp(T.KB[:, 12:24], T.RL[:, 24:36], "RL", "KB1")
+    cp(T.OW[:, 12:24], T.RL[:, 0:12], "RL OW0a", "OW0")
+    ts(T.IDF[:], T.IC[:, 16:144], T.PC[:, 3:4], A.is_equal, "IC PC3", "IDF", c=128)
+    ts(T.IDD[:], T.IC[:, 0:64], T.PC[:, 10:11], A.is_equal, "IC PC10 PC11", "IDD", s2=T.PC[:, 11:12], o1=A.mult)
+    ts(T.IT[:], T.VI[:], T.PC[:, 0:1], A.is_equal, "VI PC0", "IT")
+    ts(T.ONE[:], T.IG[:], T.PC[:, 1:2], A.is_equal, "IG PC1", "ONE", c=128)
+    ts(T.W[:], T.IC[:], T.PC[:, 2:3], A.is_equal, "IC PC2", "W", s2=1.0 / 64, o1=A.mult, c=160)
+    ts(T.PW0[:], T.IC[:], T.PC[:, 3:4], A.is_equal, "IC PC3 PC5", "PW0", s2=T.PC[:, 5:6], o1=A.mult, c=160)
+    ts(T.PW1[:], T.IC[:], T.PC[:, 3:4], A.is_equal, "IC PC3 PC4", "PW1", s2=T.PC[:, 4:5], o1=A.mult, c=160)
+    ts(T.DM[:], T.PRI[:], T.PC[:, 0:1], A.is_equal, "PRI PC0", "DM", c=384)
+    for x in range(4):
+        c = slice(512 * x, 512 * x + 512)
+        pool(lambda q, c=c, x=x: q.affine_select(T.SEL[:, c], T.ONES[:], [[-1, 4], [-16, 8], [0, 16]], A.is_equal, 0.0, -4 * x, 1),
+             "ONES", "SEL%d" % x, 512)
+        pool(lambda q, c=c: q.affine_select(T.DD[:, c], T.SEL[:, c], [[0, 4], [-16, 8], [-1, 16]], A.not_equal, -1.0, 0, 1),
+             "SEL%d" % x, "DD%d" % x, 512)
+    for x in range(8):
+        ms(T.DD[:, 16 * x:16 * x + 129 * 15 + 1:129], 0.0, "DDz%d" % x, r="DD0 DD1 DD2 DD3")
+    DDN = " ".join("DDz%d" % x for x in range(8))
 
     def keys(s):
         tt(T.K1[:], T.OT[:, 24 * s:24 * s + 24], T.KA[:], A.mult, "OT%d KA0 KA1" % s, "K1")
         tt(T.K2[:], T.K1[:], T.KB[:], A.add, "K1 KB0 KB1", "K2")
         ts(T.K3[:], T.K2[:], NC - 1, A.bitwise_and, "K2", "K3")
-        tt(T.KF[:], T.K3[:], T.KC[:], A.add, "K3 KC0 KC1", "KF")
-        cp(T.KO[:], T.KF[:], "KF", "KO")
+        cp(T.KO[:], T.K3[:], "K3", "KO")
 
     def cands(s):
-        win = T.CT[:, 0:2 * NW].indirect(T.KO[:, 0:24])
-        cp(T.CO[:], win, "CT0 CT1 d2 d3 KO", "CO")
-        tt(T.DF[:], win, T.EN[:, s, :], A.subtract, "CT0 CT1 d2 d3 KO EN", "DF")
+        for d in (1, 0):
+            c = slice(L * d, L * d + L)
+            win = T.CT[:, NW * d:NW * d + NW].indirect(T.KO[:, 12 * d:12 * d + 12])
+            cp(T.CO[:, c], win, "CT%d d2 d3 KO" % d, "CO%d" % d, k=L)
+            tt(T.DF[:, c], win, T.EN[:, s, c], A.subtract, "CT%d d2 d3 KO EN%d" % (d, d), "DF%d" % d, k=L)
 
-    keys(0)
-    cands(0)
-    tt(T.UO0[:, L:384], T.XB[:, 0:M].indirect(T.OO[:, 12:24]), T.XP[:, L:384], A.mult, "TBX OO1 XP1", "UO0_1")
-    send("UO0_1", [(prv, T.UO0[:, L:384], T.U0[:, 0:L], "arU0h", 0, 16)])
+    def entrants(s):
+        for d in (1, 0):
+            c = slice(384 * s + L * d, 384 * s + L * d + L)
+            cp(T.ENO[:, c], T.EN[:, s, L * d:L * d + L], "EN%d" % d, "ENO%d_%d" % (s, d), c=L)
+            ts(T.ENS[:, c], T.ENO[:, c], -1536.0, A.add, "ENO%d_%d" % (s, d), "ENS%d_%d" % (s, d), c=96)
+
+    def spread(name, s, ds, sem):
+        a, b = L * ds[0], L * ds[-1] + L
+        for x in range(8):
+            p = slice(16 * x, 16 * x + 16)
+            dma("s", T[name + "M"][p, x, a:b], T["%s%d" % (name, s)][p, a:b],
+                name + "Mz " + (" ".join("U%d_%d" % (s, d) for d in ds) if name == "U" else "V%d" % s),
+                " ".join("%sM%d_%d" % (name, d, x) for d in ds), sem, 128)
 
     def vsend(s):
-        tt(T["VO%d" % s][:], TE_.indirect(T.OO[:, 0:24]), T.EP[:], A.mult, "TBE OO0 OO1 EP0 EP1", "VO%d" % s)
+        tt(T["VO%d" % s][:], TE_.indirect(T.OO[:, 0:24]), T.EP[:], A.mult, "TBE OO0 OO1 EP0 EP1", "VO%d" % s, k=384)
         send("VO%d" % s, [(nxt, T["VO%d" % s][:, 0:L], T["V%d" % s][:, L:384], "arV%d" % s, 0, 8),
                           (prv, T["VO%d" % s][:, L:384], T["V%d" % s][:, 0:L], "arV%d" % s, 8, 16)])
 
+    def usend(s):
+        tt(T["UO%d" % s][:], TX_.indirect(T.OO[:, 0:24]), T.XP[:], A.mult, "TBX OO0 OO1 XP0 XP1", "UO%d" % s, k=384)
+        send("UO%d" % s, [(nxt, T["UO%d" % s][:, 0:L], T["U%d" % s][:, L:384], "arU%d" % s, 0, 8),
+                          (prv, T["UO%d" % s][:, L:384], T["U%d" % s][:, 0:L], "arU%d" % s, 8, 16)])
+        spread("U", s, (0, 1), "spU%d" % s)
+
+    keys(0)
+    entrants(0)
+    cands(0)
+    spread("U", 0, (1,), "spU0t")
+    tt(T.UO0[:, L:384], TX_.indirect(T.OO[:, 12:24]), T.XP[:, L:384], A.mult, "TBX OO1 XP1", "UO0_1", k=L)
+    send("UO0_1", [(prv, T.UO0[:, L:384], T.U0[:, 0:L], "arU0h", 0, 16)])
+    spread("U", 0, (0,), "spU0h")
     vsend(0)
-    ms(T.UP[:, UPA:12304], 0.0, "UPb")
-    ms(T.SEL[:], 1.0, "SEL")
-    cp(T.OW[:, 12:24], T.RL[:, 0:12], "RL OW0a", "OW0")
-    op("g", lambda q: q.iota(T.PRI[:], [[0, 24], [-1, 16]], 15, 0, allow_small_or_imprecise_dtypes=True), w="PRI")
-    op("g", lambda q: q.iota(T.EXI[:], [[16, 24]], 15, 0), w="EXI")
-    op("g", lambda q: q.affine_select(T.SEL[:], T.SEL[:], [[-1, 16], [-16, 8], [0, 16]], A.is_equal, 0.0, 0, 1), "SEL", "SEL")
-    op("g", lambda q: q.affine_select(T.DD[:], T.SEL[:], [[0, 16], [-16, 8], [-1, 16]], A.not_equal, -1.0, 0, 1), "SEL", "DD")
-    op("g", lambda q: q.affine_select(T.DD[:], T.DD[:], [[-1, 16], [0, 8], [1, 16]], A.not_equal, 0.0, 0, 0), "DD", "DD")
+    spread("V", 0, (0, 1), "spV0")
+    entrants(1)
+    entrants(2)
 
-    def consts():
-        ts(T.PJ[:, 2:3], T.PI[:, 0:1], 1, A.bitwise_and, "PI", "PJ2")
-        ts(T.IDB[:], T.IC[:, 16:144], T.PC[:, 3:4], A.is_equal, "IC PC3", "IDB")
-        ts(T.PC[:, 10:11], T.PJ[:, 2:3], -BIG, A.mult, "PJ2", "PC10")
-        ts(T.PC[:, 11:12], T.PJ[:, 2:3], BIG, A.mult, "PJ2", "PC11", s2=-BIG, o1=A.add)
-        ts(T.ENS[:, 0:384], T.EN[:, 0, :], -1536.0, A.add, "EN", "ENS0")
-        for x in range(4):
-            ts(T.CZ[:, x, :], T.CI[:, 16 * x:16 * x + 16], T.PC[:, 10 + x % 2:11 + x % 2], A.add, "CI PC10 PC11", "CZ%d" % x)
+    def names(pat, xs):
+        return " ".join(pat % x for x in xs)
 
-    def consts2():
-        ts(T.W[:], T.IC[:], T.PC[:, 2:3], A.is_equal, "IC PC2", "W")
-        ts(T.IDF[:], T.IC[:, 16:144], T.PC[:, 3:4], A.is_equal, "IC PC3", "IDF")
-        ts(T.PW0[:], T.IC[:], T.PC[:, 3:4], A.is_equal, "IC PC3 PC5", "PW0", s2=T.PC[:, 5:6], o1=A.mult)
-        ts(T.PW1[:], T.IC[:], T.PC[:, 3:4], A.is_equal, "IC PC3 PC4", "PW1", s2=T.PC[:, 4:5], o1=A.mult)
-        ts(T.RM[:], T.PRI[:], 15.0, A.is_equal, "PRI", "RM", s2=-1.0e9, o1=A.mult)
-        ts(T.DM[:], T.PRI[:], T.PC[:, 0:1], A.is_equal, "PRI PC0", "DM")
-        cp(T.EXO[:], T.EXI[:], "EXI", "EXO")
+    def sides(xs):
+        return sorted(set(x // 3 for x in xs))
 
-    def entrants(s):
-        c = slice(384 * s, 384 * s + 384)
-        ts(T.ENS[:, c], T.EN[:, s, :], -1536.0, A.add, "EN", "ENS%d" % s)
-        ts(T.ENO[:, c], T.ENS[:, c], 1536.0, A.add, "ENS%d" % s, "ENO%d" % s, c=212)
-
-    def xgather(s, d):
-        for h in range(3):
-            for ent in (1, 0):
-                a, o = 64 * h, 384 * s + L * d
-                off, on = (T.ENO[:, o + a:o + a + 64], "ENO%d" % s) if ent else (T.CO[:, L * d + a:L * d + a + 64], "CO")
-                cp(T["XG%d" % d][:, ent, 16 * a:16 * a + 1024], TX_.indirect(off), "TBX " + on, "XG%d_%d_%d" % (d, ent, h),
-                   either=True, c=1650)
-
-    UPN = " ".join("UP%d" % x for x in range(16))
-
-    def spread(s, d):
-        for x in range(16):
-            gg, h = divmod(x, 2)
-            o = 16 * gg + 14 + h
-            out, src, m = T.UP[:, o:o + 128 * 95 + 1:128], T["U%d" % s][:, L * d + h:L * d + L:2], T.MG[:, gg:gg + 1]
-            ts(out, src, m, A.mult, "U%d_%d MG UPa UPb" % (s, d), "UP%d" % x,
-               alt=lambda q, out=out, src=src, m=m: q.activation(out, src, F.Copy, scale=m))
-
-    def scores(d):
-        for c in range(12):
-            row = 24 * (1 - d) + 2 * c
-            out, bk = T.SC[:, row:row + 2, :, :], "s%d" % (row // 16)
-            mm(out, T.IDB[:], T.CZ[:], True, False, "IDB CZ0 CZ1 CZ2 CZ3", "sc%d" % d, bk)
-            for t in range(8):
-                q = 8 * c + t
-                o = 128 * q + 14 - 2 * t
-                mm(out, T.UP[:, o:o + 128], T["XG%d" % d][:, :, 32 * q:32 * q + 32], False, t == 7,
-                   "%s XG%d_0_%d XG%d_1_%d" % (UPN, d, c // 4, d, c // 4), "sc%d" % d, bk)
-
-    def turn(a, row, r, w):
-        op("v", lambda q: q.transpose(T.LT[:, a // 16:a // 16 + 12, :], T.LB[:, a:a + L]), r, "LT%d" % a)
-        for h in range(2):
-            for g2 in range(2):
-                o = 16 + 16 * (h - g2)
-                mm(T.SC[:, row:row + 6, h, :], T["PW%d" % h][:, o:o + 128], T.LT[:, a // 16 + g2:a // 16 + 12:2, :], g2 == 0, g2 == 1,
-                   "PW0 PW1 LT%d" % a, w, "s%d" % (row // 16), 96)
-
-    def contest(s, d):
-        c = slice(L * d, L * d + L)
-        r0, r1, both, bk = 24 * (1 - d), 32 * (1 - d), ("s1 s2", "s0 s1")[d], ("s2", "s0")[d]
-        oh, lo = T.SC[:, r1:r1 + 6, :, :], T.SC[:, r1 + 6:r1 + 12, :, :]
-        cp(T.HA[:], T.SC[:, r0:r0 + 24, 0, :], "sc%d" % d, "HA", both, either=True)
-        tt(T.SV[:], T.SC[:, r0:r0 + 24, 1, :], T.HA[:], A.max, "sc%d HA" % d, "SV", both)
-        tt(T.LB[:, 0:L], T.SV[:, 0:24:2, :], T.SV[:, 1:24:2, :], A.is_gt, "SV", "LB0")
+    def scores(s, x, slot):
+        a, d = 64 * x, x // 3
+        cp(T.XG[:, 32 * a:32 * a + 2048:2], TX_.indirect(T.ENO[:, 384 * s + a:384 * s + a + 64]), "TBX ENO%d_%d" % (s, d),
+           "XG%d_0" % x, either=True, k=1024)
+        cp(T.XG[:, 32 * a + 1:32 * a + 2048:2], TX_.indirect(T.CO[:, a:a + 64]), "TBX CO%d" % d, "XG%d_1" % x, either=True, k=1024)
+        P, bk = T.S0, "b0"
+        for q4 in range(4):
+            mms([(P[32 * q4:32 * q4 + 32, j:128:16], T.XG[:, 32 * l:32 * l + 32], T.UM[:, :, l], True, True)
+                 for j in range(16) for l in [a + 16 * q4 + j]], "XG%d_0 XG%d_1 " % (x, x) + names("UM%d_%%d" % d, range(8)),
+                "sc%d" % q4, bk, 32)
+        o, src = T.SCP[:, 128 * x:128 * x + 128], P[:, 0:128]
+        ts(o, src, 32.0, A.mult, names("sc%d", range(4)) + " PC8", "SCP%d" % x, bk, s2=T.PC[:, 8:9], o1=A.add, c=128,
+           alt=lambda q: q.activation(o, src, F.Identity, bias=T.PC[:, 8:9], scale=32.0))
+        mms([(T.B3[:, 2 * slot:2 * slot + 2, :, :], o, T.IDD[:], True, True)], "SCP%d IDD" % x, "D%d" % slot, "b3", 256)
         if s < S - 1:
-            tt(T.MX[:], T.SV[:, 0:24:2, :], T.SV[:, 1:24:2, :], A.max, "SV", "MX")
-        turn(0, r1 + 6, "LB0", "lo%d" % d)
-        if s < S - 1:
-            scan(T.SK[:, c], T.RM[:, 0:L], T.MX[:], A.add, A.max, "RM MX", "SK%d" % d)
-            tt(T.LB[:, L:384], T.SK[:, c].indirect(T.EXO[:, 0:12]), T.MX[:], A.is_equal, "SK%d EXO MX" % d, "LB1")
-            turn(L, r1, "LB1", "oh%d" % d)
-        tt(lo, lo, T.DF[:, c], A.mult, "lo%d DF" % d, "lo%d" % d, bk)
-        tt(T.AL[:, c], lo, T.ENS[:, 384 * s + L * d:384 * s + L * d + L], A.add, "lo%d ENS%d" % (d, s), "AL%d" % d, bk)
-        if s < S - 1:
-            tt(T.YB[:, c], oh, T.AL[:, c], A.mult, "oh%d AL%d" % (d, d), "YB%d" % d, bk)
-        ts(T.AO[:, c], T.AL[:, c], 1536.0, A.add, "AL%d" % d, "AO%d" % d)
+            mms([(T.KP[:, 128 * slot:128 * slot + 128], o, T.IDF[:], True, True)], "SCP%d IDF" % x, "K%d" % slot, "b2", 512)
 
-    def egather(s, d):
-        for h in range(2):
-            a = L * d + 96 * h
-            cp(T["EG%d" % (s & 1)][:, 16 * a:16 * a + 1536], TE_.indirect(T.AO[:, a:a + 96]), "TBE AO%d" % d,
-               "EG%d_%d" % (s & 1, 2 * d + h), either=True, c=2450)
+    def contest(s, xs):
+        m, a = len(xs), 64 * xs[0]
+        c, c4 = slice(a, a + 64 * m), a // 16
+        ts(T.LB[:, c], T.B3[:, 0:2 * m, :, :], 0.0, A.is_gt, names("D%d", range(m)), names("LB%d", xs), "b3", c=64 * m)
+        op("v", lambda q: q.transpose(T.LT[:, c4:c4 + 4 * m, :], T.LB[:, c]), names("LB%d", xs), names("LT%d", xs), "", vns(32 * m, 0))
+        lo = T.B3[:, 6:6 + 2 * m, :, :]
+        mms([(T.B3[:, 6:6 + 2 * m, h, :], T["PW%d" % h][:, o:o + 128], T.LT[:, c4 + g2:c4 + 4 * m:2, :], g2 == 0, g2 == 1)
+             for h in range(2) for g2 in range(2) for o in [16 + 16 * (h - g2)]], "PW0 PW1 " + names("LT%d", xs), "lo", "b3", max(64, 32 * m))
+        tt(lo, lo, T.DF[:, c], A.mult, "lo " + names("DF%d", sides(xs)), "lo", "b3", c=64 * m)
+        tt(T.AL[:, c], lo, T.ENS[:, 384 * s + a:384 * s + a + 64 * m], A.add, "lo " + names("ENS%d_%%d" % s, sides(xs)),
+           names("AL%d", xs), "b3", c=64 * m)
+        ts(T.AO[:, c], T.AL[:, c], 1536.0, A.add, names("AL%d", xs), names("AO%d", xs), c=32 * m)
+        for x in xs:
+            cp(T["EG%d" % (s & 1)][:, 1024 * x:1024 * x + 1024], TE_.indirect(T.AO[:, 64 * x:64 * x + 64]), "TBE AO%d" % x,
+               "EG%d_%d" % (s & 1, x), either=True, k=1024)
 
-    def best(s):
-        MS = T["MS%d" % s]
-        for j in range(16):
-            mm(PS[4][:, 384:408], T.W[:, 15 - j:143 - j], T.YB[:, j:384:16], j == 0, j == 15, "W YB0 YB1", "cv", "b4")
-        ts(MS[:, 0:48:2], T.SK[:, 15:384:16], 1.0 / 32, A.mult, "SK0 SK1", "MSa%d" % s, s2=-15.5 / 32, o1=A.add)
-        ts(MS[:, 1:48:2], PS[4][:, 384:408], 1536.0, A.add, "cv", "MSb%d" % s, "b4")
-        send("MSa%d MSb%d" % (s, s), [(nxt, MS[:, 0:24], T["RX%d" % s][:, 24:48], "arM%d" % s, 0, 8),
-                                      (prv, MS[:, 24:48], T["RX%d" % s][:, 0:24], "arM%d" % s, 8, 16)])
-        ts(T.BO[:], PS[4][:, 384:408], 1536.0, A.add, "cv", "BO", "b4")
+    def best(s, d):
+        MS, RX, c, h = T["MS%d" % s], T["RX%d" % s], slice(L * d, L * d + L), slice(12 * d, 12 * d + 12)
+        top = T.SK[:, 384 * d + 31:384 * d + 384:32]
+        scan(T.SK[:, 384 * d:384 * d + 384], T.RM[:], T.KP[:, 0:384], A.add, A.max, "RM K0 K1 K2", "SK%d" % d, "b2", 384)
+        ki, kn = (T.KI[:], "KI") if d else (MS[:, 0, :], "MK%d" % s)
+        cp(ki, top, "SK%d" % d, kn)
+        if d:
+            ts(MS[:, 3, :], ki, (1 << 19) - 32, A.bitwise_and, kn, "MF%d" % s)
+        else:
+            send(kn, [(nxt, MS[:, 0, :], RX[:, 3, :], "arK%d" % s, 0, 16)])
+            tt(T.MI[:, h], top, RX[:, 1, :], A.is_ge, "SK0 RXT%d" % s, "MI0")
+            ts(T.LM[:], T.MI[:, h], 32.0, A.mult, "MI0", "LM", s2=-32.0, o1=A.add)
+        ts(T.KL[:, h], ki, 31, A.bitwise_and, kn, "KL%d" % d)
+        cp(T.KS[:, h], T.KL[:, h], "KL%d" % d, "KS%d" % d)
+        tt(T.YB[:, c], T.IT[:, 0:32].indirect(T.KS[:, h]), T.AL[:, c], A.mult, "IT KS%d " % d + names("AL%d", range(3 * d, 3 * d + 3)),
+           "YB%d" % d, k=L)
+        cv = T.B3[:, 12, d, 0:12]
+        mms([(cv, T.W[:, 15 - j:143 - j], T.YB[:, L * d + j:L * d + L:16], j == 0, j == 15) for j in range(16)], "W YB%d" % d,
+            "cv%d" % d, "b3", 64)
+        if d == 0:
+            tt(T.T1[:, h], cv, T.MI[:, h], A.mult, "cv0 MI0", "T1_0", "b3")
+            tt(T.B16[:, h], T.T1[:, h], T.LM[:], A.add, "T1_0 LM", "B16_0")
+        ts(MS[:, 1 + d, :], cv, 64.0, A.mult, "cv%d" % d, "MB%d_%d" % (s, d), "b3", s2=1536.0, o1=A.add)
+        if d:
+            send("MB%d_1 MF%d" % (s, s), [(prv, MS[:, 2:4, :], RX[:, 0:2, :], "arT%d" % s, 0, 16)])
+            ts(T.CP[:], cv, 32.0, A.add, "cv1", "CP", "b3")
+        else:
+            send("MB%d_0" % s, [(nxt, MS[:, 1, :], RX[:, 2, :], "arB%d" % s, 0, 16)])
+        ts(T.BO[:, h], cv, 64.0, A.mult, "cv%d" % d, "BO%d" % d, "b3", s2=1536.0, o1=A.add)
+        ts(T.BD[:, h], MS[:, 1 + d, :], T.PC[:, 6:7], A.subtract, "MB%d_%d PC6" % (s, d), "BD%d" % d)
+        tt(T.XS[:, c], TX_.indirect(T.BO[:, h]), T.SG[:, c], A.subtract, "TBX BO%d SG%d" % (d, d), "XS%d" % d, k=L)
+        ts(T.XS[:, c], T.XS[:, c], -7.0, A.max, "XS%d" % d, "XS%d" % d, s2=7.0, o1=A.min, c=96)
 
-    WZ = T.SC[:, 0:12, :, :]
+    def firsts(src, nm, outs, whole, bk, out, on, m):
+        mms([(outs(15 - j), T.DD[:, 128 * j:128 * j + 128], src, True, True) for j in range(16)], DDN + " " + nm, on[1], bk, 64)
+        scan(out, whole, T.DM[:, 0:m], A.mult, A.add, on[1] + " DM", on[0], bk, m)
 
-    def propose1(s):
-        V = T["V%d" % s]
-        tt(T.XS[:], TX_.indirect(T.BO[:, 0:24]), T.SG[:], A.subtract, "TBX BO SG", "XS")
-        tt(T.EV[:], TE_.indirect(T.BO[:, 0:24]), V[:], A.mult, "TBE BO V%d" % s, "EV")
-        mm(WZ, T.ONE[:], T.EV[:], True, True, "ONE EV", "z3", "s0", 1536)
-        act(T.E7[:], TE_.indirect(T.BO[:, 0:24]), F.Copy, "TBE BO", "E7", scale=0.875)
-        act(WZ, WZ, F.Sigmoid, "z3", "z3", "s0", scale=0.0625)
-        act(WZ, WZ, F.Copy, "z3", "z3", "s0", scale=0.125)
-        ts(T.XS[:], T.XS[:], -7.0, A.max, "XS", "XS", s2=7.0, o1=A.min, c=212)
-        ts(T.BD[:], T["MS%d" % s][:, 1:48:2], T.PC[:, 6:7], A.subtract, "MSb%d PC6" % s, "BD")
-        tt(T.DO[:], T["MS%d" % s][:, 1:48:2], T.OW[:, 24 * s:24 * s + 24], A.subtract, "MSb%d OW%d" % (s, s), "DO")
+    def targets(s, d):
+        MS, RX, c, h = T["MS%d" % s], T["RX%d" % s], slice(L * d, L * d + L), slice(12 * d, 12 * d + 12)
+        if d:
+            tt(T.MI[:, h], MS[:, 3, :], RX[:, 3, :], A.is_gt, "MF%d RXK%d" % (s, s), "MI1")
+            tt(T.T1[:, h], T.CP[:], T.MI[:, h], A.mult, "CP MI1", "T1_1")
+            ts(T.B16[:, h], T.T1[:, h], -32.0, A.add, "T1_1", "B16_1")
+        tt(T.BM[:, h], T.BD[:, h], T.MI[:, h], A.mult, "BD%d MI%d" % (d, d), "BM%d" % d)
+        firsts(T.B16[:, h], "B16_%d" % d, lambda i: T.S0[:, 128 + i:128 + L:16], T.S0[:, 128:128 + L], "b0", T.SD[:, c], ("SD%d" % d, "dd"), L)
+        ts(T.ND[:, h], T.SD[:, L * d + 15:L * d + L:16], 0.0, A.not_equal, "SD%d" % d, "ND%d" % d)
+        tt(T.T2[:, h], T.ND[:, h], T.BM[:, h], A.mult, "ND%d BM%d" % (d, d), "T2_%d" % d)
+        ts(T.SO[:, 24 * d:24 * d + 24:2], T.T2[:, h], T.PC[:, 6:7], A.add, "T2_%d PC6" % d, "SO%d" % d)
 
-    def propose2(s):
-        tt(WZ, WZ, T["V%d" % s][:], A.mult, "V%d z3" % s, "z3", "s0")
-        tt(T.E7[:], WZ, T.E7[:], A.add, "z3 E7", "E7", "s0")
+    def write(e, d):
+        for c in range(12 * d + 11, 12 * d - 1, -1):
+            at, p = T.SO[:, 2 * c:2 * c + 1], slice(16 * c, 16 * c + 16)
+            if e:
+                tt(T.TB[:, 0:EO].indirect(at), T.E7[:, p], T.WV[:, p], A.add, "SO%d d0 E7 WV" % d, "TBE", k=-16)
+            else:
+                cp(T.XB[:, 0:EO].indirect(at), T.XS[:, p], "SO%d d1 XS%d" % (d, d), "TBX", k=-16)
 
-    def firsts(src, nm, p, bk, out, on):
-        for j in range(16):
-            mm(PS[p][:, 15 - j:384:16], T.DD[:, 128 * j:128 * j + 128], src, True, True, "DD " + nm, "dd" + on, bk)
-        scan(out, PS[p][:, 0:384], T.DM[:], A.mult, A.add, "dd%s DM" % on, on, bk)
+    def proposals(s):
+        V, Z = T["V%d" % s], T.KP[:, 0:384]
+        tt(T.EV[:], TE_.indirect(T.BO[:, 0:24]), V[:], A.mult, "TBE BO0 BO1 V%d" % s, "EV", k=384)
+        mms([(Z, T.ONE[:], T.EV[:], True, True)], "ONE EV", "K0 K1 K2", "b2", 1536)
+        act(T.E7[:], TE_.indirect(T.BO[:, 0:24]), F.Copy, "TBE BO0 BO1", "E7", scale=0.875, k=384)
+        act(Z, Z, F.Sigmoid, "K0", "K0 K1 K2", "b2", scale=0.5, c=384)
+        tt(T.WV[:], Z, V[:], A.mult, "V%d K0" % s, "WV", "b2", c=384)
 
-    def cache1():
+    def cache_targets():
         ts(T.K16[:], T.K3[:], 1.0 / 64, A.mult, "K3", "K16")
         ts(T.C1[:], T.K3[:], T.PC[:, 9:10], A.subtract, "K3 PC9", "C1")
-
-    def cache2(p):
-        firsts(T.K16[:], "K16", p, "b%d" % p, T.SD[:], "SD")
-        ts(T.NE[:], T.SD[:, 15:384:16], 0.0, A.not_equal, "SD", "NE")
+        firsts(T.K16[:], "K16", lambda i: T.KP[:, i:384:16], T.KP[:, 0:384], "b2", T.SE[:], ("SE", "K0 K1 K2"), 384)
+        ts(T.NE[:], T.SE[:, 15:384:16], 0.0, A.not_equal, "SE", "NE")
         tt(T.C2[:], T.NE[:], T.C1[:], A.mult, "NE C1", "C2")
         ts(T.CSO[:, 0:48:2], T.C2[:], T.PC[:, 9:10], A.add, "C2 PC9", "CSO")
 
-    def cache3():
-        for c in range(23, -1, -1):
-            d = c // 12
-            cp(T.CT[:, NW * d:NW * d + NW].indirect(T.CSO[:, 2 * c:2 * c + 1]), T.AO[:, 16 * c:16 * c + 16], "CSO AO%d d2 d3" % d, "CT%d" % d)
+    def cache_write(d):
+        for c in range(12 * d + 11, 12 * d - 1, -1):
+            cp(T.CT[:, NW * d:NW * d + NW].indirect(T.CSO[:, 2 * c:2 * c + 1]), T.AO[:, 16 * c:16 * c + 16],
+               "CSO AO%d d2 d3" % (c // 4), "CT%d" % d, k=-16)
 
-    def decide(s):
+    def triples(s):
         MS, RX, a, b = T["MS%d" % s], T["RX%d" % s], slice(24 * s, 24 * s + 24), slice(24 * s + 24, 24 * s + 48)
-        tt(T.MI[:, 0:12], MS[:, 0:24:2], RX[:, 0:24:2], A.is_ge, "MSa%d RX%d" % (s, s), "MI0")
-        tt(T.MI[:, 12:24], MS[:, 24:48:2], RX[:, 24:48:2], A.is_gt, "MSa%d RX%d" % (s, s), "MI1")
-        tt(T.T3[:], T.OT[:, a], RX[:, 1:48:2], A.subtract, "OT%d RX%d" % (s, s), "T3")
-        tt(T.T1[:], T.MI[:], T.BD[:], A.mult, "MI0 MI1 BD", "T1")
+        tt(T.DO[:], MS[:, 1:3, :], T.OW[:, a], A.subtract, "MB%d_0 MB%d_1 OW%d" % (s, s, s), "DO")
+        tt(T.T3[:], T.OT[:, a], RX[:, 0:3:2, :], A.subtract, "OT%d RXT%d RXB%d" % (s, s, s), "T3")
         tt(T.T4[:], T.MI[:], T.T3[:], A.mult, "MI0 MI1 T3", "T4")
-        ts(T.B16[:], T.T1[:], T.PC[:, 8:9], A.add, "T1 PC8", "B16", s2=1.0 / 64, o1=A.mult)
-        tt(T.OT[:, b], T.T4[:], RX[:, 1:48:2], A.add, "T4 RX%d" % s, "OT%d" % (s + 1))
+        tt(T.OT[:, b], T.T4[:], RX[:, 0:3:2, :], A.add, "T4 RXT%d RXB%d" % (s, s), "OT%d" % (s + 1))
         tt(T.T5[:], T.MI[:], T.DO[:], A.mult, "MI0 MI1 DO", "T5")
         keys(s + 1)
         tt(T.OW[:, b], T.T5[:], T.OW[:, a], A.add, "T5 OW%d" % s, "OW%d" % (s + 1))
-        firsts(T.B16[:], "B16", 4, "b4", T.SD[:], "SD")
         cp(T.OO[:], T.OW[:, b], "OW%d" % (s + 1), "OO0 OO1")
-        ts(T.ND[:], T.SD[:, 15:384:16], 0.0, A.not_equal, "SD", "ND")
-        tt(T.T2[:], T.ND[:], T.T1[:], A.mult, "ND T1", "T2")
-        ts(T.SO[:, 0:48:2], T.T2[:], T.PC[:, 6:7], A.add, "T2 PC6", "SO")
 
-    def write(e):
-        src, nm = ((T.XS, "XS"), (T.E7, "E7"))[e]
-        for i, c in enumerate(list(range(11, -1, -1)) + list(range(23, 11, -1))):
-            cp((T.XB, T.TB)[e][:, 0:EO].indirect(T.SO[:, 2 * c:2 * c + 1]), src[:, 16 * c:16 * c + 16], "SO d0 d1 " + nm,
-               ("TBX", "TBE")[e])
+    turns = [0, 0]
 
-    def usend(s):
-        tt(T["UO%d" % s][:], TX_.indirect(T.OO[:, 0:24]), T.XP[:], A.mult, "TBX OO0 OO1 XP0 XP1", "UO%d" % s)
-        send("UO%d" % s, [(nxt, T["UO%d" % s][:, 0:L], T["U%d" % s][:, L:384], "arU%d" % s, 0, 8),
-                          (prv, T["UO%d" % s][:, L:384], T["U%d" % s][:, 0:L], "arU%d" % s, 8, 16)])
+    def output(s, xs):
+        EG, na, l0 = T["EG%d" % (s & 1)], 2 * len(xs), 64 * xs[0]
+        y = turns[0] & 1
+        turns[0] += 1
+        WS, eg, m0, rows = T["WS%d" % y], names("EG%d_%%d" % (s & 1), xs), l0 // 16, slice(0, 32 * na)
+        ms_ = slice(m0, m0 + 2 * na)
+        w0 = m0 // 2
+        Wp = T.WP[:, w0:w0 + na, :, :]
+        for j4 in range(4):
+            js = range(4 * j4, 4 * j4 + 4)
+            mms([(T.ZP[32 * a:32 * a + 32, 8 * y:8 * y + 8, 2 * j:2 * j + 2], EG[:, 16 * l:16 * l + 32], T.VM[:, :, l:l + 2], True, True)
+                 for j in js for a in range(na) for l in [l0 + 2 * na * j + 2 * a]],
+                "EG%d_%d " % (s & 1, xs[j4 * len(xs) // 4]) + " ".join(names("VM%d_%%d" % d, range(8)) for d in sides(xs)),
+                "z%d_%d" % (y, j4), "b5", 128)
+        act(WS[rows, :], T.ZP[rows, 8 * y:8 * y + 8, :], F.Sigmoid, names("z%d_%%d" % y, range(4)), "WS%d" % y, "b5", scale=0.5, c=256)
+        wn, rn = names("Wp%d", xs), names("R%%s%d", xs)
+        mms([(T.WP[:, w0:w0 + na, h, :], WS[rows, h:256:2], T.IDF[rows, 0:na, h, :], True, True) for h in range(2)],
+            "WS%d IDF" % y, wn, "b4", 256)
+        op("v", lambda q: q.reciprocal(T.RW[:, ms_, 1:16], T.WP[:, w0:w0 + na, :, 1:16]), wn, rn.replace("%s", "W"), "b4",
+           190 + 6 * CYC * 30 * na)
+        tt(Wp, Wp, T.RW[:, ms_, 1:17], A.mult, wn + " RWc " + rn.replace("%s", "W"), wn, "b4", c=32 * na)
+        cp(T.RH[:, ms_, 1:17], Wp, wn, rn.replace("%s", "H"), "b4", either=True, c=32 * na)
+        tt(T.RO[:, ms_, 1:17], Wp, T.RH[:, ms_, 1:17], A.subtract, wn + " " + rn.replace("%s", "H"), rn.replace("%s", "O"), "b4", c=32 * na)
+        k, wide = 16 // na, 32 * na
+        for j in range(0, 16, k):
+            p = turns[1] & 1
+            turns[1] += 1
+            RB, a = T["RB%d" % p], l0 + 2 * na * j
+            mms([(RB[:, wide * i:wide * i + wide], T.SEL[:, 128 * (j + i):128 * (j + i) + 128], T[x][:, ms_, 0:16], x == "RH", x == "RO")
+                 for i in range(k) for x in ("RH", "RO")],
+                "SEL0 SEL1 SEL2 SEL3 RHc ROc " + rn.replace("%s", "H") + " " + rn.replace("%s", "O"), "rb%d" % p, "r%d" % p, wide)
+            scan(T.GS[:, 16 * a:16 * a + 512], RB[:], EG[:, 16 * a:16 * a + 512], A.mult, A.add,
+                 "rb%d EG%d_%d" % (p, s & 1, a // 64), "GS%d" % (a // 32), "r%d" % p, 512)
 
-    def vcopy(s):
-        cp(PS[2][:, 0:384], T["V%d" % s][:], "V%d" % s, "vp", "b2", either=True)
-
-    def sign(s):
-        act(T.SG[:], T["U%d" % s][:], F.Sign, "U%d_0 U%d_1" % (s, s), "SG")
-
-    def ev(s, ks, ds):
-        a, b = ds[0], ds[-1] + 1
-        for k in ks:
-            tt(T.PE[:, 1536 * a + k:1536 * b:16], T["EG%d" % (s & 1)][:, 1536 * a + k:1536 * b:16], PS[2][:, 96 * a:96 * b], A.mult,
-               "vp " + " ".join("EG%d_%d" % (s & 1, x) for x in ds), " ".join("PE%d_%d" % (d, k) for d in ds), "b2",
-               c=20 + 96 * len(ds))
-
-    def pen(ds):
-        return " ".join("PE%d_%d" % (d, k) for d in ds for k in range(16))
-
-    def zsum(js, p):
-        for j in js:
-            for x in range(3):
-                b = 3 * j + x
-                mm(PS[p][:, 128 * x + j:128 * x + 128:16], T.PE[:, 128 * b:128 * b + 128], T.ONE[:, 0:128:16], True, True,
-                   "ONE " + pen([j // 4]), "z%d" % p, "b%d" % p, 256)
-
-    def zturn(p):
-        cp(T.ZS[:], PS[p][:, 0:384], "z%d" % p, "ZS", "b%d" % p, either=True)
-        for x in range(3):
-            mm(PS[p][:, 128 * x:128 * x + 128], T.ZS[:, 128 * x:128 * x + 128], T.IDF[:], True, True, "ZS IDF", "z%d" % p, "b%d" % p, 512)
-
-    def weights(p, y, exp_first=False):
-        bk, z, P = "b%d" % p, "z%d" % p, PS[p][:, 0:384]
-        if exp_first:
-            act(T.QX[:], P, F.Exp, z, "QX", bk, scale=-0.0625)
-            act(P, P, F.Sigmoid, z, z, bk, scale=0.0625, c=1950)
-            ts(T.QX[:], T.QX[:], 1.0, A.add, "QX", "QX", alt=lambda q: q.activation(T.QX[:], T.QX[:], F.Identity, bias=1.0))
-            w, q1, wn = PS[p], T.QX, z
-        else:
-            act(T.QX[:], P, F.Sigmoid, z, "QX", bk, scale=0.0625)
-            act(P, P, F.Exp, z, z, bk, scale=-0.0625, c=1950)
-            act(P, P, F.Identity, z, z, bk, bias=1.0)
-            w, q1, wn = T.QX, PS[p], "QX"
-        cp(T.R[:, 384:408], w[:, 15:384:16], wn, "Rl", bk if exp_first else "")
-        tt(T.R[:, 1:384], w[:, 0:383], q1[:, 1:384], A.mult, z + " QX", "R", bk)
-        op("v", lambda q: q.memset(T.R[:, 0:384:16], 0.0), "", "R", c=84)
-        cp(T["RH%d" % y][:], T.R[:], "R Rl", "RH%d" % y, either=True)
-        tt(T["RO%d" % y][:], T.R[:], T["RH%d" % y][:], A.subtract, "R Rl RH%d" % y, "RO%d" % y)
-
-    def gscan(s, js, y, pz):
-        z, zb = "wl%d" % pz, "b%d" % pz
-        for j in js:
-            for i, x in enumerate(("RH%d" % y, "RO%d" % y)):
-                mm(PS[pz][:, 24 * j:24 * j + 24], T.SEL[:, 128 * j:128 * j + 128], T[x][:, 384:408], i == 0, i == 1, "SEL " + x, z, zb)
-        for j in js:
-            p, x8 = 6 + (j & 1), j % 8
-            for i, x in enumerate(("RH%d" % y, "RO%d" % y)):
-                mm(PS[p][:, 0:384], T.SEL[:, 128 * j:128 * j + 128], T[x][:, 0:384], i == 0, i == 1, "SEL " + x, "rb%d" % p, "b%d" % p, 384)
-            scan(T.GS[:, 384 * x8:384 * x8 + 384], PS[p][:, 0:384], T["EG%d" % (s & 1)][:, 384 * j:384 * j + 384], A.mult, A.add,
-                 "rb%d EG%d_%d" % (p, s & 1, j // 4), "GS%d" % x8, "b%d" % p)
-            if j % 4 == 3:
-                a, o = 24 * (j - 3), 384 * (x8 - 3)
-                tt((PS[pz] if s else T.ACC)[:, a:a + 96], PS[pz][:, a:a + 96], T.GS[:, o + 15:o + 1536:16], A.mult,
-                   z + "".join(" GS%d" % k for k in range(x8 - 3, x8 + 1)), "G%d_%d" % (min(s, 1), j // 4), zb, c=116)
-        if s:
-            a, b = 24 * js[0], 24 * js[-1] + 24
-            acc = " ".join(sorted(set("ACC%d" % (j // 8) for j in js)))
-            tt(T.ACC[:, a:b], PS[pz][:, a:b], T.ACC[:, a:b], A.add, " ".join("G0_%d G1_%d" % (j // 4, j // 4) for j in js[::4]), acc, zb,
-               c=20 + b - a)
-
-    ALL, KS = list(range(16)), list(range(16))
-    for s in range(S):
-        last = s == S - 1
-        step[0] = str(s)
-        H, TL = ALL[:8], ALL[8:]
+    def gather_up(s, xs, na):
+        a, b, w = 64 * xs[0], 64 * xs[-1] + 64, 2 * na
+        flat = T.WL[:, a // 128, a % 128:a % 128 + b - a] if b - a <= 128 else T.WL[:, a // 128:b // 128, :]
+        mms([(T.WL[:, a // 128:(b + 127) // 128, a % 128 + w * j:a % 128 + w * j + w], T.SEL[:, 128 * j:128 * j + 128],
+              T[x][:, a // 16:b // 16, 16], x == "RH", x == "RO") for j in range(16) for x in ("RH", "RO")],
+            "SEL0 SEL1 SEL2 SEL3 " + names("RH%d", xs) + " " + names("RO%d", xs), names("wl%d", xs), "b1", 64)
+        gs = names("wl%d", xs) + " " + names("GS%d", range(a // 32, b // 32))
+        last = T.GS[:, 16 * a + 15:16 * b:16]
         if s == 0:
-            consts(); consts2(); entrants(1); entrants(2)
-        if not last:
-            cache1(); cache2(4); sign(s)
-        for d in (1, 0):
-            step[0] = str(s) + "ht"[d]
-            xgather(s, d); spread(s, d); scores(d); contest(s, d); egather(s, d)
-        step[0] = str(s)
-        if not last:
-            best(s); propose1(s); cache3(); decide(s); cands(s + 1)
-            write(0); usend(s + 1)
-            propose2(s); write(1); vsend(s + 1)
-            vcopy(s); ev(s, KS, (2, 3)); step[0] = str(s) + "h"; ev(s, KS, (0, 1)); step[0] = str(s); zsum(TL + H, 5); zturn(5); weights(5, s & 1)
-            gscan(s, ALL, s & 1, 5)
+            tt(T.ACC[:, a:b], flat, last, A.mult, gs, names("ACC%d", xs), "b1", c=b - a)
         else:
-            vcopy(s)
-            step[0] = "2t"
-            ev(s, KS, (2, 3)); zsum(TL, 4); zturn(4); weights(4, 0, True)
-            step[0] = "2h"
-            ev(s, KS, (0,)); ev(s, KS, (1,)); zsum(H, 5); zturn(5); weights(5, 1)
-            step[0] = "2t"
-            gscan(s, TL, 0, 4)
-            dma("s", T.yt[:], T.ACC[:, L:384], "ACC1", "yt", "out1", 16)
-            step[0] = "2h"
-            gscan(s, H, 1, 5)
-            dma("s", T.yh[:], T.ACC[:, 0:L], "ACC0", "yh", "out0", 16)
+            tt(flat, flat, last, A.mult, gs, names("wl%d", xs), "b1", c=b - a)
+            tt(T.ACC[:, a:b], flat, T.ACC[:, a:b], A.add, names("wl%d", xs) + " " + names("ACC%d", xs), names("ACC%d", xs), "b1", c=b - a)
+
+    for s in range(S):
+        step[0] = str(s)
+        if s < S - 1:
+            cache_targets()
+            for d in (1, 0):
+                step[0] = str(s) + "ht"[d]
+                c = slice(L * d, L * d + L)
+                act(T.SG[:, c], T["U%d" % s][:, c], F.Sign, "U%d_%d" % (s, d), "SG%d" % d, c=L)
+                for x in range(3):
+                    scores(s, 3 * d + x, x)
+                contest(s, range(3 * d, 3 * d + 3))
+                best(s, d)
+                cache_write(d)
+            step[0] = str(s)
+            targets(s, 0); write(0, 0); targets(s, 1); write(0, 1)
+            triples(s); cands(s + 1); usend(s + 1)
+            proposals(s); write(1, 0); write(1, 1); vsend(s + 1)
+            for xs in ((4, 5), (2, 3), (0, 1)):
+                output(s, xs)
+            gather_up(s, range(6), 4)
+            spread("V", s + 1, (0, 1), "spV%d" % (s + 1))
+        else:
+            for xs in LASTUNITS:
+                for i, x in enumerate(xs):
+                    scores(s, x, i)
+                contest(s, xs)
+                output(s, xs)
+                gather_up(s, xs, 2 * len(xs))
+            dma("s", T.yt[:], T.ACC[:, L:384], "ACC3 ACC4 ACC5", "yt", "out1", 16)
+            dma("s", T.yh[:], T.ACC[:, 0:L], "ACC0 ACC1 ACC2", "yh", "out0", 16)
 
     if "order" not in _ORDER:
-        _ORDER["order"] = _order(ops, raised)[0]
+        _ORDER["order"], _ORDER["time"] = _order(ops, raised)
         _ORDER["ops"] = (ops, raised)
     order = _ORDER["order"]
     on = dict(order)

@@ -1,3 +1,5 @@
+import math
+import numpy as np
 from concourse.bass import DstId, RemoteDMATransfer
 from concourse.mybir import AluOpType as A, ActivationFunctionType as F
 
@@ -14,10 +16,10 @@ def _sb(n, d):
 
 SCRATCH = {
     "XB": _sb(EO, bf), "TB": _sb(EO, f32), "CT": _sb(2 * NW, i32), "EN": _sb([3, 384], i32),
-    "ENO": _sb(1152, u16), "ENS": _sb(1152, f16), "LN": _sb(36, i32), "RL": _sb(36, i32), "XR": _sb(64, bf), "ER": _sb(64, bf),
+    "ENO": _sb(1152, u16), "ENS": _sb(1152, f16), "LN": _sb(36, i32), "RL": _sb(68, i32), "XR": _sb(256, bf),
     "XP": _sb(384, bf), "EP": _sb(384, bf), "OW": _sb(72, f32), "OT": _sb(72, f32), "KA": _sb(24, f32), "KB": _sb(24, f32),
     "K1": _sb(24, f32), "K2": _sb(24, i32), "K3": _sb(24, i32), "KO": _sb(24, u16),
-    "K16": _sb(24, f16), "PO": _sb(12, u16), "OO": _sb(24, u16), "CO": _sb(384, u16), "DF": _sb(384, f32),
+    "K16": _sb(24, f16), "PO": _sb(24, u16), "OO": _sb(24, u16), "CO": _sb(384, u16), "DF": _sb(384, f32),
     "XG": _sb(12288, bf), "UM": _sb([8, 384], bf), "VM": _sb([8, 384], f32),
     "EG0": _sb(6144, f32), "EG1": _sb(6144, f32), "GS": _sb(6144, f32),
     "SCP": _sb(768, f32), "SK": _sb(768, f32), "LB": _sb(384, bf), "LT": _sb([24, 16], bf), "KI": _sb(12, i32),
@@ -26,14 +28,14 @@ SCRATCH = {
     "MI": _sb(24, f32), "LM": _sb(12, f32), "CP": _sb(12, f32), "BD": _sb(24, f32), "BM": _sb(24, f32), "DO": _sb(24, f32),
     "T1": _sb(24, f32), "T2": _sb(24, f32), "T3": _sb(24, f32), "T4": _sb(24, f32), "T5": _sb(24, f32), "B16": _sb(24, f16),
     "SD": _sb(384, f32), "SE": _sb(384, f32), "ND": _sb(24, f32), "SO": _sb(48, u16), "NE": _sb(24, f32), "C1": _sb(24, f32),
-    "C2": _sb(24, f32), "CSO": _sb(48, u16), "WS0": _sb(256, f32), "WS1": _sb(256, f32),
+    "C2": _sb(24, f32), "CSO": _sb(48, u16), "WS0": _sb([8, 32], f32), "WS1": _sb([8, 32], f32),
     "RW": _sb([24, 17], f32), "RH": _sb([24, 17], bf), "RO": _sb([24, 17], f16), "ACC": _sb(384, f32),
     "PI": _sb(8, i32), "PJ": _sb(8, i32), "PC": _sb(16, f32), "IC": _sb(160, f32), "IG": _sb(128, f32), "PRI": _sb(384, bf),
     "VI": _sb(32, f32), "IT": _sb(32, bf), "W": _sb(160, bf), "PW0": _sb(160, bf), "PW1": _sb(160, bf),
     "IDF": _sb([4, 2, 16], f32), "IDD": _sb(64, f32), "ONE": _sb(128, f32), "RM": _sb(384, f32), "DM": _sb(384, f32),
     "ONES": _sb(512, bf), "SEL": _sb(2048, bf), "DD": _sb(2048, bf),
     "S0": ("psum", [128, 512], f32), "WL": ("psum", [128, 4, 128], f32), "KP": ("psum", [128, 512], f32),
-    "B3": ("psum", [128, 16, 2, 16], f32), "WP": ("psum", [128, 16, 2, 16], f32), "ZP": ("psum", [128, 16, 32], f32),
+    "B3": ("psum", [128, 16, 2, 16], f32), "WP": ("psum", [128, 16, 2, 16], f32), "ZP": ("psum", [128, 64, 8], f32),
     "RB0": ("psum", [128, 512], f32), "RB1": ("psum", [128, 512], f32),
 }
 for _s in range(S):
@@ -51,8 +53,13 @@ SEMAPHORES = ["cg", "cv", "ca", "cp", "sent", "ldL", "ldR", "ldX", "ldC0", "ldC1
 CNT = {"g": "cg", "v": "cv", "a": "ca", "p": "cp"}
 CYC, PEC, HOP, GAT, SCA = 0.85, 0.43, 140, 1.56, 3.8
 LATE = {"ldL": 2200, "ldN1": 2800, "ldN0": 4500, "ldX": 3600, "ldR": 2500, "ldC1": 4600, "ldC0": 5200, "ldTE": 6500}
-TUNE = {"bias": 2000, "patience": 1.0, "turns": 3, "shy": 600}
+TUNE = {"bias": 6000, "patience": 1.0, "turns": 12000, "heat": 200, "seed": 1}
 LASTUNITS = [(4, 5), (2, 3), (0, 1)]
+HINTS = [{}, {}, {}]
+RECIP = set()
+ONV = set()
+WIDE = {(s, x) for s in range(S) for x in (0, 2, 4)}
+E16 = math.exp(16.0)
 _ORDER = {}
 QS = "vagsp"
 
@@ -128,36 +135,73 @@ def _order(ops, raised):
             if not left[k]:
                 for e2 in ops[k][5]:
                     ready[e2][k] = at[k]
-    best = (max(free.values()), out)
+    rng = np.random.RandomState(TUNE["seed"])
 
-    def pack(seq, before, on, choose):
-        busy, end, res = {e: [] for e in QS}, [0.0] * n, {}
-        for i in seq:
-            t0, pick = max([end[j] + lag for j, lag in before[i]] or [0.0]), None
-            for e in (sorted(ops[i][5]) if choose else [on[i]]):
-                c, t, k, b = ops[i][5][e], t0, len(busy[e]), busy[e]
-                while k and b[k - 1][1] > t0:
-                    k -= 1
-                while k < len(b) and b[k][0] < t + c:
-                    t = max(t, b[k][1])
-                    k += 1
-                late = t + c + (TUNE["shy"] if e == "v" else 0)
-                if pick is None or late < pick[0]:
-                    pick = (late, t, c, e, k)
-            late, t, c, e, k = pick
-            busy[e].insert(k, (t, t + c))
-            end[i], res[i] = t + c, (t, e)
-        return end, res
+    def pack(key, on):
+        st, en, beg, end = {e: [] for e in QS}, {e: [] for e in QS}, [0.0] * n, [0.0] * n
+        for i in sorted(range(n), key=lambda i: key[i]):
+            t = 0.0
+            for j, lag in pre[i]:
+                if end[j] + lag > t:
+                    t = end[j] + lag
+            c, a, b = ops[i][5][on[i]], st[on[i]], en[on[i]]
+            k = m = len(a)
+            while k and b[k - 1] > t:
+                k -= 1
+            while k < m and a[k] < t + c:
+                t = max(t, b[k])
+                k += 1
+            a.insert(k, t)
+            b.insert(k, t + c)
+            beg[i], end[i] = t, t + c
+        return beg, end
 
-    on = dict(out)
-    end = [begin[i] + ops[i][5][on[i]] for i in range(n)]
+    def binding(beg, end, on):
+        before, last, pairs = {}, {}, []
+        for i in sorted(range(n), key=lambda i: beg[i]):
+            before[i], last[on[i]] = last.get(on[i]), i
+        i = max(range(n), key=lambda i: end[i])
+        while i is not None:
+            p, nx = before[i], None
+            for j, lag in pre[i]:
+                if abs(end[j] + lag - beg[i]) < 1:
+                    nx = j
+            if p is not None and abs(end[p] - beg[i]) < 1 and (nx is None or rng.rand() < 0.5):
+                pairs.append((i, p))
+                nx = p
+            i = nx
+        return pairs
+
+    on = [e for i, e in sorted(out)]
+    beg, end = pack(begin, on)
+    now, best, pairs = max(end) + 0.03 * sum(beg) / n, (max(end), beg, on), binding(beg, end, on)
     for turn in range(TUNE["turns"]):
-        end, res = pack(sorted(range(n), key=lambda i: (-end[i], -i)), post, on, False)
-        end, res = pack(sorted(range(n), key=lambda i: (prio[i] < 5e8, -end[i], i)), pre, on, True)
-        on = {i: res[i][1] for i in res}
-        if max(end) < best[0]:
-            best = (max(end), [(i, on[i]) for i in sorted(range(n), key=lambda i: (res[i][0], i))])
-    return best[1], best[0]
+        key, on2, u = list(beg), on, rng.rand()
+        i, p = pairs[rng.randint(len(pairs))]
+        both = [x for x in (i, p) if len(ops[x][5]) > 1]
+        if u < 0.3 and both:
+            x, on2 = both[rng.randint(len(both))], list(on)
+            on2[x] = "a" if on[x] == "v" else "v"
+        elif u < 0.65:
+            key[p] = beg[i] + (1, 300, 1000, 3000, 8000)[rng.randint(5)]
+        else:
+            key[i] = beg[p] - (1, 300, 1000, 3000)[rng.randint(4)]
+            for a in range(i, -1, -1):
+                for j, lag in post[a]:
+                    if key[j] <= key[a]:
+                        key[a] = key[j] - 0.01
+        for a in range(n):
+            for j, lag in pre[a]:
+                if key[j] >= key[a]:
+                    key[a] = key[j] + 0.01
+        beg2, end2 = pack(key, on2)
+        cost = max(end2) + 0.03 * sum(beg2) / n
+        if cost <= now + TUNE["heat"] * (1 - turn / TUNE["turns"]) * rng.rand():
+            now, beg, end, on = cost, beg2, end2, on2
+            pairs = binding(beg, end, on)
+            if max(end) < best[0]:
+                best = (max(end), beg, on)
+    return [(i, best[2][i]) for i in sorted(range(n), key=lambda i: (best[1][i], i))], best[0]
 
 
 def rank_program(g, core, T, topo):
@@ -167,7 +211,7 @@ def rank_program(g, core, T, topo):
     n = len(T.cores)
     nxt, prv = T.cores[(rank + 1) % n], T.cores[(rank - 1) % n]
     Q = {"g": g, "v": g.vector, "a": g.scalar, "p": g.tensor, "s": g.sync}
-    ops, wr, rd, bank, sent, raised, step = [], {}, {}, {}, [0], {}, ["s"]
+    ops, wr, rd, bank, sent, raised, step, hint = [], {}, {}, {}, [0], {}, ["s"], {}
 
     def op(e, f, r, w, b, c, dma=None, alt=None):
         i = len(ops)
@@ -190,6 +234,7 @@ def rank_program(g, core, T, topo):
         if e == "p":
             soft.update(d for d in deps if d[0] == "e" and ops[d[1]][0] == "p")
             deps -= soft
+        soft.update(wr[x] for x in hint.pop(w, "").split() if wr[x] not in deps)
         for x in r.split():
             rd.setdefault(x, []).append(me)
         for x in w.split():
@@ -224,8 +269,8 @@ def rank_program(g, core, T, topo):
     def tt(out, a, b, o, r, w, bk="", c=0, k=0):
         op("v", lambda q: q.tensor_tensor(out, a, b, o), r, w, bk, vns(c, k))
 
-    def ts(out, a, s1, o0, r, w, bk="", s2=None, o1=None, c=0, k=0, alt=None):
-        alt = alt and (alt, ans(c, k))
+    def ts(out, a, s1, o0, r, w, bk="", s2=None, o1=None, c=0, k=0, alt=None, ca=0):
+        alt = alt and (alt, ans(ca or c, k))
         if o1 is None:
             op("v", lambda q: q.tensor_scalar(out, a, s1, None, o0), r, w, bk, vns(c, k), alt=alt)
         else:
@@ -254,7 +299,7 @@ def rank_program(g, core, T, topo):
         op("g", f, r, w, "", 150 + 2 * CYC * c)
 
     TX_, TE_ = T.XB[:, 0:M], T.TB[:, 0:M]
-    for x, sem, val in (("RL", "arL", 16), ("XP1", "arP", 8), ("EP1", "arP", 8), ("U0_0", "arU0h", 16), ("U0_1", "arU0t", 8)):
+    for x, sem, val in (("RL", "arL", 16), ("U0_0", "arU0h", 16), ("U0_1", "arU0t", 16)):
         wr[x] = ("s", sem, val)
     for s in range(S):
         wr["V%d" % s] = ("s", "arV%d" % s, 16)
@@ -267,8 +312,8 @@ def rank_program(g, core, T, topo):
     dma("s", T.LN[:, 0:12], T.tl[:], "", "LN", "ldL", 48)
     dma("s", T.LN[:, 12:24], T.hl[:], "", "LN", "ldL", 48)
     dma("s", T.LN[:, 24:36], T.rl[:], "", "LN", "ldL", 48)
-    dma("a", T.XR[:], T.xr[:], "", "XR", "ldR", 32)
-    dma("a", T.ER[:], T.er[:], "", "XR", "ldR", 32)
+    dma("a", T.XR[:, 0:64], T.xr[:], "", "XR", "ldR", 32)
+    dma("a", T.XR[:, 64:128], T.er[:], "", "XR", "ldR", 32)
     dma("a", T.EN[:, :, 192:384], T.nt[:], "", "EN1", "ldN1", 16)
     dma("s", TX_, T.xe[:], "", "TBX", "ldX", 16)
     dma("s", T.CT[:, NW:NW + NC], T.tc[:], "", "CT1", "ldC1", 16)
@@ -279,22 +324,26 @@ def rank_program(g, core, T, topo):
     pool(lambda q: q.iota(T.IG[:], [[16, 8], [0, 16]], 0, 0, allow_small_or_imprecise_dtypes=True), "", "IG", 128)
     pool(lambda q: q.iota(T.VI[:], [[-1, 16], [0, 2]], 15, 0, allow_small_or_imprecise_dtypes=True), "", "VI", 32)
     pool(lambda q: q.iota(T.PRI[:], [[0, 24], [-1, 16]], 15, 0, allow_small_or_imprecise_dtypes=True), "", "PRI", 384)
-    send("LN", [(nxt, T.LN[:], T.RL[:], "arL", 0, 16)])
+    send("LN XR", [(nxt, T.LN[:, 0:32], T.RL[:, 0:32], "arL", 0, 4), (nxt, T.LN[:, 4:36], T.RL[:, 36:68], "arL", 4, 8),
+                   (nxt, T.XR[:, 0:64], T.XR[:, 128:192], "arL", 8, 12), (nxt, T.XR[:, 64:128], T.XR[:, 192:256], "arL", 12, 16)])
 
     ms(T.UM[:], 0.0, "UMz", 1536)
     act(T.VM[:], T.UM[:], F.Copy, "UMz", "VMz", c=3072)
     ms(T.KA[:, 0:12], 1.0, "KA0"); ms(T.KA[:, 12:24], 37.0, "KA1")
     ms(T.TB[:, M:EO], 0.0, "d0"); ms(T.XB[:, M:EO], 0.0, "d1"); ms(T.CT[:, NC:NW], 0, "d2"); ms(T.CT[:, NW + NC:2 * NW], 0, "d3")
-    ms(T.ONES[:], 1.0, "ONES", 256)
+    ms(T.ONES[:], 1.0, "ONES", 256); ms(T.PC[:, 7:8], -16.0, "PC7")
     ms(T.RM[:], 0.0, "RM", 384); ms(T.RM[:, 0:384:32], -1.0e9, "RM")
     ms(T.RW[:, :, 16], 1.0, "RWc"); ms(T.RH[:, :, 0], 0.0, "RHc"); ms(T.RO[:, :, 0], 0.0, "ROc")
-    cp(T.PO[:], T.LN[:, 24:36], "LN", "PO")
+    cp(T.PO[:, 0:12], T.LN[:, 24:36], "LN", "PO0")
+    cp(T.PO[:, 12:24], T.RL[:, 56:68], "RL", "PO1")
     cp(T.OO[:, 0:12], T.LN[:, 12:24], "LN", "OO0")
-    cp(T.XP[:, 0:L], T.XR[:, 0:64].indirect(T.PO[:, 0:12]), "XR PO", "XP0", k=L)
-    ts(T.EP[:, 0:L], T.ER[:, 0:64].indirect(T.PO[:, 0:12]), 0.125, A.mult, "XR PO", "EP0", k=L)
+    for d in range(2):
+        c, at, r = slice(L * d, L * d + L), T.PO[:, 12 * d:12 * d + 12], ("XR", "RL")[d] + " PO%d" % d
+        x, e = T.XR[:, 128 * d:128 * d + 64].indirect(at), T.XR[:, 128 * d + 64:128 * d + 128].indirect(at)
+        cp(T.XP[:, c], x, r, "XP%d" % d, either=True, k=L)
+        ts(T.EP[:, c], e, 0.125, A.mult, r, "EP%d" % d, k=L, alt=lambda q, c=c, e=e: q.activation(T.EP[:, c], e, F.Copy, scale=0.125))
     tt(T.UO0[:, 0:L], TX_.indirect(T.OO[:, 0:12]), T.XP[:, 0:L], A.mult, "TBX OO0 XP0", "UO0_0", k=L)
-    send("XP0 EP0 UO0_0", [(nxt, T.XP[:, 0:L], T.XP[:, L:384], "arP", 0, 4), (nxt, T.EP[:, 0:L], T.EP[:, L:384], "arP", 4, 8),
-                           (nxt, T.UO0[:, 0:L], T.U0[:, L:384], "arU0t", 8, 16)])
+    send("UO0_0", [(nxt, T.UO0[:, 0:L], T.U0[:, L:384], "arU0t", 0, 16)])
     ts(T.PJ[:, 0:1], T.PI[:, 0:1], 15, A.bitwise_and, "PI", "PJ0")
     ts(T.PJ[:, 1:2], T.PI[:, 0:1], 4, A.arith_shift_right, "PI", "PJ1", s2=1, o1=A.bitwise_and)
     ts(T.PJ[:, 2:3], T.PI[:, 0:1], 1, A.arith_shift_right, "PI", "PJ2")
@@ -316,7 +365,7 @@ def rank_program(g, core, T, topo):
     ts(T.KB[:, 0:12], T.LN[:, 24:36], 37.0, A.mult, "LN", "KB0")
     cp(T.OO[:, 12:24], T.RL[:, 0:12], "RL", "OO1")
     cp(T.OT[:, 12:24], T.RL[:, 12:24], "RL OT0a", "OT0")
-    cp(T.KB[:, 12:24], T.RL[:, 24:36], "RL", "KB1")
+    cp(T.KB[:, 12:24], T.RL[:, 56:68], "RL", "KB1")
     cp(T.OW[:, 12:24], T.RL[:, 0:12], "RL OW0a", "OW0")
     ts(T.IDF[:], T.IC[:, 16:144], T.PC[:, 3:4], A.is_equal, "IC PC3", "IDF", c=128)
     ts(T.IDD[:], T.IC[:, 0:64], T.PC[:, 10:11], A.is_equal, "IC PC10 PC11", "IDD", s2=T.PC[:, 11:12], o1=A.mult)
@@ -337,9 +386,9 @@ def rank_program(g, core, T, topo):
     DDN = " ".join("DDz%d" % x for x in range(8))
 
     def keys(s):
-        tt(T.K1[:], T.OT[:, 24 * s:24 * s + 24], T.KA[:], A.mult, "OT%d KA0 KA1" % s, "K1")
-        tt(T.K2[:], T.K1[:], T.KB[:], A.add, "K1 KB0 KB1", "K2")
-        ts(T.K3[:], T.K2[:], NC - 1, A.bitwise_and, "K2", "K3")
+        tt(T.K1[:], T.OT[:, 24 * s:24 * s + 24], T.KA[:], A.mult, "OT%d KA0 KA1" % s, "Ka")
+        tt(T.K2[:], T.K1[:], T.KB[:], A.add, "Ka KB0 KB1", "Kb")
+        ts(T.K3[:], T.K2[:], NC - 1, A.bitwise_and, "Kb", "K3")
         cp(T.KO[:], T.K3[:], "K3", "KO")
 
     def cands(s):
@@ -360,8 +409,14 @@ def rank_program(g, core, T, topo):
         for x in range(8):
             p = slice(16 * x, 16 * x + 16)
             dma("s", T[name + "M"][p, x, a:b], T["%s%d" % (name, s)][p, a:b],
-                name + "Mz " + (" ".join("U%d_%d" % (s, d) for d in ds) if name == "U" else "V%d" % s),
+                "VMz " + (" ".join("U%d_%d" % (s, d) for d in ds) if name == "U" else "V%d" % s),
                 " ".join("%sM%d_%d" % (name, d, x) for d in ds), sem, 128)
+
+    def spread_now(s, d):
+        for x in range(8):
+            o, src, m = T.UM[:, x, L * d:L * d + L], T["U%d" % s][:, L * d:L * d + L], T.ONE[:, 16 * x:16 * x + 1]
+            ts(o, src, m, A.mult, "VMz ONE U%d_%d" % (s, d), "UM%d_%d" % (d, x), c=96,
+               alt=lambda q, o=o, src=src, m=m: q.activation(o, src, F.Copy, scale=m), ca=L)
 
     def vsend(s):
         tt(T["VO%d" % s][:], TE_.indirect(T.OO[:, 0:24]), T.EP[:], A.mult, "TBE OO0 OO1 EP0 EP1", "VO%d" % s, k=384)
@@ -372,12 +427,13 @@ def rank_program(g, core, T, topo):
         tt(T["UO%d" % s][:], TX_.indirect(T.OO[:, 0:24]), T.XP[:], A.mult, "TBX OO0 OO1 XP0 XP1", "UO%d" % s, k=384)
         send("UO%d" % s, [(nxt, T["UO%d" % s][:, 0:L], T["U%d" % s][:, L:384], "arU%d" % s, 0, 8),
                           (prv, T["UO%d" % s][:, L:384], T["U%d" % s][:, 0:L], "arU%d" % s, 8, 16)])
-        spread("U", s, (0, 1), "spU%d" % s)
+        spread_now(s, 1)
+        spread("U", s, (0,), "spU%d" % s)
 
     keys(0)
     entrants(0)
     cands(0)
-    spread("U", 0, (1,), "spU0t")
+    spread_now(0, 1)
     tt(T.UO0[:, L:384], TX_.indirect(T.OO[:, 12:24]), T.XP[:, L:384], A.mult, "TBX OO1 XP1", "UO0_1", k=L)
     send("UO0_1", [(prv, T.UO0[:, L:384], T.U0[:, 0:L], "arU0h", 0, 16)])
     spread("U", 0, (0,), "spU0h")
@@ -392,11 +448,14 @@ def rank_program(g, core, T, topo):
     def sides(xs):
         return sorted(set(x // 3 for x in xs))
 
+    def gather(out, src, r, w, which):
+        cp(out, src, r, w, k=1024, either=True)
+
     def scores(s, x, slot):
         a, d = 64 * x, x // 3
-        cp(T.XG[:, 32 * a:32 * a + 2048:2], TX_.indirect(T.ENO[:, 384 * s + a:384 * s + a + 64]), "TBX ENO%d_%d" % (s, d),
-           "XG%d_0" % x, either=True, k=1024)
-        cp(T.XG[:, 32 * a + 1:32 * a + 2048:2], TX_.indirect(T.CO[:, a:a + 64]), "TBX CO%d" % d, "XG%d_1" % x, either=True, k=1024)
+        gather(T.XG[:, 32 * a:32 * a + 2048:2], TX_.indirect(T.ENO[:, 384 * s + a:384 * s + a + 64]), "TBX ENO%d_%d" % (s, d),
+               "XG%d_0" % x, (s, x, 0))
+        gather(T.XG[:, 32 * a + 1:32 * a + 2048:2], TX_.indirect(T.CO[:, a:a + 64]), "TBX CO%d" % d, "XG%d_1" % x, (s, x, 1))
         P, bk = T.S0, "b0"
         for q4 in range(4):
             mms([(P[32 * q4:32 * q4 + 32, j:128:16], T.XG[:, 32 * l:32 * l + 32], T.UM[:, :, l], True, True)
@@ -412,7 +471,8 @@ def rank_program(g, core, T, topo):
     def contest(s, xs):
         m, a = len(xs), 64 * xs[0]
         c, c4 = slice(a, a + 64 * m), a // 16
-        ts(T.LB[:, c], T.B3[:, 0:2 * m, :, :], 0.0, A.is_gt, names("D%d", range(m)), names("LB%d", xs), "b3", c=64 * m)
+        ts(T.LB[:, c], T.B3[:, 0:2 * m, :, :], 0.0, A.is_gt, names("D%d", range(m)), names("LB%d", xs), "b3", c=64 * m,
+           alt=lambda q: q.activation(T.LB[:, c], T.B3[:, 0:2 * m, :, :], F.Sigmoid, scale=128.0))
         op("v", lambda q: q.transpose(T.LT[:, c4:c4 + 4 * m, :], T.LB[:, c]), names("LB%d", xs), names("LT%d", xs), "", vns(32 * m, 0))
         lo = T.B3[:, 6:6 + 2 * m, :, :]
         mms([(T.B3[:, 6:6 + 2 * m, h, :], T["PW%d" % h][:, o:o + 128], T.LT[:, c4 + g2:c4 + 4 * m:2, :], g2 == 0, g2 == 1)
@@ -422,8 +482,8 @@ def rank_program(g, core, T, topo):
            names("AL%d", xs), "b3", c=64 * m)
         ts(T.AO[:, c], T.AL[:, c], 1536.0, A.add, names("AL%d", xs), names("AO%d", xs), c=32 * m)
         for x in xs:
-            cp(T["EG%d" % (s & 1)][:, 1024 * x:1024 * x + 1024], TE_.indirect(T.AO[:, 64 * x:64 * x + 64]), "TBE AO%d" % x,
-               "EG%d_%d" % (s & 1, x), either=True, k=1024)
+            gather(T["EG%d" % (s & 1)][:, 1024 * x:1024 * x + 1024], TE_.indirect(T.AO[:, 64 * x:64 * x + 64]), "TBE AO%d" % x,
+                   "EG%d_%d" % (s & 1, x), (s, x, 2))
 
     def best(s, d):
         MS, RX, c, h = T["MS%d" % s], T["RX%d" % s], slice(L * d, L * d + L), slice(12 * d, 12 * d + 12)
@@ -493,7 +553,7 @@ def rank_program(g, core, T, topo):
     def cache_targets():
         ts(T.K16[:], T.K3[:], 1.0 / 64, A.mult, "K3", "K16")
         ts(T.C1[:], T.K3[:], T.PC[:, 9:10], A.subtract, "K3 PC9", "C1")
-        firsts(T.K16[:], "K16", lambda i: T.KP[:, i:384:16], T.KP[:, 0:384], "b2", T.SE[:], ("SE", "K0 K1 K2"), 384)
+        firsts(T.K16[:], "K16", lambda i: T.S0[:, 128 + i:512:16], T.S0[:, 128:512], "b0", T.SE[:], ("SE", "dd"), 384)
         ts(T.NE[:], T.SE[:, 15:384:16], 0.0, A.not_equal, "SE", "NE")
         tt(T.C2[:], T.NE[:], T.C1[:], A.mult, "NE C1", "C2")
         ts(T.CSO[:, 0:48:2], T.C2[:], T.PC[:, 9:10], A.add, "C2 PC9", "CSO")
@@ -524,18 +584,42 @@ def rank_program(g, core, T, topo):
         ms_ = slice(m0, m0 + 2 * na)
         w0 = m0 // 2
         Wp = T.WP[:, w0:w0 + na, :, :]
-        for j4 in range(4):
-            js = range(4 * j4, 4 * j4 + 4)
-            mms([(T.ZP[32 * a:32 * a + 32, 8 * y:8 * y + 8, 2 * j:2 * j + 2], EG[:, 16 * l:16 * l + 32], T.VM[:, :, l:l + 2], True, True)
-                 for j in js for a in range(na) for l in [l0 + 2 * na * j + 2 * a]],
-                "EG%d_%d " % (s & 1, xs[j4 * len(xs) // 4]) + " ".join(names("VM%d_%%d" % d, range(8)) for d in sides(xs)),
-                "z%d_%d" % (y, j4), "b5", 128)
-        act(WS[rows, :], T.ZP[rows, 8 * y:8 * y + 8, :], F.Sigmoid, names("z%d_%%d" % y, range(4)), "WS%d" % y, "b5", scale=0.5, c=256)
+        twice = (s, xs[0]) not in RECIP
+        vm = " ".join(names("VM%d_%%d" % d, range(8)) for d in sides(xs))
+
+        def fetch(o, src, r, w, bk, c):
+            if twice:
+                cp(o, src, r, w, bk, either=True, c=c)
+            else:
+                act(o, src, F.Sigmoid, r, w, bk, scale=0.5, c=c)
+
+        if (s, xs[0]) in WIDE:
+            for b in range(2):
+                Z, bk = T.ZP, "b5"
+                for j2 in range(2):
+                    mms([(Z[:, j % 8:64:8, :], EG[:, 16 * l:16 * l + 128], T.VM[:, :, l:l + 8], True, True)
+                         for j in range(8 * b + 4 * j2, 8 * b + 4 * j2 + 4) for l in [l0 + 8 * j]],
+                        "EG%d_%d " % (s & 1, xs[b]) + vm, "z%s_%d" % (bk, j2), bk, 256)
+                for a in range(4):
+                    p = slice(32 * a, 32 * a + 32)
+                    fetch(WS[p, :, 16 * b:16 * b + 16], Z[p, :, 2 * a:2 * a + 2], "z%s_0 z%s_1" % (bk, bk), "WS%d_%d" % (y, 4 * b + a), bk, 128)
+        else:
+            for j4 in range(4):
+                mms([(T.ZP[32 * a:32 * a + 32, 32 * y + j // 4:32 * y + 32:4, 2 * (j % 4):2 * (j % 4) + 2], EG[:, 16 * l:16 * l + 32],
+                      T.VM[:, :, l:l + 2], True, True) for j in range(4 * j4, 4 * j4 + 4) for a in range(na)
+                     for l in [l0 + 2 * na * j + 2 * a]], "EG%d_%d " % (s & 1, xs[j4 * len(xs) // 4]) + vm, "zb5_%d" % j4, "b5", 128)
+            fetch(WS[rows, :, :], T.ZP[rows, 32 * y:32 * y + 32, :], names("zb5_%d", range(4)), names("WS%d_%%d" % y, range(8)), "b5", 256)
         wn, rn = names("Wp%d", xs), names("R%%s%d", xs)
-        mms([(T.WP[:, w0:w0 + na, h, :], WS[rows, h:256:2], T.IDF[rows, 0:na, h, :], True, True) for h in range(2)],
-            "WS%d IDF" % y, wn, "b4", 256)
-        op("v", lambda q: q.reciprocal(T.RW[:, ms_, 1:16], T.WP[:, w0:w0 + na, :, 1:16]), wn, rn.replace("%s", "W"), "b4",
-           190 + 6 * CYC * 30 * na)
+        mms([(T.WP[:, w0:w0 + na, h, :], WS[rows, :, h:32:2], T.IDF[rows, 0:na, h, :], True, True) for h in range(2)],
+            "IDF " + names("WS%d_%%d" % y, range(8)), wn, "b4", 256)
+        q1 = T.RW[:, ms_, 1:16]
+        if twice:
+            act(q1, T.WP[:, w0:w0 + na, :, 1:16], F.Sigmoid, wn + " PC7", rn.replace("%s", "W"), "b4", bias=T.PC[:, 7:8], scale=-0.5, c=30 * na)
+            act(Wp, Wp, F.Sigmoid, wn, wn, "b4", scale=0.5, c=32 * na)
+            ts(q1, q1, E16, A.mult, rn.replace("%s", "W"), rn.replace("%s", "W"), s2=1.0, o1=A.add, c=30 * na,
+               alt=lambda q: q.activation(q1, q1, F.Identity, bias=1.0, scale=E16))
+        else:
+            op("v", lambda q: q.reciprocal(q1, T.WP[:, w0:w0 + na, :, 1:16]), wn, rn.replace("%s", "W"), "b4", 190 + 6 * CYC * 30 * na)
         tt(Wp, Wp, T.RW[:, ms_, 1:17], A.mult, wn + " RWc " + rn.replace("%s", "W"), wn, "b4", c=32 * na)
         cp(T.RH[:, ms_, 1:17], Wp, wn, rn.replace("%s", "H"), "b4", either=True, c=32 * na)
         tt(T.RO[:, ms_, 1:17], Wp, T.RH[:, ms_, 1:17], A.subtract, wn + " " + rn.replace("%s", "H"), rn.replace("%s", "O"), "b4", c=32 * na)
@@ -566,8 +650,10 @@ def rank_program(g, core, T, topo):
 
     for s in range(S):
         step[0] = str(s)
+        hint.update(HINTS[s])
         if s < S - 1:
-            cache_targets()
+            if s:
+                cache_targets()
             for d in (1, 0):
                 step[0] = str(s) + "ht"[d]
                 c = slice(L * d, L * d + L)
@@ -576,8 +662,10 @@ def rank_program(g, core, T, topo):
                     scores(s, 3 * d + x, x)
                 contest(s, range(3 * d, 3 * d + 3))
                 best(s, d)
-                cache_write(d)
             step[0] = str(s)
+            if s == 0:
+                cache_targets()
+            cache_write(1); cache_write(0)
             targets(s, 0); write(0, 0); targets(s, 1); write(0, 1)
             triples(s); cands(s + 1); usend(s + 1)
             proposals(s); write(1, 0); write(1, 1); vsend(s + 1)

@@ -6,7 +6,7 @@ from concourse.mybir import AluOpType as A, ActivationFunctionType as F
 M, L, S, NC = 3072, 192, 3, 1024
 EO = M + 32
 NW = NC + 16
-KEY0 = 1 << 18
+KEY0 = 1 << 19
 f32, bf, i32, u16, f16 = "float32", "bfloat16", "int32", "uint16", "float16"
 
 
@@ -25,14 +25,16 @@ SCRATCH = {
     "SCP": _sb(768, f32), "SK": _sb(768, f32), "LB": _sb(384, bf), "LT": _sb([24, 16], bf), "KI": _sb(12, i32),
     "KL": _sb(24, i32), "KS": _sb(24, u16), "AL": _sb(384, f16), "AO": _sb(384, u16), "YB": _sb(384, f16),
     "BO": _sb(24, u16), "SG": _sb(384, bf), "XS": _sb(384, bf), "EV": _sb(384, f32), "E7": _sb(384, f32), "WV": _sb(384, f32),
-    "MI": _sb(24, f32), "LM": _sb(12, f32), "CP": _sb(12, f32), "BD": _sb(24, f32), "BM": _sb(24, f32), "DO": _sb(24, f32),
-    "T1": _sb(24, f32), "T2": _sb(24, f32), "T3": _sb(24, f32), "T4": _sb(24, f32), "T5": _sb(24, f32), "B16": _sb(24, f16),
-    "SD": _sb(384, f32), "SE": _sb(384, f32), "ND": _sb(24, f32), "SO": _sb(48, u16), "NE": _sb(24, f32), "C1": _sb(24, f32),
+    "MI": _sb(24, f32), "LM": _sb(12, f16), "DO": _sb(24, f32),
+    "T1": _sb(32, f32), "T2": _sb(24, f32), "T3": _sb(24, f32), "T4": _sb(24, f32), "T5": _sb(24, f32), "B16": _sb(24, f16),
+    "SD": _sb(384, f32), "SE": _sb(384, f32), "ND": _sb(48, f32), "SO": _sb(24, u16), "NE": _sb(24, f32),
     "C2": _sb(24, f32), "CSO": _sb(48, u16), "WS0": _sb([8, 32], f32), "WS1": _sb([8, 32], f32),
     "RW": _sb([24, 17], f32), "RH": _sb([24, 17], bf), "RO": _sb([24, 17], f16), "ACC": _sb(384, f32),
     "PI": _sb(8, i32), "PJ": _sb(8, i32), "PC": _sb(16, f32), "IC": _sb(160, f32), "IG": _sb(128, f32), "PRI": _sb(384, bf),
-    "VI": _sb(32, f32), "IT": _sb(32, bf), "W": _sb(160, bf), "PW0": _sb(160, bf), "PW1": _sb(160, bf),
-    "IDF": _sb([4, 2, 16], f32), "IDD": _sb(64, f32), "ONE": _sb(128, f32), "RM": _sb(384, f32), "DM": _sb(384, f32),
+    "VI": _sb(64, f32), "IT": _sb(64, bf), "W": _sb(160, bf), "PW0": _sb(160, bf), "PW1": _sb(160, bf),
+    "IDF": _sb([4, 2, 16], f32), "IDD": _sb(64, f32), "ONE": _sb(128, f32), "RM": _sb(384, f32), "DM": _sb(384, bf),
+    "DN": _sb(384, bf), "NI": _sb(128, bf), "BL": _sb(12, u16), "BR": _sb(192, f16),
+    "P80": _sb(160, bf), "P81": _sb(160, bf), "SE2": _sb(1024, bf), "TS0": _sb(256, f16), "TS1": _sb(256, f16), "TW": _sb(48, f16),
     "ONES": _sb(512, bf), "SEL": _sb(2048, bf), "DD": _sb(2048, bf),
     "S0": ("psum", [128, 512], f32), "WL": ("psum", [128, 4, 128], f32), "KP": ("psum", [128, 512], f32),
     "B3": ("psum", [128, 16, 2, 16], f32), "WP": ("psum", [128, 16, 2, 16], f32), "ZP": ("psum", [128, 64, 8], f32),
@@ -47,18 +49,21 @@ for _s in range(S - 1):
     SCRATCH["MS%d" % _s] = _sb([4, 12], i32)
     SCRATCH["RX%d" % _s] = _sb([4, 12], i32)
 
-SEMAPHORES = ["cg", "cv", "ca", "cp", "sent", "ldL", "ldR", "ldX", "ldC0", "ldC1", "ldN0", "ldN1", "ldTE", "out0", "out1", "out2",
-              "arL", "arP", "arU0h", "arU0t", "arU1", "arU2", "arV0", "arV1", "arV2", "arT0", "arT1", "arK0", "arK1", "arB0", "arB1",
+SEMAPHORES = ["cg", "cv", "ca", "cp", "sent", "ldL", "ldR", "ldX", "ldC0", "ldC1", "ldN0", "ldN1", "ldN2", "ldTE", "out0", "out1", "out2",
+              "arL", "arP", "arU0h", "arU0t", "arU1", "arU2", "arV0", "arV1", "arV2", "arT0", "arT1", "arK0", "arK1", "arB0", "arB1", "arF0", "arF1",
               "spU0h", "spU0t", "spU1", "spU2", "spV0", "spV1", "spV2"]
 CNT = {"g": "cg", "v": "cv", "a": "ca", "p": "cp"}
-CYC, PEC, HOP, GAT, SCA = 0.85, 0.43, 140, 1.56, 3.8
-LATE = {"ldL": 2200, "ldN1": 2800, "ldN0": 4500, "ldX": 3600, "ldR": 2500, "ldC1": 4600, "ldC0": 5200, "ldTE": 6500}
-TUNE = {"bias": 6000, "patience": 1.0, "turns": 12000, "heat": 200, "seed": 1}
+CYC, PEC, HOP, GAT, SCA = 0.84, 0.44, 220, 1.56, 3.8
+LATE = {"ldL": 2200, "ldN1": 2600, "ldN0": 3000, "ldX": 4200, "ldR": 2400, "ldC1": 5200, "ldC0": 6000, "ldN2": 7000, "ldTE": 6500, "arL": 3400}
+TUNE = {"bias": 10000, "patience": 1.0, "turns": 20000, "heat": 300, "seed": 2}
 LASTUNITS = [(4, 5), (2, 3), (0, 1)]
-HINTS = [{}, {}, {}]
+SUMS = {2: 6, 0: 2}
+HALVES = set()
+HINTS = [{}, {"SK0": "GS11"}, {}]
 RECIP = set()
 ONV = set()
-WIDE = {(s, x) for s in range(S) for x in (0, 2, 4)}
+STACK = {(s, x) for s in range(S) for x in (0, 2, 4)}
+WIDE = {(S - 1, x) for x in (0, 2, 4)}
 E16 = math.exp(16.0)
 _ORDER = {}
 QS = "vagsp"
@@ -75,6 +80,13 @@ def _order(ops, raised):
             elif d[2]:
                 p += [(j, LATE.get(d[1], 2400)) for j in raised[d[1]]]
         pre.append(p)
+    above = []
+    for i in range(n):
+        far = 0
+        for j, lag in pre[i]:
+            far |= above[j]
+        pre[i] = [(j, lag) for j, lag in pre[i] if lag > HOP or not far >> j & 1]
+        above.append(far | sum(1 << j for j in set(j for j, lag in pre[i])))
     post = [[] for _ in ops]
     for i in range(n):
         for j, lag in pre[i]:
@@ -298,14 +310,14 @@ def rank_program(g, core, T, topo):
     def pool(f, r, w, c):
         op("g", f, r, w, "", 150 + 2 * CYC * c)
 
-    TX_, TE_ = T.XB[:, 0:M], T.TB[:, 0:M]
+    TX_, TE_ = T.XB[:, 32:EO], T.TB[:, 32:EO]
     for x, sem, val in (("RL", "arL", 16), ("U0_0", "arU0h", 16), ("U0_1", "arU0t", 16)):
         wr[x] = ("s", sem, val)
     for s in range(S):
         wr["V%d" % s] = ("s", "arV%d" % s, 16)
         if s:
             wr["U%d_0" % s] = wr["U%d_1" % s] = ("s", "arU%d" % s, 16)
-            for x in "TKB":
+            for x in "TKBF":
                 wr["RX%s%d" % (x, s - 1)] = ("s", "ar%s%d" % (x, s - 1), 16)
 
     dma("g", TE_, T.ee[:], "", "TBE", "ldTE", 16)
@@ -314,15 +326,17 @@ def rank_program(g, core, T, topo):
     dma("s", T.LN[:, 24:36], T.rl[:], "", "LN", "ldL", 48)
     dma("a", T.XR[:, 0:64], T.xr[:], "", "XR", "ldR", 32)
     dma("a", T.XR[:, 64:128], T.er[:], "", "XR", "ldR", 32)
-    dma("a", T.EN[:, :, 192:384], T.nt[:], "", "EN1", "ldN1", 16)
+    dma("a", T.EN[:, 0, 192:384], T.nt[:, 0:L], "", "EN0_1", "ldN1", 16)
     dma("s", TX_, T.xe[:], "", "TBX", "ldX", 16)
-    dma("s", T.CT[:, NW:NW + NC], T.tc[:], "", "CT1", "ldC1", 16)
-    dma("a", T.EN[:, :, 0:192], T.nh[:], "", "EN0", "ldN0", 16)
-    dma("s", T.CT[:, 0:NC], T.hc[:], "", "CT0", "ldC0", 16)
+    dma("s", T.CT[:, NW + 16:2 * NW], T.tc[:], "", "CT1", "ldC1", 16)
+    dma("a", T.EN[:, 0, 0:192], T.nh[:, 0:L], "", "EN0_0", "ldN0", 16)
+    dma("s", T.CT[:, 16:NW], T.hc[:], "", "CT0", "ldC0", 16)
+    dma("s", T.EN[:, 1:3, 192:384], T.nt[:, L:3 * L], "", "EN1_1 EN2_1", "ldN2", 32)
+    dma("s", T.EN[:, 1:3, 0:192], T.nh[:, L:3 * L], "", "EN1_0 EN2_0", "ldN2", 32)
     pool(lambda q: q.iota(T.PI[:, 0:1], [[0, 1]], 0, 1), "", "PI", 1)
     pool(lambda q: q.iota(T.IC[:], [[1, 160]], 0, 0, allow_small_or_imprecise_dtypes=True), "", "IC", 160)
     pool(lambda q: q.iota(T.IG[:], [[16, 8], [0, 16]], 0, 0, allow_small_or_imprecise_dtypes=True), "", "IG", 128)
-    pool(lambda q: q.iota(T.VI[:], [[-1, 16], [0, 2]], 15, 0, allow_small_or_imprecise_dtypes=True), "", "VI", 32)
+    pool(lambda q: q.iota(T.VI[:], [[-1, 32], [0, 2]], 31, 0, allow_small_or_imprecise_dtypes=True), "", "VI", 64)
     pool(lambda q: q.iota(T.PRI[:], [[0, 24], [-1, 16]], 15, 0, allow_small_or_imprecise_dtypes=True), "", "PRI", 384)
     send("LN XR", [(nxt, T.LN[:, 0:32], T.RL[:, 0:32], "arL", 0, 4), (nxt, T.LN[:, 4:36], T.RL[:, 36:68], "arL", 4, 8),
                    (nxt, T.XR[:, 0:64], T.XR[:, 128:192], "arL", 8, 12), (nxt, T.XR[:, 64:128], T.XR[:, 192:256], "arL", 12, 16)])
@@ -330,7 +344,7 @@ def rank_program(g, core, T, topo):
     ms(T.UM[:], 0.0, "UMz", 1536)
     act(T.VM[:], T.UM[:], F.Copy, "UMz", "VMz", c=3072)
     ms(T.KA[:, 0:12], 1.0, "KA0"); ms(T.KA[:, 12:24], 37.0, "KA1")
-    ms(T.TB[:, M:EO], 0.0, "d0"); ms(T.XB[:, M:EO], 0.0, "d1"); ms(T.CT[:, NC:NW], 0, "d2"); ms(T.CT[:, NW + NC:2 * NW], 0, "d3")
+    ms(T.TB[:, 0:32], 0.0, "d0"); ms(T.XB[:, 0:32], 0.0, "d1"); ms(T.CT[:, 0:16], 0, "d2"); ms(T.CT[:, NW:NW + 16], 0, "d3")
     ms(T.ONES[:], 1.0, "ONES", 256); ms(T.PC[:, 7:8], -16.0, "PC7")
     ms(T.RM[:], 0.0, "RM", 384); ms(T.RM[:, 0:384:32], -1.0e9, "RM")
     ms(T.RW[:, :, 16], 1.0, "RWc"); ms(T.RH[:, :, 0], 0.0, "RHc"); ms(T.RO[:, :, 0], 0.0, "ROc")
@@ -355,18 +369,16 @@ def rank_program(g, core, T, topo):
     ts(T.PC[:, 3:4], T.PI[:, 0:1], 16.0, A.add, "PI", "PC3")
     cp(T.PC[:, 4:5], T.PJ[:, 1:2], "PJ1", "PC4")
     ts(T.PC[:, 5:6], T.PJ[:, 1:2], -1.0, A.mult, "PJ1", "PC5", s2=1.0, o1=A.add)
-    ts(T.PC[:, 6:7], T.PJ[:, 0:1], float(M), A.add, "PJ0", "PC6")
-    ts(T.PC[:, 12:13], T.PJ[:, 3:4], 2.0, A.mult, "PJ3", "PC12", s2=float(30 + KEY0), o1=A.add)
+    ts(T.PC[:, 12:13], T.PJ[:, 3:4], 2.0, A.mult, "PJ3", "PC12", s2=float(62 + KEY0), o1=A.add)
     tt(T.PC[:, 8:9], T.PC[:, 12:13], T.PJ[:, 4:5], A.subtract, "PC12 PJ4", "PC8")
-    ts(T.PC[:, 9:10], T.PJ[:, 0:1], float(NC), A.add, "PJ0", "PC9")
     cp(T.PC[:, 10:11], T.PJ[:, 2:3], "PJ2", "PC10")
     ts(T.PC[:, 11:12], T.PJ[:, 3:4], 2.0, A.mult, "PJ3", "PC11", s2=-1.0, o1=A.add)
-    cp(T.OW[:, 0:12], T.LN[:, 12:24], "LN", "OW0a"); cp(T.OT[:, 0:12], T.LN[:, 0:12], "LN", "OT0a")
+    ts(T.OW[:, 0:12], T.LN[:, 12:24], float(NC), A.add, "LN", "OW0a"); cp(T.OT[:, 0:12], T.LN[:, 0:12], "LN", "OT0a")
     ts(T.KB[:, 0:12], T.LN[:, 24:36], 37.0, A.mult, "LN", "KB0")
     cp(T.OO[:, 12:24], T.RL[:, 0:12], "RL", "OO1")
     cp(T.OT[:, 12:24], T.RL[:, 12:24], "RL OT0a", "OT0")
     cp(T.KB[:, 12:24], T.RL[:, 56:68], "RL", "KB1")
-    cp(T.OW[:, 12:24], T.RL[:, 0:12], "RL OW0a", "OW0")
+    ts(T.OW[:, 12:24], T.RL[:, 0:12], float(NC), A.add, "RL OW0a", "OW0")
     ts(T.IDF[:], T.IC[:, 16:144], T.PC[:, 3:4], A.is_equal, "IC PC3", "IDF", c=128)
     ts(T.IDD[:], T.IC[:, 0:64], T.PC[:, 10:11], A.is_equal, "IC PC10 PC11", "IDD", s2=T.PC[:, 11:12], o1=A.mult)
     ts(T.IT[:], T.VI[:], T.PC[:, 0:1], A.is_equal, "VI PC0", "IT")
@@ -374,13 +386,25 @@ def rank_program(g, core, T, topo):
     ts(T.W[:], T.IC[:], T.PC[:, 2:3], A.is_equal, "IC PC2", "W", s2=1.0 / 64, o1=A.mult, c=160)
     ts(T.PW0[:], T.IC[:], T.PC[:, 3:4], A.is_equal, "IC PC3 PC5", "PW0", s2=T.PC[:, 5:6], o1=A.mult, c=160)
     ts(T.PW1[:], T.IC[:], T.PC[:, 3:4], A.is_equal, "IC PC3 PC4", "PW1", s2=T.PC[:, 4:5], o1=A.mult, c=160)
-    ts(T.DM[:], T.PRI[:], T.PC[:, 0:1], A.is_equal, "PRI PC0", "DM", c=384)
+    ts(T.DM[:], T.PRI[:], T.PC[:, 0:1], A.is_equal, "PRI PC0", "DM", c=192)
+    ts(T.DN[:, 0:L], T.PRI[:, 0:L], T.PC[:, 0:1], A.is_equal, "PRI PC0", "DNa", c=96)
+    ms(T.DN[:, L:384], 0.0, "DNb", 96); ms(T.DN[:, L + 15:384:32], 1.0, "DN", r="DNa DNb")
+    ts(T.NI[:], T.IC[:, 16:144], T.PC[:, 3:4], A.is_equal, "IC PC3", "NI", s2=-1.0, o1=A.mult, c=128)
+    ts(T.PC[:, 6:7], T.PJ[:, 0:1], 16.0, A.add, "PJ0", "PC6")
+    ms(T.T1[:], 2560.0, "T1c T1_0 T1_1")
+    cp(T.BL[:], T.IC[:, 0:12], "IC", "BL"); ms(T.BL[:, 0:12:2], 12, "BL")
     for x in range(4):
         c = slice(512 * x, 512 * x + 512)
         pool(lambda q, c=c, x=x: q.affine_select(T.SEL[:, c], T.ONES[:], [[-1, 4], [-16, 8], [0, 16]], A.is_equal, 0.0, -4 * x, 1),
              "ONES", "SEL%d" % x, 512)
         pool(lambda q, c=c: q.affine_select(T.DD[:, c], T.SEL[:, c], [[0, 4], [-16, 8], [-1, 16]], A.not_equal, -1.0, 0, 1),
              "SEL%d" % x, "DD%d" % x, 512)
+    pool(lambda q: q.affine_select(T.SE2[:], T.SEL[:, 0:1024], [[-1, 8], [-16, 8], [0, 16]], A.not_equal, 1.0, -8, 1), "SEL0 SEL1", "SE2", 1024)
+    ts(T.PJ[:, 5:6], T.PI[:, 0:1], 3, A.arith_shift_right, "PI", "PJ5", s2=1, o1=A.bitwise_and)
+    cp(T.PC[:, 14:15], T.PJ[:, 5:6], "PJ5", "PC14")
+    ts(T.PC[:, 13:14], T.PJ[:, 5:6], -1.0, A.mult, "PJ5", "PC13", s2=1.0, o1=A.add)
+    for h in range(2):
+        ts(T["P8%d" % h][:], T.IC[:], T.PC[:, 3:4], A.is_equal, "IC PC3 PC%d" % (13 + h), "P8%d" % h, s2=T.PC[:, 13 + h:14 + h], o1=A.mult, c=160)
     for x in range(8):
         ms(T.DD[:, 16 * x:16 * x + 129 * 15 + 1:129], 0.0, "DDz%d" % x, r="DD0 DD1 DD2 DD3")
     DDN = " ".join("DDz%d" % x for x in range(8))
@@ -394,14 +418,14 @@ def rank_program(g, core, T, topo):
     def cands(s):
         for d in (1, 0):
             c = slice(L * d, L * d + L)
-            win = T.CT[:, NW * d:NW * d + NW].indirect(T.KO[:, 12 * d:12 * d + 12])
-            cp(T.CO[:, c], win, "CT%d d2 d3 KO" % d, "CO%d" % d, k=L)
-            tt(T.DF[:, c], win, T.EN[:, s, c], A.subtract, "CT%d d2 d3 KO EN%d" % (d, d), "DF%d" % d, k=L)
+            win = T.CT[:, NW * d + 16:NW * d + NW].indirect(T.KO[:, 12 * d:12 * d + 12])
+            cp(T.CO[:, c], win, "CT%d KO" % d, "CO%d" % d, k=L)
+            tt(T.DF[:, c], win, T.EN[:, s, c], A.subtract, "CT%d KO EN%d_%d" % (d, s, d), "DF%d" % d, k=L)
 
     def entrants(s):
         for d in (1, 0):
             c = slice(384 * s + L * d, 384 * s + L * d + L)
-            cp(T.ENO[:, c], T.EN[:, s, L * d:L * d + L], "EN%d" % d, "ENO%d_%d" % (s, d), c=L)
+            cp(T.ENO[:, c], T.EN[:, s, L * d:L * d + L], "EN%d_%d" % (s, d), "ENO%d_%d" % (s, d), c=L)
             ts(T.ENS[:, c], T.ENO[:, c], -1536.0, A.add, "ENO%d_%d" % (s, d), "ENS%d_%d" % (s, d), c=96)
 
     def spread(name, s, ds, sem):
@@ -456,14 +480,15 @@ def rank_program(g, core, T, topo):
         gather(T.XG[:, 32 * a:32 * a + 2048:2], TX_.indirect(T.ENO[:, 384 * s + a:384 * s + a + 64]), "TBX ENO%d_%d" % (s, d),
                "XG%d_0" % x, (s, x, 0))
         gather(T.XG[:, 32 * a + 1:32 * a + 2048:2], TX_.indirect(T.CO[:, a:a + 64]), "TBX CO%d" % d, "XG%d_1" % x, (s, x, 1))
-        P, bk = T.S0, "b0"
+        P, bk, more = ((lambda p, c: T.S0[p, c], "b0", ""), (lambda p, c: T.WL[p, 3, c], "b1", ""),
+                       (lambda p, c: T.KP[p, c], "b2", " K0"))[(x & 1) * (1 + s // 2)]
         for q4 in range(4):
-            mms([(P[32 * q4:32 * q4 + 32, j:128:16], T.XG[:, 32 * l:32 * l + 32], T.UM[:, :, l], True, True)
+            mms([(P(slice(32 * q4, 32 * q4 + 32), slice(j, 128, 16)), T.XG[:, 32 * l:32 * l + 32], T.UM[:, :, l], True, True)
                  for j in range(16) for l in [a + 16 * q4 + j]], "XG%d_0 XG%d_1 " % (x, x) + names("UM%d_%%d" % d, range(8)),
-                "sc%d" % q4, bk, 32)
-        o, src = T.SCP[:, 128 * x:128 * x + 128], P[:, 0:128]
-        ts(o, src, 32.0, A.mult, names("sc%d", range(4)) + " PC8", "SCP%d" % x, bk, s2=T.PC[:, 8:9], o1=A.add, c=128,
-           alt=lambda q: q.activation(o, src, F.Identity, bias=T.PC[:, 8:9], scale=32.0))
+                "sc%s_%d" % (bk, q4) + more, bk, 32)
+        o, src = T.SCP[:, 128 * x:128 * x + 128], P(slice(0, 128), slice(0, 128))
+        ts(o, src, 64.0, A.mult, names("sc%s_%%d" % bk, range(4)) + " PC8", "SCP%d" % x, bk, s2=T.PC[:, 8:9], o1=A.add, c=128,
+           alt=lambda q: q.activation(o, src, F.Identity, bias=T.PC[:, 8:9], scale=64.0))
         mms([(T.B3[:, 2 * slot:2 * slot + 2, :, :], o, T.IDD[:], True, True)], "SCP%d IDD" % x, "D%d" % slot, "b3", 256)
         if s < S - 1:
             mms([(T.KP[:, 128 * slot:128 * slot + 128], o, T.IDF[:], True, True)], "SCP%d IDF" % x, "K%d" % slot, "b2", 512)
@@ -482,8 +507,14 @@ def rank_program(g, core, T, topo):
            names("AL%d", xs), "b3", c=64 * m)
         ts(T.AO[:, c], T.AL[:, c], 1536.0, A.add, names("AL%d", xs), names("AO%d", xs), c=32 * m)
         for x in xs:
-            gather(T["EG%d" % (s & 1)][:, 1024 * x:1024 * x + 1024], TE_.indirect(T.AO[:, 64 * x:64 * x + 64]), "TBE AO%d" % x,
-                   "EG%d_%d" % (s & 1, x), (s, x, 2))
+            EG = T["EG%d" % (s & 1)]
+            if (s, x) in HALVES:
+                for y in (2 * x, 2 * x + 1):
+                    cp(EG[:, 512 * y:512 * y + 512], TE_.indirect(T.AO[:, 32 * y:32 * y + 32]), "TBE AO%d" % x, "EG%d_%d" % (s & 1, y),
+                       either=True, k=512)
+            else:
+                cp(EG[:, 1024 * x:1024 * x + 1024], TE_.indirect(T.AO[:, 64 * x:64 * x + 64]), "TBE AO%d" % x,
+                   names("EG%d_%%d" % (s & 1), (2 * x, 2 * x + 1)), either=True, k=1024)
 
     def best(s, d):
         MS, RX, c, h = T["MS%d" % s], T["RX%d" % s], slice(L * d, L * d + L), slice(12 * d, 12 * d + 12)
@@ -492,29 +523,34 @@ def rank_program(g, core, T, topo):
         ki, kn = (T.KI[:], "KI") if d else (MS[:, 0, :], "MK%d" % s)
         cp(ki, top, "SK%d" % d, kn)
         if d:
-            ts(MS[:, 3, :], ki, (1 << 19) - 32, A.bitwise_and, kn, "MF%d" % s)
+            ts(MS[:, 3, :], ki, 2 * KEY0 - 64, A.bitwise_and, kn, "MF%d" % s)
+            send("MF%d" % s, [(prv, MS[:, 3, :], RX[:, 1, :], "arF%d" % s, 0, 16)])
         else:
             send(kn, [(nxt, MS[:, 0, :], RX[:, 3, :], "arK%d" % s, 0, 16)])
-            tt(T.MI[:, h], top, RX[:, 1, :], A.is_ge, "SK0 RXT%d" % s, "MI0")
-            ts(T.LM[:], T.MI[:, h], 32.0, A.mult, "MI0", "LM", s2=-32.0, o1=A.add)
-        ts(T.KL[:, h], ki, 31, A.bitwise_and, kn, "KL%d" % d)
-        cp(T.KS[:, h], T.KL[:, h], "KL%d" % d, "KS%d" % d)
-        tt(T.YB[:, c], T.IT[:, 0:32].indirect(T.KS[:, h]), T.AL[:, c], A.mult, "IT KS%d " % d + names("AL%d", range(3 * d, 3 * d + 3)),
-           "YB%d" % d, k=L)
-        cv = T.B3[:, 12, d, 0:12]
-        mms([(cv, T.W[:, 15 - j:143 - j], T.YB[:, L * d + j:L * d + L:16], j == 0, j == 15) for j in range(16)], "W YB%d" % d,
-            "cv%d" % d, "b3", 64)
+            tt(T.MI[:, h], top, RX[:, 1, :], A.is_ge, "SK0 RXF%d" % s, "MI0")
+            ts(T.LM[:], T.MI[:, h], -40.0, A.mult, "MI0", "LM", s2=40.0, o1=A.add)
+        ts(T.KL[:, h], ki, 63, A.bitwise_and, kn, "KL%d" % d)
         if d == 0:
-            tt(T.T1[:, h], cv, T.MI[:, h], A.mult, "cv0 MI0", "T1_0", "b3")
-            tt(T.B16[:, h], T.T1[:, h], T.LM[:], A.add, "T1_0 LM", "B16_0")
-        ts(MS[:, 1 + d, :], cv, 64.0, A.mult, "cv%d" % d, "MB%d_%d" % (s, d), "b3", s2=1536.0, o1=A.add)
+            tt(T.KL[:, h], T.KL[:, h], T.MI[:, h], A.mult, "KL0 MI0", "KL0")
+        cp(T.KS[:, h], T.KL[:, h], "KL%d" % d, "KS%d" % d)
+        tt(T.YB[:, c], T.IT[:, 0:64].indirect(T.KS[:, h]), T.AL[:, c], A.mult, "IT KS%d " % d + names("AL%d", range(3 * d, 3 * d + 3)),
+           "YB%d" % d, k=L)
+
+    def entity(s, d):
+        MS, RX, c, h = T["MS%d" % s], T["RX%d" % s], slice(L * d, L * d + L), slice(12 * d, 12 * d + 12)
+        cv = T.WL[:, 0, 16 * d:16 * d + 12]
+        mms([(cv, T.NI[:], T.LM[:], True, False)][d:] +
+            [(cv, T.W[:, 15 - j:143 - j], T.YB[:, L * d + j:L * d + L:16], d == 1 and j == 0, j == 15) for j in range(16)],
+            "W YB%d" % d + " NI LM" * (1 - d), "cv%d" % d, "b1", 64)
+        if d == 0:
+            cp(T.B16[:, h], cv, "cv0", "B16_0", "b1")
+            ts(T.T1[:, 0:12], cv, 64.0, A.mult, "cv0", "T1_0", "b1", s2=1536.0 + NC, o1=A.add)
+        ts(MS[:, 1 + d, :], cv, 64.0, A.mult, "cv%d" % d, "MB%d_%d" % (s, d), "b1", s2=1536.0 + NC, o1=A.add)
         if d:
-            send("MB%d_1 MF%d" % (s, s), [(prv, MS[:, 2:4, :], RX[:, 0:2, :], "arT%d" % s, 0, 16)])
-            ts(T.CP[:], cv, 32.0, A.add, "cv1", "CP", "b3")
+            send("MB%d_1" % s, [(prv, MS[:, 2, :], RX[:, 0, :], "arT%d" % s, 0, 16)])
         else:
             send("MB%d_0" % s, [(nxt, MS[:, 1, :], RX[:, 2, :], "arB%d" % s, 0, 16)])
-        ts(T.BO[:, h], cv, 64.0, A.mult, "cv%d" % d, "BO%d" % d, "b3", s2=1536.0, o1=A.add)
-        ts(T.BD[:, h], MS[:, 1 + d, :], T.PC[:, 6:7], A.subtract, "MB%d_%d PC6" % (s, d), "BD%d" % d)
+        ts(T.BO[:, h], cv, 64.0, A.mult, "cv%d" % d, "BO%d" % d, "b1", s2=1536.0, o1=A.add)
         tt(T.XS[:, c], TX_.indirect(T.BO[:, h]), T.SG[:, c], A.subtract, "TBX BO%d SG%d" % (d, d), "XS%d" % d, k=L)
         ts(T.XS[:, c], T.XS[:, c], -7.0, A.max, "XS%d" % d, "XS%d" % d, s2=7.0, o1=A.min, c=96)
 
@@ -526,21 +562,30 @@ def rank_program(g, core, T, topo):
         MS, RX, c, h = T["MS%d" % s], T["RX%d" % s], slice(L * d, L * d + L), slice(12 * d, 12 * d + 12)
         if d:
             tt(T.MI[:, h], MS[:, 3, :], RX[:, 3, :], A.is_gt, "MF%d RXK%d" % (s, s), "MI1")
-            tt(T.T1[:, h], T.CP[:], T.MI[:, h], A.mult, "CP MI1", "T1_1")
-            ts(T.B16[:, h], T.T1[:, h], -32.0, A.add, "T1_1", "B16_1")
-        tt(T.BM[:, h], T.BD[:, h], T.MI[:, h], A.mult, "BD%d MI%d" % (d, d), "BM%d" % d)
-        firsts(T.B16[:, h], "B16_%d" % d, lambda i: T.S0[:, 128 + i:128 + L:16], T.S0[:, 128:128 + L], "b0", T.SD[:, c], ("SD%d" % d, "dd"), L)
-        ts(T.ND[:, h], T.SD[:, L * d + 15:L * d + L:16], 0.0, A.not_equal, "SD%d" % d, "ND%d" % d)
-        tt(T.T2[:, h], T.ND[:, h], T.BM[:, h], A.mult, "ND%d BM%d" % (d, d), "T2_%d" % d)
-        ts(T.SO[:, 24 * d:24 * d + 24:2], T.T2[:, h], T.PC[:, 6:7], A.add, "T2_%d PC6" % d, "SO%d" % d)
+            tt(T.T1[:, 16:28], MS[:, 2, :], T.MI[:, h], A.mult, "MB%d_1 MI1" % s, "T1_1")
+            ts(T.B16[:, h], T.T1[:, 16:28], 1.0 / 64, A.mult, "T1_1", "B16_1", s2=-40.0, o1=A.add)
+        t1, nd = T.T1[:, 16 * d:16 * d + 12], T.ND[:, 24 * d:24 * d + 24]
+        ts(T.BR[:], T.T1[:, 16 * d:16 * d + 16].indirect(T.BL[:, 0:12]), 1.0 / 64, A.mult, "T1c BL T1_%d" % d, "BR", s2=-40.0, o1=A.add, k=L)
+        mms([(T.S0[:, 143 - j:320:16], T.DD[:, 128 * j:128 * j + 128], T.B16[:, h], True, True) for j in range(16)],
+            DDN + " B16_%d" % d, "dd", "b0", 64)
+        mms([(T.S0[:, 320:512], T.NI[:], T.BR[:], True, False)] +
+            [(T.S0[:, 336 + j:512:32], T.SEL[:, 128 * j:128 * j + 128], T.B16[:, 12 * d:12 * d + 12:2], False, j == 15) for j in range(16)],
+            "SEL0 SEL1 SEL2 SEL3 NI BR B16_%d" % d, "de", "b0", 72)
+        scan(T.SD[:], T.S0[:, 128:512], T.DN[:], A.mult, A.add, "dd de DN", "SD", "b0", 384)
+        ts(nd, T.SD[:, 15:384:16], 0.0, A.not_equal, "SD", "ND%d" % d)
+        tt(T.T2[:, h], T.ND[:, 24 * d:24 * d + 12], t1, A.mult, "ND%d T1_%d" % (d, d), "T2_%d" % d)
+        tt(T.T2[:, h], T.T2[:, h], T.ND[:, 24 * d + 12:24 * d + 24], A.mult, "ND%d T2_%d" % (d, d), "T2_%d" % d)
+        for o in range(2):
+            ts(T.SO[:, 12 * d + o:12 * d + 12:2], T.T2[:, 12 * d + o:12 * d + 12:2], 32.0 - NC, A.add, "T2_%d PC0 PC6" % d, "SO%d_%d" % (d, o),
+               s2=T.PC[:, 6 * o:6 * o + 1], o1=A.max)
 
     def write(e, d):
-        for c in range(12 * d + 11, 12 * d - 1, -1):
-            at, p = T.SO[:, 2 * c:2 * c + 1], slice(16 * c, 16 * c + 16)
+        for c in range(6 * d + 5, 6 * d - 1, -1):
+            at, p = T.SO[:, 2 * c:2 * c + 2], slice(32 * c, 32 * c + 32)
             if e:
-                tt(T.TB[:, 0:EO].indirect(at), T.E7[:, p], T.WV[:, p], A.add, "SO%d d0 E7 WV" % d, "TBE", k=-16)
+                tt(T.TB[:, 0:EO].indirect(at), T.E7[:, p], T.WV[:, p], A.add, "SO%d_0 SO%d_1 d0 E7 WV" % (d, d), "TBE", k=-32)
             else:
-                cp(T.XB[:, 0:EO].indirect(at), T.XS[:, p], "SO%d d1 XS%d" % (d, d), "TBX", k=-16)
+                cp(T.XB[:, 0:EO].indirect(at), T.XS[:, p], "SO%d_0 SO%d_1 d1 XS%d" % (d, d, d), "TBX", k=-32)
 
     def proposals(s):
         V, Z = T["V%d" % s], T.KP[:, 0:384]
@@ -551,12 +596,11 @@ def rank_program(g, core, T, topo):
         tt(T.WV[:], Z, V[:], A.mult, "V%d K0" % s, "WV", "b2", c=384)
 
     def cache_targets():
-        ts(T.K16[:], T.K3[:], 1.0 / 64, A.mult, "K3", "K16")
-        ts(T.C1[:], T.K3[:], T.PC[:, 9:10], A.subtract, "K3 PC9", "C1")
-        firsts(T.K16[:], "K16", lambda i: T.S0[:, 128 + i:512:16], T.S0[:, 128:512], "b0", T.SE[:], ("SE", "dd"), 384)
+        ts(T.K16[:], T.K3[:], 16.0, A.add, "K3", "K16", s2=1.0 / 64, o1=A.mult)
+        firsts(T.K16[:], "K16", lambda i: T.S0[:, 128 + i:512:16], T.S0[:, 128:512], "b0", T.SE[:], ("SE", "dd de"), 384)
         ts(T.NE[:], T.SE[:, 15:384:16], 0.0, A.not_equal, "SE", "NE")
-        tt(T.C2[:], T.NE[:], T.C1[:], A.mult, "NE C1", "C2")
-        ts(T.CSO[:, 0:48:2], T.C2[:], T.PC[:, 9:10], A.add, "C2 PC9", "CSO")
+        tt(T.C2[:], T.NE[:], T.K16[:], A.mult, "NE K16", "C2")
+        ts(T.CSO[:, 0:48:2], T.C2[:], 64.0, A.mult, "C2 PC0", "CSO", s2=T.PC[:, 0:1], o1=A.max)
 
     def cache_write(d):
         for c in range(12 * d + 11, 12 * d - 1, -1):
@@ -572,7 +616,7 @@ def rank_program(g, core, T, topo):
         tt(T.T5[:], T.MI[:], T.DO[:], A.mult, "MI0 MI1 DO", "T5")
         keys(s + 1)
         tt(T.OW[:, b], T.T5[:], T.OW[:, a], A.add, "T5 OW%d" % s, "OW%d" % (s + 1))
-        cp(T.OO[:], T.OW[:, b], "OW%d" % (s + 1), "OO0 OO1")
+        ts(T.OO[:], T.OW[:, b], -float(NC), A.add, "OW%d" % (s + 1), "OO0 OO1")
 
     turns = [0, 0]
 
@@ -599,15 +643,16 @@ def rank_program(g, core, T, topo):
                 for j2 in range(2):
                     mms([(Z[:, j % 8:64:8, :], EG[:, 16 * l:16 * l + 128], T.VM[:, :, l:l + 8], True, True)
                          for j in range(8 * b + 4 * j2, 8 * b + 4 * j2 + 4) for l in [l0 + 8 * j]],
-                        "EG%d_%d " % (s & 1, xs[b]) + vm, "z%s_%d" % (bk, j2), bk, 256)
-                for a in range(4):
-                    p = slice(32 * a, 32 * a + 32)
-                    fetch(WS[p, :, 16 * b:16 * b + 16], Z[p, :, 2 * a:2 * a + 2], "z%s_0 z%s_1" % (bk, bk), "WS%d_%d" % (y, 4 * b + a), bk, 128)
+                        "EG%d_%d " % (s & 1, 2 * xs[b] + j2) + vm, "z%s_%d" % (bk, j2), bk, 256)
+                four = [(WS[32 * a:32 * a + 32, :, 16 * b:16 * b + 16], Z[32 * a:32 * a + 32, :, 2 * a:2 * a + 2]) for a in range(4)]
+                op("v", lambda q, four=four: [q.tensor_copy(o, i) for o, i in four][-1], "z%s_0 z%s_1" % (bk, bk),
+                   names("WS%d_%%d" % y, range(4 * b, 4 * b + 4)), bk, 4 * vns(128, 0),
+                   alt=(lambda q, four=four: [q.activation(o, i, F.Copy) for o, i in four][-1], 4 * ans(128, 0)))
         else:
             for j4 in range(4):
                 mms([(T.ZP[32 * a:32 * a + 32, 32 * y + j // 4:32 * y + 32:4, 2 * (j % 4):2 * (j % 4) + 2], EG[:, 16 * l:16 * l + 32],
                       T.VM[:, :, l:l + 2], True, True) for j in range(4 * j4, 4 * j4 + 4) for a in range(na)
-                     for l in [l0 + 2 * na * j + 2 * a]], "EG%d_%d " % (s & 1, xs[j4 * len(xs) // 4]) + vm, "zb5_%d" % j4, "b5", 128)
+                     for l in [l0 + 2 * na * j + 2 * a]], "EG%d_%d " % (s & 1, 2 * xs[0] + j4 * len(xs) // 2) + vm, "zb5_%d" % j4, "b5", 128)
             fetch(WS[rows, :, :], T.ZP[rows, 32 * y:32 * y + 32, :], names("zb5_%d", range(4)), names("WS%d_%%d" % y, range(8)), "b5", 256)
         wn, rn = names("Wp%d", xs), names("R%%s%d", xs)
         mms([(T.WP[:, w0:w0 + na, h, :], WS[rows, :, h:32:2], T.IDF[rows, 0:na, h, :], True, True) for h in range(2)],
@@ -623,23 +668,37 @@ def rank_program(g, core, T, topo):
         tt(Wp, Wp, T.RW[:, ms_, 1:17], A.mult, wn + " RWc " + rn.replace("%s", "W"), wn, "b4", c=32 * na)
         cp(T.RH[:, ms_, 1:17], Wp, wn, rn.replace("%s", "H"), "b4", either=True, c=32 * na)
         tt(T.RO[:, ms_, 1:17], Wp, T.RH[:, ms_, 1:17], A.subtract, wn + " " + rn.replace("%s", "H"), rn.replace("%s", "O"), "b4", c=32 * na)
-        k, wide = 16 // na, 32 * na
+        k, wide, stack = 16 // na, 32 * na, (s, xs[0]) in STACK
+        both = "RHc ROc " + rn.replace("%s", "H") + " " + rn.replace("%s", "O")
+        if stack:
+            for h, o in enumerate((Wp, T.WP[:, 12:16, :, :])):
+                mms([(o, T["P8%d" % h][:, 16 + 8 * (h - i):144 + 8 * (h - i)], T[x][:, ms_, 0:16], i == 0, i == 1)
+                     for i, x in enumerate(("RH", "RO"))], "P80 P81 " + both, (wn, "Wx")[h], "b4", 128)
+                op("v", lambda q, h=h, o=o: q.tensor_copy(T["TS%d" % y][:, 128 * h:128 * h + 128], o), (wn, "Wx")[h], "TS%d_%d" % (y, h), "b4",
+                   vns(128, 0))
         for j in range(0, 16, k):
             p = turns[1] & 1
             turns[1] += 1
             RB, a = T["RB%d" % p], l0 + 2 * na * j
-            mms([(RB[:, wide * i:wide * i + wide], T.SEL[:, 128 * (j + i):128 * (j + i) + 128], T[x][:, ms_, 0:16], x == "RH", x == "RO")
-                 for i in range(k) for x in ("RH", "RO")],
-                "SEL0 SEL1 SEL2 SEL3 RHc ROc " + rn.replace("%s", "H") + " " + rn.replace("%s", "O"), "rb%d" % p, "r%d" % p, wide)
+            if stack:
+                mms([(RB[:, 128 * i:128 * i + 128], T.SE2[:, 128 * ((j + i) % 8):128 * ((j + i) % 8) + 128],
+                      T["TS%d" % y][:, 128 * (j // 8):128 * (j // 8) + 128], True, True) for i in range(k)],
+                    "SE2 TS%d_%d" % (y, j // 8), "rb%d" % p, "r%d" % p, 128)
+            else:
+                mms([(RB[:, wide * i:wide * i + wide], T.SEL[:, 128 * (j + i):128 * (j + i) + 128], T[x][:, ms_, 0:16], x == "RH", x == "RO")
+                     for i in range(k) for x in ("RH", "RO")], "SEL0 SEL1 SEL2 SEL3 " + both, "rb%d" % p, "r%d" % p, wide)
             scan(T.GS[:, 16 * a:16 * a + 512], RB[:], EG[:, 16 * a:16 * a + 512], A.mult, A.add,
-                 "rb%d EG%d_%d" % (p, s & 1, a // 64), "GS%d" % (a // 32), "r%d" % p, 512)
+                 "rb%d EG%d_%d" % (p, s & 1, a // 32), "GS%d" % (a // 32), "r%d" % p, 512)
 
     def gather_up(s, xs, na):
         a, b, w = 64 * xs[0], 64 * xs[-1] + 64, 2 * na
         flat = T.WL[:, a // 128, a % 128:a % 128 + b - a] if b - a <= 128 else T.WL[:, a // 128:b // 128, :]
-        mms([(T.WL[:, a // 128:(b + 127) // 128, a % 128 + w * j:a % 128 + w * j + w], T.SEL[:, 128 * j:128 * j + 128],
-              T[x][:, a // 16:b // 16, 16], x == "RH", x == "RO") for j in range(16) for x in ("RH", "RO")],
-            "SEL0 SEL1 SEL2 SEL3 " + names("RH%d", xs) + " " + names("RO%d", xs), names("wl%d", xs), "b1", 64)
+        m = (b - a) // 16
+        mms([(T.WL[:, a // 128, m * h:m * h + m], T["P8%d" % h][:, 16 + 8 * (h - i):144 + 8 * (h - i)], T[x][:, a // 16:b // 16, 16], i == 0, i == 1)
+             for h in range(2) for i, x in enumerate(("RH", "RO"))], "P80 P81 " + names("RH%d", xs) + " " + names("RO%d", xs), "wl%d" % xs[0], "b1", 64)
+        op("v", lambda q: q.tensor_copy(T.TW[:, 0:2 * m], T.WL[:, a // 128, 0:2 * m]), "wl%d" % xs[0], "TW", "b1", vns(0, 0))
+        mms([(T.WL[:, a // 128:(b + 127) // 128, a % 128 + w * j:a % 128 + w * j + w], T.SE2[:, 128 * (j % 8):128 * (j % 8) + 128],
+              T.TW[:, m * (j // 8):m * (j // 8) + m], True, True) for j in range(16)], "SE2 TW", names("wl%d", xs), "b1", 64)
         gs = names("wl%d", xs) + " " + names("GS%d", range(a // 32, b // 32))
         last = T.GS[:, 16 * a + 15:16 * b:16]
         if s == 0:
@@ -657,21 +716,28 @@ def rank_program(g, core, T, topo):
             for d in (1, 0):
                 step[0] = str(s) + "ht"[d]
                 c = slice(L * d, L * d + L)
-                act(T.SG[:, c], T["U%d" % s][:, c], F.Sign, "U%d_%d" % (s, d), "SG%d" % d, c=L)
+                ts(T.SG[:, c], T["U%d" % s][:, c], -1.0, A.max, "U%d_%d" % (s, d), "SG%d" % d, s2=1.0, o1=A.min, c=96, ca=L,
+                   alt=lambda q, c=c, s=s: q.activation(T.SG[:, c], T["U%d" % s][:, c], F.Sign))
                 for x in range(3):
                     scores(s, 3 * d + x, x)
+                if d == 0:
+                    entity(s, 1)
                 contest(s, range(3 * d, 3 * d + 3))
                 best(s, d)
+            entity(s, 0)
             step[0] = str(s)
             if s == 0:
                 cache_targets()
+            else:
+                gather_up(0, range(6), 4)
             cache_write(1); cache_write(0)
             targets(s, 0); write(0, 0); targets(s, 1); write(0, 1)
             triples(s); cands(s + 1); usend(s + 1)
             proposals(s); write(1, 0); write(1, 1); vsend(s + 1)
             for xs in ((4, 5), (2, 3), (0, 1)):
                 output(s, xs)
-            gather_up(s, range(6), 4)
+            if s:
+                gather_up(s, range(6), 4)
             spread("V", s + 1, (0, 1), "spV%d" % (s + 1))
         else:
             for xs in LASTUNITS:
@@ -679,7 +745,8 @@ def rank_program(g, core, T, topo):
                     scores(s, x, i)
                 contest(s, xs)
                 output(s, xs)
-                gather_up(s, xs, 2 * len(xs))
+                if xs[0] in SUMS:
+                    gather_up(s, range(xs[0], SUMS[xs[0]]), 2 * len(xs))
             dma("s", T.yt[:], T.ACC[:, L:384], "ACC3 ACC4 ACC5", "yt", "out1", 16)
             dma("s", T.yh[:], T.ACC[:, 0:L], "ACC0 ACC1 ACC2", "yh", "out0", 16)
 

import math
import numpy as np
from concourse.bass import DstId, RemoteDMATransfer
from concourse.mybir import AluOpType as A, ActivationFunctionType as F

M, L, S, NC = 3072, 192, 3, 1024
EO = M + 32
NW = NC + 16
KEY0 = 1 << 19
f32, bf, i32, u16, f16 = "float32", "bfloat16", "int32", "uint16", "float16"


def _sb(n, d):
    return ("sbuf", [128] + (n if isinstance(n, list) else [n]), d)


SCRATCH = {
    "XB": _sb(EO, bf), "TB": _sb(EO, f32), "CT": _sb(2 * NW, i32), "EN": _sb([3, 384], i32),
    "ENO": _sb(1152, u16), "ENS": _sb(1152, f16), "LN": _sb(36, i32), "RL": _sb(68, i32), "XR": _sb(256, bf),
    "XP": _sb(384, bf), "EP": _sb(384, bf), "OW": _sb(72, f32), "OT": _sb(72, f32), "KA": _sb(24, f32), "KB": _sb(24, f32),
    "K1": _sb(24, f32), "K2": _sb(24, i32), "K3": _sb(24, i32), "KO": _sb(24, u16),
    "K16": _sb(24, f16), "PO": _sb(24, u16), "OO": _sb(24, u16), "CO": _sb(384, u16), "DF": _sb(384, f32),
    "XG": _sb(12288, bf), "UM": _sb([8, 384], bf), "VM": _sb([8, 384], f32),
    "EG0": _sb(6144, f32), "EG1": _sb(6144, f32), "GS": _sb(6144, f32),
    "SCP": _sb(768, f32), "SK": _sb(768, f32), "LB": _sb(384, bf), "LT": _sb([24, 16], bf), "KI": _sb(12, i32),
    "KL": _sb(24, i32), "KS": _sb(24, u16), "AL": _sb(384, f16), "AO": _sb(384, u16), "YB": _sb(384, f16),
    "BO": _sb(24, u16), "SG": _sb(384, bf), "XS": _sb(384, bf), "EV": _sb(384, f32), "E7": _sb(384, f32), "WV": _sb(384, f32),
    "MI": _sb(24, f32), "LM": _sb(12, f16), "DO": _sb(24, f32),
    "T1": _sb(32, f32), "T2": _sb(24, f32), "T3": _sb(24, f32), "T4": _sb(24, f32), "T5": _sb(24, f32), "B16": _sb(24, f16),
    "SD": _sb(384, f32), "SE": _sb(384, f32), "ND": _sb(48, f32), "SO": _sb(24, u16), "NE": _sb(24, f32),
    "C2": _sb(24, f32), "CSO": _sb(48, u16), "WS0": _sb([8, 32], f32), "WS1": _sb([8, 32], f32),
    "RW": _sb([24, 17], f32), "RH": _sb([24, 17], bf), "RO": _sb([24, 17], f16), "ACC": _sb(384, f32),
    "PI": _sb(8, i32), "PJ": _sb(8, i32), "PC": _sb(16, f32), "IC": _sb(160, f32), "IG": _sb(128, f32), "PRI": _sb(384, bf),
    "VI": _sb(64, f32), "IT": _sb(64, bf), "W": _sb(160, bf), "PW0": _sb(160, bf), "PW1": _sb(160, bf),
    "IDF": _sb([4, 2, 16], f32), "IDD": _sb(64, f32), "ONE": _sb(128, f32), "RM": _sb(384, f32), "DM": _sb(384, bf),
    "DN": _sb(384, bf), "NI": _sb(128, bf), "BL": _sb(12, u16), "BR": _sb(192, f16),
    "P80": _sb(160, bf), "P81": _sb(160, bf), "SE2": _sb(1024, bf), "TS0": _sb(256, f16), "TS1": _sb(256, f16), "TW": _sb(48, f16),
    "ONES": _sb(512, bf), "SEL": _sb(2048, bf), "DD": _sb(2048, bf),
    "S0": ("psum", [128, 512], f32), "WL": ("psum", [128, 4, 128], f32), "KP": ("psum", [128, 512], f32),
    "B3": ("psum", [128, 16, 2, 16], f32), "WP": ("psum", [128, 16, 2, 16], f32), "ZP": ("psum", [128, 64, 8], f32),
    "RB0": ("psum", [128, 512], f32), "RB1": ("psum", [128, 512], f32),
}
for _s in range(S):
    SCRATCH["U%d" % _s] = _sb(384, bf)
    SCRATCH["V%d" % _s] = _sb(384, f32)
    SCRATCH["UO%d" % _s] = _sb(384, bf)
    SCRATCH["VO%d" % _s] = _sb(384, f32)
for _s in range(S - 1):
    SCRATCH["MS%d" % _s] = _sb([4, 12], i32)
    SCRATCH["RX%d" % _s] = _sb([4, 12], i32)

SEMAPHORES = ["cg", "cv", "ca", "cp", "sent", "ldL", "ldR", "ldX", "ldC0", "ldC1", "ldN0", "ldN1", "ldN2", "ldTE", "out0", "out1", "out2",
              "arL", "arP", "arU0h", "arU0t", "arU1", "arU2", "arV0", "arV1", "arV2", "arT0", "arT1", "arK0", "arK1", "arB0", "arB1", "arF0", "arF1",
              "spU0h", "spU0t", "spU1", "spU2", "spV0", "spV1", "spV2"]
CNT = {"g": "cg", "v": "cv", "a": "ca", "p": "cp"}
CYC, PEC, HOP, GAT, SCA = 0.84, 0.44, 220, 1.56, 3.8
LATE = {"ldL": 2200, "ldN1": 2600, "ldN0": 3000, "ldX": 4200, "ldR": 2400, "ldC1": 5200, "ldC0": 6000, "ldN2": 7000, "ldTE": 6500, "arL": 3400}
TUNE = {"bias": 10000, "patience": 1.0, "turns": 20000, "heat": 300, "seed": 2}
LASTUNITS = [(4, 5), (2, 3), (0, 1)]
SUMS = {2: 6, 0: 2}
HALVES = set()
HINTS = [{}, {"SK0": "GS11"}, {}]
RECIP = set()
ONV = set()
STACK = {(s, x) for s in range(S) for x in (0, 2, 4)}
WIDE = {(S - 1, x) for x in (0, 2, 4)}
E16 = math.exp(16.0)
_ORDER = {}
QS = "vagsp"


def _order(ops, raised):
    n = len(ops)
    pre = []
    for e, fs, deps, dma, soft, cost, tag in ops:
        p = []
        for d in list(deps) + list(soft):
            if d[0] == "e":
                p.append((d[1], 0 if d in soft else HOP))
            elif d[2]:
                p += [(j, LATE.get(d[1], 2400)) for j in raised[d[1]]]
        pre.append(p)
    above = []
    for i in range(n):
        far = 0
        for j, lag in pre[i]:
            far |= above[j]
        pre[i] = [(j, lag) for j, lag in pre[i] if lag > HOP or not far >> j & 1]
        above.append(far | sum(1 << j for j in set(j for j, lag in pre[i])))
    post = [[] for _ in ops]
    for i in range(n):
        for j, lag in pre[i]:
            post[j].append((i, lag))
    left = [len(p) for p in post]
    prio = [0.0] * n
    todo = [i for i in range(n) if not left[i]]
    while todo:
        i = todo.pop()
        prio[i] = min(ops[i][5].values()) + max([prio[k] + lag for k, lag in post[i]] or [0])
        for j, lag in pre[i]:
            left[j] -= 1
            if not left[j]:
                todo.append(j)
    for i in range(n):
        if ops[i][3] and not pre[i]:
            prio[i] = 1e9 - i
        prio[i] += 1000.0 * TUNE.get(ops[i][6], 0)
    left = [len(p) for p in pre]
    ready = {e: {} for e in QS}
    for i in range(n):
        if not left[i]:
            for e in ops[i][5]:
                ready[e][i] = 0.0
    free = {e: 0.0 for e in QS}
    out, at, begin = [], [0.0] * n, [0.0] * n
    while len(out) < n:
        pick = None
        for e in QS:
            cand = ready[e]
            if not cand:
                continue
            t = max(free[e], min(cand.values()))
            pr = {i: prio[i] - (TUNE["bias"] if e == "v" and len(ops[i][5]) > 1 else 0) for i in cand}
            top = max(cand, key=lambda i: (pr[i] - max(0.0, cand[i] - t), -i))
            if cand[top] > t:
                gap = cand[top] - t
                now = [i for i in cand if cand[i] <= t]
                fits = [i for i in now if ops[i][5][e] <= gap + HOP]
                if fits:
                    top = max(fits, key=lambda i: (pr[i], -i))
                else:
                    b = max(now, key=lambda i: (pr[i], -i))
                    if gap > TUNE["patience"] * (ops[b][5][e] - gap) or pr[top] - pr[b] < ops[b][5][e]:
                        top = b
            t = max(t, cand[top])
            if pick is None or (t, ops[top][5][e]) < pick[0]:
                pick = ((t, ops[top][5][e]), e, top)
        (t, c), e, i = pick
        for e2 in ops[i][5]:
            del ready[e2][i]
        free[e] = t + c
        out.append((i, e))
        begin[i] = t
        for k, lag in post[i]:
            left[k] -= 1
            at[k] = max(at[k], t + c + lag)
            if not left[k]:
                for e2 in ops[k][5]:
                    ready[e2][k] = at[k]
    rng = np.random.RandomState(TUNE["seed"])

    def pack(key, on):
        st, en, beg, end = {e: [] for e in QS}, {e: [] for e in QS}, [0.0] * n, [0.0] * n
        for i in sorted(range(n), key=lambda i: key[i]):
            t = 0.0
            for j, lag in pre[i]:
                if end[j] + lag > t:
                    t = end[j] + lag
            c, a, b = ops[i][5][on[i]], st[on[i]], en[on[i]]
            k = m = len(a)
            while k and b[k - 1] > t:
                k -= 1
            while k < m and a[k] < t + c:
                t = max(t, b[k])
                k += 1
            a.insert(k, t)
            b.insert(k, t + c)
            beg[i], end[i] = t, t + c
        return beg, end

    def binding(beg, end, on):
        before, last, pairs = {}, {}, []
        for i in sorted(range(n), key=lambda i: beg[i]):
            before[i], last[on[i]] = last.get(on[i]), i
        i = max(range(n), key=lambda i: end[i])
        while i is not None:
            p, nx = before[i], None
            for j, lag in pre[i]:
                if abs(end[j] + lag - beg[i]) < 1:
                    nx = j
            if p is not None and abs(end[p] - beg[i]) < 1 and (nx is None or rng.rand() < 0.5):
                pairs.append((i, p))
                nx = p
            i = nx
        return pairs

    on = [e for i, e in sorted(out)]
    beg, end = pack(begin, on)
    now, best, pairs = max(end) + 0.03 * sum(beg) / n, (max(end), beg, on), binding(beg, end, on)
    for turn in range(TUNE["turns"]):
        key, on2, u = list(beg), on, rng.rand()
        i, p = pairs[rng.randint(len(pairs))]
        both = [x for x in (i, p) if len(ops[x][5]) > 1]
        if u < 0.3 and both:
            x, on2 = both[rng.randint(len(both))], list(on)
            on2[x] = "a" if on[x] == "v" else "v"
        elif u < 0.65:
            key[p] = beg[i] + (1, 300, 1000, 3000, 8000)[rng.randint(5)]
        else:
            key[i] = beg[p] - (1, 300, 1000, 3000)[rng.randint(4)]
            for a in range(i, -1, -1):
                for j, lag in post[a]:
                    if key[j] <= key[a]:
                        key[a] = key[j] - 0.01
        for a in range(n):
            for j, lag in pre[a]:
                if key[j] >= key[a]:
                    key[a] = key[j] + 0.01
        beg2, end2 = pack(key, on2)
        cost = max(end2) + 0.03 * sum(beg2) / n
        if cost <= now + TUNE["heat"] * (1 - turn / TUNE["turns"]) * rng.rand():
            now, beg, end, on = cost, beg2, end2, on2
            pairs = binding(beg, end, on)
            if max(end) < best[0]:
                best = (max(end), beg, on)
    return [(i, best[2][i]) for i in sorted(range(n), key=lambda i: (best[1][i], i))], best[0]


def rank_program(g, core, T, topo):
    rank = T.rank_of(core)
    if rank is None:
        return
    n = len(T.cores)
    nxt, prv = T.cores[(rank + 1) % n], T.cores[(rank - 1) % n]
    Q = {"g": g, "v": g.vector, "a": g.scalar, "p": g.tensor, "s": g.sync}
    ops, wr, rd, bank, sent, raised, step, hint = [], {}, {}, {}, [0], {}, ["s"], {}

    def op(e, f, r, w, b, c, dma=None, alt=None):
        i = len(ops)
        me = ("s",) + dma if dma else ("e", i)
        deps, soft = set(), set()
        for x in r.split():
            deps.add(wr[x])
        for x in w.split():
            deps.update(d for d in [wr.get(x)] + rd.get(x, []) if d)
        eng = "?%d" % i if alt else e
        for x in b.split():
            st = bank.setdefault(x, [None, [], []])
            if st[0] != eng:
                st[:] = [eng, [], st[1]]
            deps.update(st[2])
            if e == "p":
                soft.update(st[1][-1:])
            st[1].append(me)
        deps.discard(me)
        if e == "p":
            soft.update(d for d in deps if d[0] == "e" and ops[d[1]][0] == "p")
            deps -= soft
        soft.update(wr[x] for x in hint.pop(w, "").split() if wr[x] not in deps)
        for x in r.split():
            rd.setdefault(x, []).append(me)
        for x in w.split():
            wr[x] = me
            rd[x] = []
        if dma and dma[1]:
            raised.setdefault(dma[0], []).append(i)
        fs, cost = {e: f}, {e: c}
        if alt:
            fs["a"], cost["a"] = alt
        ops.append((e, fs, deps, dma, soft, cost, (w.split() or ["-"])[0].rstrip("0123456789_") + step[0]))

    def mask(dst, a, b):
        return sum(1 << e for e in topo.engines(core, dst)[a:b])

    def send(r, parts):
        trs = []
        for dst, src_ap, dst_ap, sem, a, b in parts:
            rid, pid = topo.addr(dst)[:2]
            trs.append(RemoteDMATransfer(dst_ids=[DstId(rid=rid, pnc=pid)], dma_engine_mask=mask(dst, a, b),
                                         remote_sem=T.sem[sem], src=src_ap, dst=dst_ap))
            sent[0] += b - a
            raised.setdefault(sem, []).append(len(ops))
        op("g", lambda q: q.remote_dma_fused(trs, local_sem=T.sem.sent), r, "", "", 900, dma=("sent", 0))

    def vns(c, k):
        return 50 + CYC * (GAT * k if k > 0 else -SCA * k) if k else 20 + CYC * max(64, c)

    def ans(c, k):
        return 65 + CYC * (GAT * k if k else c)

    def tt(out, a, b, o, r, w, bk="", c=0, k=0):
        op("v", lambda q: q.tensor_tensor(out, a, b, o), r, w, bk, vns(c, k))

    def ts(out, a, s1, o0, r, w, bk="", s2=None, o1=None, c=0, k=0, alt=None, ca=0):
        alt = alt and (alt, ans(ca or c, k))
        if o1 is None:
            op("v", lambda q: q.tensor_scalar(out, a, s1, None, o0), r, w, bk, vns(c, k), alt=alt)
        else:
            op("v", lambda q: q.tensor_scalar(out, a, s1, s2, o0, o1), r, w, bk, vns(c, k), alt=alt)

    def cp(out, a, r, w, bk="", either=False, c=0, k=0):
        op("v", lambda q: q.tensor_copy(out, a), r, w, bk, vns(c, k),
           alt=((lambda q: q.activation(out, a, F.Copy)), ans(c, k)) if either else None)

    def ms(out, v, w, c=0, r=""):
        op("v", lambda q: q.memset(out, v), r, w, "", vns(c, 0))

    def scan(out, a, b, o0, o1, r, w, bk, c):
        op("v", lambda q: q.tensor_tensor_scan(out, a, b, 0.0, o0, o1), r, w, bk, vns(c, 0))

    def act(out, a, fn, r, w, bk="", bias=0.0, scale=1.0, c=0, k=0):
        op("a", lambda q: q.activation(out, a, fn, bias=bias, scale=scale), r, w, bk, ans(c, k))

    def mms(calls, r, w, bk, c):
        op("p", lambda q: [q.matmul(*x) for x in calls][-1], r, w, bk, c * PEC * len(calls))

    def dma(e, out, a, r, w, sem, val):
        op(e, lambda q: q.dma_start(out, a), r, w, "", 900 if e == "g" else 100, dma=(sem, val))

    def pool(f, r, w, c):
        op("g", f, r, w, "", 150 + 2 * CYC * c)

    TX_, TE_ = T.XB[:, 32:EO], T.TB[:, 32:EO]
    for x, sem, val in (("RL", "arL", 16), ("U0_0", "arU0h", 16), ("U0_1", "arU0t", 16)):
        wr[x] = ("s", sem, val)
    for s in range(S):
        wr["V%d" % s] = ("s", "arV%d" % s, 16)
        if s:
            wr["U%d_0" % s] = wr["U%d_1" % s] = ("s", "arU%d" % s, 16)
            for x in "TKBF":
                wr["RX%s%d" % (x, s - 1)] = ("s", "ar%s%d" % (x, s - 1), 16)

    dma("g", TE_, T.ee[:], "", "TBE", "ldTE", 16)
    dma("s", T.LN[:, 0:12], T.tl[:], "", "LN", "ldL", 48)
    dma("s", T.LN[:, 12:24], T.hl[:], "", "LN", "ldL", 48)
    dma("s", T.LN[:, 24:36], T.rl[:], "", "LN", "ldL", 48)
    dma("a", T.XR[:, 0:64], T.xr[:], "", "XR", "ldR", 32)
    dma("a", T.XR[:, 64:128], T.er[:], "", "XR", "ldR", 32)
    dma("a", T.EN[:, 0, 192:384], T.nt[:, 0:L], "", "EN0_1", "ldN1", 16)
    dma("s", TX_, T.xe[:], "", "TBX", "ldX", 16)
    dma("s", T.CT[:, NW + 16:2 * NW], T.tc[:], "", "CT1", "ldC1", 16)
    dma("a", T.EN[:, 0, 0:192], T.nh[:, 0:L], "", "EN0_0", "ldN0", 16)
    dma("s", T.CT[:, 16:NW], T.hc[:], "", "CT0", "ldC0", 16)
    dma("s", T.EN[:, 1:3, 192:384], T.nt[:, L:3 * L], "", "EN1_1 EN2_1", "ldN2", 32)
    dma("s", T.EN[:, 1:3, 0:192], T.nh[:, L:3 * L], "", "EN1_0 EN2_0", "ldN2", 32)
    pool(lambda q: q.iota(T.PI[:, 0:1], [[0, 1]], 0, 1), "", "PI", 1)
    pool(lambda q: q.iota(T.IC[:], [[1, 160]], 0, 0, allow_small_or_imprecise_dtypes=True), "", "IC", 160)
    pool(lambda q: q.iota(T.IG[:], [[16, 8], [0, 16]], 0, 0, allow_small_or_imprecise_dtypes=True), "", "IG", 128)
    pool(lambda q: q.iota(T.VI[:], [[-1, 32], [0, 2]], 31, 0, allow_small_or_imprecise_dtypes=True), "", "VI", 64)
    pool(lambda q: q.iota(T.PRI[:], [[0, 24], [-1, 16]], 15, 0, allow_small_or_imprecise_dtypes=True), "", "PRI", 384)
    send("LN XR", [(nxt, T.LN[:, 0:32], T.RL[:, 0:32], "arL", 0, 4), (nxt, T.LN[:, 4:36], T.RL[:, 36:68], "arL", 4, 8),
                   (nxt, T.XR[:, 0:64], T.XR[:, 128:192], "arL", 8, 12), (nxt, T.XR[:, 64:128], T.XR[:, 192:256], "arL", 12, 16)])

    ms(T.UM[:], 0.0, "UMz", 1536)
    act(T.VM[:], T.UM[:], F.Copy, "UMz", "VMz", c=3072)
    ms(T.KA[:, 0:12], 1.0, "KA0"); ms(T.KA[:, 12:24], 37.0, "KA1")
    ms(T.TB[:, 0:32], 0.0, "d0"); ms(T.XB[:, 0:32], 0.0, "d1"); ms(T.CT[:, 0:16], 0, "d2"); ms(T.CT[:, NW:NW + 16], 0, "d3")
    ms(T.ONES[:], 1.0, "ONES", 256); ms(T.PC[:, 7:8], -16.0, "PC7")
    ms(T.RM[:], 0.0, "RM", 384); ms(T.RM[:, 0:384:32], -1.0e9, "RM")
    ms(T.RW[:, :, 16], 1.0, "RWc"); ms(T.RH[:, :, 0], 0.0, "RHc"); ms(T.RO[:, :, 0], 0.0, "ROc")
    cp(T.PO[:, 0:12], T.LN[:, 24:36], "LN", "PO0")
    cp(T.PO[:, 12:24], T.RL[:, 56:68], "RL", "PO1")
    cp(T.OO[:, 0:12], T.LN[:, 12:24], "LN", "OO0")
    for d in range(2):
        c, at, r = slice(L * d, L * d + L), T.PO[:, 12 * d:12 * d + 12], ("XR", "RL")[d] + " PO%d" % d
        x, e = T.XR[:, 128 * d:128 * d + 64].indirect(at), T.XR[:, 128 * d + 64:128 * d + 128].indirect(at)
        cp(T.XP[:, c], x, r, "XP%d" % d, either=True, k=L)
        ts(T.EP[:, c], e, 0.125, A.mult, r, "EP%d" % d, k=L, alt=lambda q, c=c, e=e: q.activation(T.EP[:, c], e, F.Copy, scale=0.125))
    tt(T.UO0[:, 0:L], TX_.indirect(T.OO[:, 0:12]), T.XP[:, 0:L], A.mult, "TBX OO0 XP0", "UO0_0", k=L)
    send("UO0_0", [(nxt, T.UO0[:, 0:L], T.U0[:, L:384], "arU0t", 0, 16)])
    ts(T.PJ[:, 0:1], T.PI[:, 0:1], 15, A.bitwise_and, "PI", "PJ0")
    ts(T.PJ[:, 1:2], T.PI[:, 0:1], 4, A.arith_shift_right, "PI", "PJ1", s2=1, o1=A.bitwise_and)
    ts(T.PJ[:, 2:3], T.PI[:, 0:1], 1, A.arith_shift_right, "PI", "PJ2")
    ts(T.PJ[:, 3:4], T.PI[:, 0:1], 1, A.bitwise_and, "PI", "PJ3")
    ts(T.PJ[:, 4:5], T.PI[:, 0:1], 31, A.bitwise_and, "PI", "PJ4")
    cp(T.PC[:, 0:1], T.PJ[:, 0:1], "PJ0", "PC0")
    tt(T.PC[:, 1:2], T.PI[:, 0:1], T.PJ[:, 0:1], A.subtract, "PI PJ0", "PC1")
    ts(T.PC[:, 2:3], T.PC[:, 1:2], 15.0, A.add, "PC1", "PC2")
    ts(T.PC[:, 3:4], T.PI[:, 0:1], 16.0, A.add, "PI", "PC3")
    cp(T.PC[:, 4:5], T.PJ[:, 1:2], "PJ1", "PC4")
    ts(T.PC[:, 5:6], T.PJ[:, 1:2], -1.0, A.mult, "PJ1", "PC5", s2=1.0, o1=A.add)
    ts(T.PC[:, 12:13], T.PJ[:, 3:4], 2.0, A.mult, "PJ3", "PC12", s2=float(62 + KEY0), o1=A.add)
    tt(T.PC[:, 8:9], T.PC[:, 12:13], T.PJ[:, 4:5], A.subtract, "PC12 PJ4", "PC8")
    cp(T.PC[:, 10:11], T.PJ[:, 2:3], "PJ2", "PC10")
    ts(T.PC[:, 11:12], T.PJ[:, 3:4], 2.0, A.mult, "PJ3", "PC11", s2=-1.0, o1=A.add)
    ts(T.OW[:, 0:12], T.LN[:, 12:24], float(NC), A.add, "LN", "OW0a"); cp(T.OT[:, 0:12], T.LN[:, 0:12], "LN", "OT0a")
    ts(T.KB[:, 0:12], T.LN[:, 24:36], 37.0, A.mult, "LN", "KB0")
    cp(T.OO[:, 12:24], T.RL[:, 0:12], "RL", "OO1")
    cp(T.OT[:, 12:24], T.RL[:, 12:24], "RL OT0a", "OT0")
    cp(T.KB[:, 12:24], T.RL[:, 56:68], "RL", "KB1")
    ts(T.OW[:, 12:24], T.RL[:, 0:12], float(NC), A.add, "RL OW0a", "OW0")
    ts(T.IDF[:], T.IC[:, 16:144], T.PC[:, 3:4], A.is_equal, "IC PC3", "IDF", c=128)
    ts(T.IDD[:], T.IC[:, 0:64], T.PC[:, 10:11], A.is_equal, "IC PC10 PC11", "IDD", s2=T.PC[:, 11:12], o1=A.mult)
    ts(T.IT[:], T.VI[:], T.PC[:, 0:1], A.is_equal, "VI PC0", "IT")
    ts(T.ONE[:], T.IG[:], T.PC[:, 1:2], A.is_equal, "IG PC1", "ONE", c=128)
    ts(T.W[:], T.IC[:], T.PC[:, 2:3], A.is_equal, "IC PC2", "W", s2=1.0 / 64, o1=A.mult, c=160)
    ts(T.PW0[:], T.IC[:], T.PC[:, 3:4], A.is_equal, "IC PC3 PC5", "PW0", s2=T.PC[:, 5:6], o1=A.mult, c=160)
    ts(T.PW1[:], T.IC[:], T.PC[:, 3:4], A.is_equal, "IC PC3 PC4", "PW1", s2=T.PC[:, 4:5], o1=A.mult, c=160)
    ts(T.DM[:], T.PRI[:], T.PC[:, 0:1], A.is_equal, "PRI PC0", "DM", c=192)
    ts(T.DN[:, 0:L], T.PRI[:, 0:L], T.PC[:, 0:1], A.is_equal, "PRI PC0", "DNa", c=96)
    ms(T.DN[:, L:384], 0.0, "DNb", 96); ms(T.DN[:, L + 15:384:32], 1.0, "DN", r="DNa DNb")
    ts(T.NI[:], T.IC[:, 16:144], T.PC[:, 3:4], A.is_equal, "IC PC3", "NI", s2=-1.0, o1=A.mult, c=128)
    ts(T.PC[:, 6:7], T.PJ[:, 0:1], 16.0, A.add, "PJ0", "PC6")
    ms(T.T1[:], 2560.0, "T1c T1_0 T1_1")
    cp(T.BL[:], T.IC[:, 0:12], "IC", "BL"); ms(T.BL[:, 0:12:2], 12, "BL")
    for x in range(4):
        c = slice(512 * x, 512 * x + 512)
        pool(lambda q, c=c, x=x: q.affine_select(T.SEL[:, c], T.ONES[:], [[-1, 4], [-16, 8], [0, 16]], A.is_equal, 0.0, -4 * x, 1),
             "ONES", "SEL%d" % x, 512)
        pool(lambda q, c=c: q.affine_select(T.DD[:, c], T.SEL[:, c], [[0, 4], [-16, 8], [-1, 16]], A.not_equal, -1.0, 0, 1),
             "SEL%d" % x, "DD%d" % x, 512)
    pool(lambda q: q.affine_select(T.SE2[:], T.SEL[:, 0:1024], [[-1, 8], [-16, 8], [0, 16]], A.not_equal, 1.0, -8, 1), "SEL0 SEL1", "SE2", 1024)
    ts(T.PJ[:, 5:6], T.PI[:, 0:1], 3, A.arith_shift_right, "PI", "PJ5", s2=1, o1=A.bitwise_and)
    cp(T.PC[:, 14:15], T.PJ[:, 5:6], "PJ5", "PC14")
    ts(T.PC[:, 13:14], T.PJ[:, 5:6], -1.0, A.mult, "PJ5", "PC13", s2=1.0, o1=A.add)
    for h in range(2):
        ts(T["P8%d" % h][:], T.IC[:], T.PC[:, 3:4], A.is_equal, "IC PC3 PC%d" % (13 + h), "P8%d" % h, s2=T.PC[:, 13 + h:14 + h], o1=A.mult, c=160)
    for x in range(8):
        ms(T.DD[:, 16 * x:16 * x + 129 * 15 + 1:129], 0.0, "DDz%d" % x, r="DD0 DD1 DD2 DD3")
    DDN = " ".join("DDz%d" % x for x in range(8))

    def keys(s):
        tt(T.K1[:], T.OT[:, 24 * s:24 * s + 24], T.KA[:], A.mult, "OT%d KA0 KA1" % s, "Ka")
        tt(T.K2[:], T.K1[:], T.KB[:], A.add, "Ka KB0 KB1", "Kb")
        ts(T.K3[:], T.K2[:], NC - 1, A.bitwise_and, "Kb", "K3")
        cp(T.KO[:], T.K3[:], "K3", "KO")

    def cands(s):
        for d in (1, 0):
            c = slice(L * d, L * d + L)
            win = T.CT[:, NW * d + 16:NW * d + NW].indirect(T.KO[:, 12 * d:12 * d + 12])
            cp(T.CO[:, c], win, "CT%d KO" % d, "CO%d" % d, k=L)
            tt(T.DF[:, c], win, T.EN[:, s, c], A.subtract, "CT%d KO EN%d_%d" % (d, s, d), "DF%d" % d, k=L)

    def entrants(s):
        for d in (1, 0):
            c = slice(384 * s + L * d, 384 * s + L * d + L)
            cp(T.ENO[:, c], T.EN[:, s, L * d:L * d + L], "EN%d_%d" % (s, d), "ENO%d_%d" % (s, d), c=L)
            ts(T.ENS[:, c], T.ENO[:, c], -1536.0, A.add, "ENO%d_%d" % (s, d), "ENS%d_%d" % (s, d), c=96)

    def spread(name, s, ds, sem):
        a, b = L * ds[0], L * ds[-1] + L
        for x in range(8):
            p = slice(16 * x, 16 * x + 16)
            dma("s", T[name + "M"][p, x, a:b], T["%s%d" % (name, s)][p, a:b],
                "VMz " + (" ".join("U%d_%d" % (s, d) for d in ds) if name == "U" else "V%d" % s),
                " ".join("%sM%d_%d" % (name, d, x) for d in ds), sem, 128)

    def spread_now(s, d):
        for x in range(8):
            o, src, m = T.UM[:, x, L * d:L * d + L], T["U%d" % s][:, L * d:L * d + L], T.ONE[:, 16 * x:16 * x + 1]
            ts(o, src, m, A.mult, "VMz ONE U%d_%d" % (s, d), "UM%d_%d" % (d, x), c=96,
               alt=lambda q, o=o, src=src, m=m: q.activation(o, src, F.Copy, scale=m), ca=L)

    def vsend(s):
        tt(T["VO%d" % s][:], TE_.indirect(T.OO[:, 0:24]), T.EP[:], A.mult, "TBE OO0 OO1 EP0 EP1", "VO%d" % s, k=384)
        send("VO%d" % s, [(nxt, T["VO%d" % s][:, 0:L], T["V%d" % s][:, L:384], "arV%d" % s, 0, 8),
                          (prv, T["VO%d" % s][:, L:384], T["V%d" % s][:, 0:L], "arV%d" % s, 8, 16)])

    def usend(s):
        tt(T["UO%d" % s][:], TX_.indirect(T.OO[:, 0:24]), T.XP[:], A.mult, "TBX OO0 OO1 XP0 XP1", "UO%d" % s, k=384)
        send("UO%d" % s, [(nxt, T["UO%d" % s][:, 0:L], T["U%d" % s][:, L:384], "arU%d" % s, 0, 8),
                          (prv, T["UO%d" % s][:, L:384], T["U%d" % s][:, 0:L], "arU%d" % s, 8, 16)])
        spread_now(s, 1)
        spread("U", s, (0,), "spU%d" % s)

    keys(0)
    entrants(0)
    cands(0)
    spread_now(0, 1)
    tt(T.UO0[:, L:384], TX_.indirect(T.OO[:, 12:24]), T.XP[:, L:384], A.mult, "TBX OO1 XP1", "UO0_1", k=L)
    send("UO0_1", [(prv, T.UO0[:, L:384], T.U0[:, 0:L], "arU0h", 0, 16)])
    spread("U", 0, (0,), "spU0h")
    vsend(0)
    spread("V", 0, (0, 1), "spV0")
    entrants(1)
    entrants(2)

    def names(pat, xs):
        return " ".join(pat % x for x in xs)

    def sides(xs):
        return sorted(set(x // 3 for x in xs))

    def gather(out, src, r, w, which):
        cp(out, src, r, w, k=1024, either=True)

    def scores(s, x, slot):
        a, d = 64 * x, x // 3
        gather(T.XG[:, 32 * a:32 * a + 2048:2], TX_.indirect(T.ENO[:, 384 * s + a:384 * s + a + 64]), "TBX ENO%d_%d" % (s, d),
               "XG%d_0" % x, (s, x, 0))
        gather(T.XG[:, 32 * a + 1:32 * a + 2048:2], TX_.indirect(T.CO[:, a:a + 64]), "TBX CO%d" % d, "XG%d_1" % x, (s, x, 1))
        P, bk, more = ((lambda p, c: T.S0[p, c], "b0", ""), (lambda p, c: T.WL[p, 3, c], "b1", ""),
                       (lambda p, c: T.KP[p, c], "b2", " K0"))[(x & 1) * (1 + s // 2)]
        for q4 in range(4):
            mms([(P(slice(32 * q4, 32 * q4 + 32), slice(j, 128, 16)), T.XG[:, 32 * l:32 * l + 32], T.UM[:, :, l], True, True)
                 for j in range(16) for l in [a + 16 * q4 + j]], "XG%d_0 XG%d_1 " % (x, x) + names("UM%d_%%d" % d, range(8)),
                "sc%s_%d" % (bk, q4) + more, bk, 32)
        o, src = T.SCP[:, 128 * x:128 * x + 128], P(slice(0, 128), slice(0, 128))
        ts(o, src, 64.0, A.mult, names("sc%s_%%d" % bk, range(4)) + " PC8", "SCP%d" % x, bk, s2=T.PC[:, 8:9], o1=A.add, c=128,
           alt=lambda q: q.activation(o, src, F.Identity, bias=T.PC[:, 8:9], scale=64.0))
        mms([(T.B3[:, 2 * slot:2 * slot + 2, :, :], o, T.IDD[:], True, True)], "SCP%d IDD" % x, "D%d" % slot, "b3", 256)
        if s < S - 1:
            mms([(T.KP[:, 128 * slot:128 * slot + 128], o, T.IDF[:], True, True)], "SCP%d IDF" % x, "K%d" % slot, "b2", 512)

    def contest(s, xs):
        m, a = len(xs), 64 * xs[0]
        c, c4 = slice(a, a + 64 * m), a // 16
        ts(T.LB[:, c], T.B3[:, 0:2 * m, :, :], 0.0, A.is_gt, names("D%d", range(m)), names("LB%d", xs), "b3", c=64 * m,
           alt=lambda q: q.activation(T.LB[:, c], T.B3[:, 0:2 * m, :, :], F.Sigmoid, scale=128.0))
        op("v", lambda q: q.transpose(T.LT[:, c4:c4 + 4 * m, :], T.LB[:, c]), names("LB%d", xs), names("LT%d", xs), "", vns(32 * m, 0))
        lo = T.B3[:, 6:6 + 2 * m, :, :]
        mms([(T.B3[:, 6:6 + 2 * m, h, :], T["PW%d" % h][:, o:o + 128], T.LT[:, c4 + g2:c4 + 4 * m:2, :], g2 == 0, g2 == 1)
             for h in range(2) for g2 in range(2) for o in [16 + 16 * (h - g2)]], "PW0 PW1 " + names("LT%d", xs), "lo", "b3", max(64, 32 * m))
        tt(lo, lo, T.DF[:, c], A.mult, "lo " + names("DF%d", sides(xs)), "lo", "b3", c=64 * m)
        tt(T.AL[:, c], lo, T.ENS[:, 384 * s + a:384 * s + a + 64 * m], A.add, "lo " + names("ENS%d_%%d" % s, sides(xs)),
           names("AL%d", xs), "b3", c=64 * m)
        ts(T.AO[:, c], T.AL[:, c], 1536.0, A.add, names("AL%d", xs), names("AO%d", xs), c=32 * m)
        for x in xs:
            EG = T["EG%d" % (s & 1)]
            if (s, x) in HALVES:
                for y in (2 * x, 2 * x + 1):
                    cp(EG[:, 512 * y:512 * y + 512], TE_.indirect(T.AO[:, 32 * y:32 * y + 32]), "TBE AO%d" % x, "EG%d_%d" % (s & 1, y),
                       either=True, k=512)
            else:
                cp(EG[:, 1024 * x:1024 * x + 1024], TE_.indirect(T.AO[:, 64 * x:64 * x + 64]), "TBE AO%d" % x,
                   names("EG%d_%%d" % (s & 1), (2 * x, 2 * x + 1)), either=True, k=1024)

    def best(s, d):
        MS, RX, c, h = T["MS%d" % s], T["RX%d" % s], slice(L * d, L * d + L), slice(12 * d, 12 * d + 12)
        top = T.SK[:, 384 * d + 31:384 * d + 384:32]
        scan(T.SK[:, 384 * d:384 * d + 384], T.RM[:], T.KP[:, 0:384], A.add, A.max, "RM K0 K1 K2", "SK%d" % d, "b2", 384)
        ki, kn = (T.KI[:], "KI") if d else (MS[:, 0, :], "MK%d" % s)
        cp(ki, top, "SK%d" % d, kn)
        if d:
            ts(MS[:, 3, :], ki, 2 * KEY0 - 64, A.bitwise_and, kn, "MF%d" % s)
            send("MF%d" % s, [(prv, MS[:, 3, :], RX[:, 1, :], "arF%d" % s, 0, 16)])
        else:
            send(kn, [(nxt, MS[:, 0, :], RX[:, 3, :], "arK%d" % s, 0, 16)])
            tt(T.MI[:, h], top, RX[:, 1, :], A.is_ge, "SK0 RXF%d" % s, "MI0")
            ts(T.LM[:], T.MI[:, h], -40.0, A.mult, "MI0", "LM", s2=40.0, o1=A.add)
        ts(T.KL[:, h], ki, 63, A.bitwise_and, kn, "KL%d" % d)
        if d == 0:
            tt(T.KL[:, h], T.KL[:, h], T.MI[:, h], A.mult, "KL0 MI0", "KL0")
        cp(T.KS[:, h], T.KL[:, h], "KL%d" % d, "KS%d" % d)
        tt(T.YB[:, c], T.IT[:, 0:64].indirect(T.KS[:, h]), T.AL[:, c], A.mult, "IT KS%d " % d + names("AL%d", range(3 * d, 3 * d + 3)),
           "YB%d" % d, k=L)

    def entity(s, d):
        MS, RX, c, h = T["MS%d" % s], T["RX%d" % s], slice(L * d, L * d + L), slice(12 * d, 12 * d + 12)
        cv = T.WL[:, 0, 16 * d:16 * d + 12]
        mms([(cv, T.NI[:], T.LM[:], True, False)][d:] +
            [(cv, T.W[:, 15 - j:143 - j], T.YB[:, L * d + j:L * d + L:16], d == 1 and j == 0, j == 15) for j in range(16)],
            "W YB%d" % d + " NI LM" * (1 - d), "cv%d" % d, "b1", 64)
        if d == 0:
            cp(T.B16[:, h], cv, "cv0", "B16_0", "b1")
            ts(T.T1[:, 0:12], cv, 64.0, A.mult, "cv0", "T1_0", "b1", s2=1536.0 + NC, o1=A.add)
        ts(MS[:, 1 + d, :], cv, 64.0, A.mult, "cv%d" % d, "MB%d_%d" % (s, d), "b1", s2=1536.0 + NC, o1=A.add)
        if d:
            send("MB%d_1" % s, [(prv, MS[:, 2, :], RX[:, 0, :], "arT%d" % s, 0, 16)])
        else:
            send("MB%d_0" % s, [(nxt, MS[:, 1, :], RX[:, 2, :], "arB%d" % s, 0, 16)])
        ts(T.BO[:, h], cv, 64.0, A.mult, "cv%d" % d, "BO%d" % d, "b1", s2=1536.0, o1=A.add)
        tt(T.XS[:, c], TX_.indirect(T.BO[:, h]), T.SG[:, c], A.subtract, "TBX BO%d SG%d" % (d, d), "XS%d" % d, k=L)
        ts(T.XS[:, c], T.XS[:, c], -7.0, A.max, "XS%d" % d, "XS%d" % d, s2=7.0, o1=A.min, c=96)

    def firsts(src, nm, outs, whole, bk, out, on, m):
        mms([(outs(15 - j), T.DD[:, 128 * j:128 * j + 128], src, True, True) for j in range(16)], DDN + " " + nm, on[1], bk, 64)
        scan(out, whole, T.DM[:, 0:m], A.mult, A.add, on[1] + " DM", on[0], bk, m)

    def targets(s, d):
        MS, RX, c, h = T["MS%d" % s], T["RX%d" % s], slice(L * d, L * d + L), slice(12 * d, 12 * d + 12)
        if d:
            tt(T.MI[:, h], MS[:, 3, :], RX[:, 3, :], A.is_gt, "MF%d RXK%d" % (s, s), "MI1")
            tt(T.T1[:, 16:28], MS[:, 2, :], T.MI[:, h], A.mult, "MB%d_1 MI1" % s, "T1_1")
            ts(T.B16[:, h], T.T1[:, 16:28], 1.0 / 64, A.mult, "T1_1", "B16_1", s2=-40.0, o1=A.add)
        t1, nd = T.T1[:, 16 * d:16 * d + 12], T.ND[:, 24 * d:24 * d + 24]
        ts(T.BR[:], T.T1[:, 16 * d:16 * d + 16].indirect(T.BL[:, 0:12]), 1.0 / 64, A.mult, "T1c BL T1_%d" % d, "BR", s2=-40.0, o1=A.add, k=L)
        mms([(T.S0[:, 143 - j:320:16], T.DD[:, 128 * j:128 * j + 128], T.B16[:, h], True, True) for j in range(16)],
            DDN + " B16_%d" % d, "dd", "b0", 64)
        mms([(T.S0[:, 320:512], T.NI[:], T.BR[:], True, False)] +
            [(T.S0[:, 336 + j:512:32], T.SEL[:, 128 * j:128 * j + 128], T.B16[:, 12 * d:12 * d + 12:2], False, j == 15) for j in range(16)],
            "SEL0 SEL1 SEL2 SEL3 NI BR B16_%d" % d, "de", "b0", 72)
        scan(T.SD[:], T.S0[:, 128:512], T.DN[:], A.mult, A.add, "dd de DN", "SD", "b0", 384)
        ts(nd, T.SD[:, 15:384:16], 0.0, A.not_equal, "SD", "ND%d" % d)
        tt(T.T2[:, h], T.ND[:, 24 * d:24 * d + 12], t1, A.mult, "ND%d T1_%d" % (d, d), "T2_%d" % d)
        tt(T.T2[:, h], T.T2[:, h], T.ND[:, 24 * d + 12:24 * d + 24], A.mult, "ND%d T2_%d" % (d, d), "T2_%d" % d)
        for o in range(2):
            ts(T.SO[:, 12 * d + o:12 * d + 12:2], T.T2[:, 12 * d + o:12 * d + 12:2], 32.0 - NC, A.add, "T2_%d PC0 PC6" % d, "SO%d_%d" % (d, o),
               s2=T.PC[:, 6 * o:6 * o + 1], o1=A.max)

    def write(e, d):
        for c in range(6 * d + 5, 6 * d - 1, -1):
            at, p = T.SO[:, 2 * c:2 * c + 2], slice(32 * c, 32 * c + 32)
            if e:
                tt(T.TB[:, 0:EO].indirect(at), T.E7[:, p], T.WV[:, p], A.add, "SO%d_0 SO%d_1 d0 E7 WV" % (d, d), "TBE", k=-32)
            else:
                cp(T.XB[:, 0:EO].indirect(at), T.XS[:, p], "SO%d_0 SO%d_1 d1 XS%d" % (d, d, d), "TBX", k=-32)

    def proposals(s):
        V, Z = T["V%d" % s], T.KP[:, 0:384]
        tt(T.EV[:], TE_.indirect(T.BO[:, 0:24]), V[:], A.mult, "TBE BO0 BO1 V%d" % s, "EV", k=384)
        mms([(Z, T.ONE[:], T.EV[:], True, True)], "ONE EV", "K0 K1 K2", "b2", 1536)
        act(T.E7[:], TE_.indirect(T.BO[:, 0:24]), F.Copy, "TBE BO0 BO1", "E7", scale=0.875, k=384)
        act(Z, Z, F.Sigmoid, "K0", "K0 K1 K2", "b2", scale=0.5, c=384)
        tt(T.WV[:], Z, V[:], A.mult, "V%d K0" % s, "WV", "b2", c=384)

    def cache_targets():
        ts(T.K16[:], T.K3[:], 16.0, A.add, "K3", "K16", s2=1.0 / 64, o1=A.mult)
        firsts(T.K16[:], "K16", lambda i: T.S0[:, 128 + i:512:16], T.S0[:, 128:512], "b0", T.SE[:], ("SE", "dd de"), 384)
        ts(T.NE[:], T.SE[:, 15:384:16], 0.0, A.not_equal, "SE", "NE")
        tt(T.C2[:], T.NE[:], T.K16[:], A.mult, "NE K16", "C2")
        ts(T.CSO[:, 0:48:2], T.C2[:], 64.0, A.mult, "C2 PC0", "CSO", s2=T.PC[:, 0:1], o1=A.max)

    def cache_write(d):
        for c in range(12 * d + 11, 12 * d - 1, -1):
            cp(T.CT[:, NW * d:NW * d + NW].indirect(T.CSO[:, 2 * c:2 * c + 1]), T.AO[:, 16 * c:16 * c + 16],
               "CSO AO%d d2 d3" % (c // 4), "CT%d" % d, k=-16)

    def triples(s):
        MS, RX, a, b = T["MS%d" % s], T["RX%d" % s], slice(24 * s, 24 * s + 24), slice(24 * s + 24, 24 * s + 48)
        tt(T.DO[:], MS[:, 1:3, :], T.OW[:, a], A.subtract, "MB%d_0 MB%d_1 OW%d" % (s, s, s), "DO")
        tt(T.T3[:], T.OT[:, a], RX[:, 0:3:2, :], A.subtract, "OT%d RXT%d RXB%d" % (s, s, s), "T3")
        tt(T.T4[:], T.MI[:], T.T3[:], A.mult, "MI0 MI1 T3", "T4")
        tt(T.OT[:, b], T.T4[:], RX[:, 0:3:2, :], A.add, "T4 RXT%d RXB%d" % (s, s), "OT%d" % (s + 1))
        tt(T.T5[:], T.MI[:], T.DO[:], A.mult, "MI0 MI1 DO", "T5")
        keys(s + 1)
        tt(T.OW[:, b], T.T5[:], T.OW[:, a], A.add, "T5 OW%d" % s, "OW%d" % (s + 1))
        ts(T.OO[:], T.OW[:, b], -float(NC), A.add, "OW%d" % (s + 1), "OO0 OO1")

    turns = [0, 0]

    def output(s, xs):
        EG, na, l0 = T["EG%d" % (s & 1)], 2 * len(xs), 64 * xs[0]
        y = turns[0] & 1
        turns[0] += 1
        WS, eg, m0, rows = T["WS%d" % y], names("EG%d_%%d" % (s & 1), xs), l0 // 16, slice(0, 32 * na)
        ms_ = slice(m0, m0 + 2 * na)
        w0 = m0 // 2
        Wp = T.WP[:, w0:w0 + na, :, :]
        twice = (s, xs[0]) not in RECIP
        vm = " ".join(names("VM%d_%%d" % d, range(8)) for d in sides(xs))

        def fetch(o, src, r, w, bk, c):
            if twice:
                cp(o, src, r, w, bk, either=True, c=c)
            else:
                act(o, src, F.Sigmoid, r, w, bk, scale=0.5, c=c)

        if (s, xs[0]) in WIDE:
            for b in range(2):
                Z, bk = T.ZP, "b5"
                for j2 in range(2):
                    mms([(Z[:, j % 8:64:8, :], EG[:, 16 * l:16 * l + 128], T.VM[:, :, l:l + 8], True, True)
                         for j in range(8 * b + 4 * j2, 8 * b + 4 * j2 + 4) for l in [l0 + 8 * j]],
                        "EG%d_%d " % (s & 1, 2 * xs[b] + j2) + vm, "z%s_%d" % (bk, j2), bk, 256)
                four = [(WS[32 * a:32 * a + 32, :, 16 * b:16 * b + 16], Z[32 * a:32 * a + 32, :, 2 * a:2 * a + 2]) for a in range(4)]
                op("v", lambda q, four=four: [q.tensor_copy(o, i) for o, i in four][-1], "z%s_0 z%s_1" % (bk, bk),
                   names("WS%d_%%d" % y, range(4 * b, 4 * b + 4)), bk, 4 * vns(128, 0),
                   alt=(lambda q, four=four: [q.activation(o, i, F.Copy) for o, i in four][-1], 4 * ans(128, 0)))
        else:
            for j4 in range(4):
                mms([(T.ZP[32 * a:32 * a + 32, 32 * y + j // 4:32 * y + 32:4, 2 * (j % 4):2 * (j % 4) + 2], EG[:, 16 * l:16 * l + 32],
                      T.VM[:, :, l:l + 2], True, True) for j in range(4 * j4, 4 * j4 + 4) for a in range(na)
                     for l in [l0 + 2 * na * j + 2 * a]], "EG%d_%d " % (s & 1, 2 * xs[0] + j4 * len(xs) // 2) + vm, "zb5_%d" % j4, "b5", 128)
            fetch(WS[rows, :, :], T.ZP[rows, 32 * y:32 * y + 32, :], names("zb5_%d", range(4)), names("WS%d_%%d" % y, range(8)), "b5", 256)
        wn, rn = names("Wp%d", xs), names("R%%s%d", xs)
        mms([(T.WP[:, w0:w0 + na, h, :], WS[rows, :, h:32:2], T.IDF[rows, 0:na, h, :], True, True) for h in range(2)],
            "IDF " + names("WS%d_%%d" % y, range(8)), wn, "b4", 256)
        q1 = T.RW[:, ms_, 1:16]
        if twice:
            act(q1, T.WP[:, w0:w0 + na, :, 1:16], F.Sigmoid, wn + " PC7", rn.replace("%s", "W"), "b4", bias=T.PC[:, 7:8], scale=-0.5, c=30 * na)
            act(Wp, Wp, F.Sigmoid, wn, wn, "b4", scale=0.5, c=32 * na)
            ts(q1, q1, E16, A.mult, rn.replace("%s", "W"), rn.replace("%s", "W"), s2=1.0, o1=A.add, c=30 * na,
               alt=lambda q: q.activation(q1, q1, F.Identity, bias=1.0, scale=E16))
        else:
            op("v", lambda q: q.reciprocal(q1, T.WP[:, w0:w0 + na, :, 1:16]), wn, rn.replace("%s", "W"), "b4", 190 + 6 * CYC * 30 * na)
        tt(Wp, Wp, T.RW[:, ms_, 1:17], A.mult, wn + " RWc " + rn.replace("%s", "W"), wn, "b4", c=32 * na)
        cp(T.RH[:, ms_, 1:17], Wp, wn, rn.replace("%s", "H"), "b4", either=True, c=32 * na)
        tt(T.RO[:, ms_, 1:17], Wp, T.RH[:, ms_, 1:17], A.subtract, wn + " " + rn.replace("%s", "H"), rn.replace("%s", "O"), "b4", c=32 * na)
        k, wide, stack = 16 // na, 32 * na, (s, xs[0]) in STACK
        both = "RHc ROc " + rn.replace("%s", "H") + " " + rn.replace("%s", "O")
        if stack:
            for h, o in enumerate((Wp, T.WP[:, 12:16, :, :])):
                mms([(o, T["P8%d" % h][:, 16 + 8 * (h - i):144 + 8 * (h - i)], T[x][:, ms_, 0:16], i == 0, i == 1)
                     for i, x in enumerate(("RH", "RO"))], "P80 P81 " + both, (wn, "Wx")[h], "b4", 128)
                op("v", lambda q, h=h, o=o: q.tensor_copy(T["TS%d" % y][:, 128 * h:128 * h + 128], o), (wn, "Wx")[h], "TS%d_%d" % (y, h), "b4",
                   vns(128, 0))
        for j in range(0, 16, k):
            p = turns[1] & 1
            turns[1] += 1
            RB, a = T["RB%d" % p], l0 + 2 * na * j
            if stack:
                mms([(RB[:, 128 * i:128 * i + 128], T.SE2[:, 128 * ((j + i) % 8):128 * ((j + i) % 8) + 128],
                      T["TS%d" % y][:, 128 * (j // 8):128 * (j // 8) + 128], True, True) for i in range(k)],
                    "SE2 TS%d_%d" % (y, j // 8), "rb%d" % p, "r%d" % p, 128)
            else:
                mms([(RB[:, wide * i:wide * i + wide], T.SEL[:, 128 * (j + i):128 * (j + i) + 128], T[x][:, ms_, 0:16], x == "RH", x == "RO")
                     for i in range(k) for x in ("RH", "RO")], "SEL0 SEL1 SEL2 SEL3 " + both, "rb%d" % p, "r%d" % p, wide)
            scan(T.GS[:, 16 * a:16 * a + 512], RB[:], EG[:, 16 * a:16 * a + 512], A.mult, A.add,
                 "rb%d EG%d_%d" % (p, s & 1, a // 32), "GS%d" % (a // 32), "r%d" % p, 512)

    def gather_up(s, xs, na):
        a, b, w = 64 * xs[0], 64 * xs[-1] + 64, 2 * na
        flat = T.WL[:, a // 128, a % 128:a % 128 + b - a] if b - a <= 128 else T.WL[:, a // 128:b // 128, :]
        m = (b - a) // 16
        mms([(T.WL[:, a // 128, m * h:m * h + m], T["P8%d" % h][:, 16 + 8 * (h - i):144 + 8 * (h - i)], T[x][:, a // 16:b // 16, 16], i == 0, i == 1)
             for h in range(2) for i, x in enumerate(("RH", "RO"))], "P80 P81 " + names("RH%d", xs) + " " + names("RO%d", xs), "wl%d" % xs[0], "b1", 64)
        op("v", lambda q: q.tensor_copy(T.TW[:, 0:2 * m], T.WL[:, a // 128, 0:2 * m]), "wl%d" % xs[0], "TW", "b1", vns(0, 0))
        mms([(T.WL[:, a // 128:(b + 127) // 128, a % 128 + w * j:a % 128 + w * j + w], T.SE2[:, 128 * (j % 8):128 * (j % 8) + 128],
              T.TW[:, m * (j // 8):m * (j // 8) + m], True, True) for j in range(16)], "SE2 TW", names("wl%d", xs), "b1", 64)
        gs = names("wl%d", xs) + " " + names("GS%d", range(a // 32, b // 32))
        last = T.GS[:, 16 * a + 15:16 * b:16]
        if s == 0:
            tt(T.ACC[:, a:b], flat, last, A.mult, gs, names("ACC%d", xs), "b1", c=b - a)
        else:
            tt(flat, flat, last, A.mult, gs, names("wl%d", xs), "b1", c=b - a)
            tt(T.ACC[:, a:b], flat, T.ACC[:, a:b], A.add, names("wl%d", xs) + " " + names("ACC%d", xs), names("ACC%d", xs), "b1", c=b - a)

    for s in range(S):
        step[0] = str(s)
        hint.update(HINTS[s])
        if s < S - 1:
            if s:
                cache_targets()
            for d in (1, 0):
                step[0] = str(s) + "ht"[d]
                c = slice(L * d, L * d + L)
                ts(T.SG[:, c], T["U%d" % s][:, c], -1.0, A.max, "U%d_%d" % (s, d), "SG%d" % d, s2=1.0, o1=A.min, c=96, ca=L,
                   alt=lambda q, c=c, s=s: q.activation(T.SG[:, c], T["U%d" % s][:, c], F.Sign))
                for x in range(3):
                    scores(s, 3 * d + x, x)
                if d == 0:
                    entity(s, 1)
                contest(s, range(3 * d, 3 * d + 3))
                best(s, d)
            entity(s, 0)
            step[0] = str(s)
            if s == 0:
                cache_targets()
            else:
                gather_up(0, range(6), 4)
            cache_write(1); cache_write(0)
            targets(s, 0); write(0, 0); targets(s, 1); write(0, 1)
            triples(s); cands(s + 1); usend(s + 1)
            proposals(s); write(1, 0); write(1, 1); vsend(s + 1)
            for xs in ((4, 5), (2, 3), (0, 1)):
                output(s, xs)
            if s:
                gather_up(s, range(6), 4)
            spread("V", s + 1, (0, 1), "spV%d" % (s + 1))
        else:
            for xs in LASTUNITS:
                for i, x in enumerate(xs):
                    scores(s, x, i)
                contest(s, xs)
                output(s, xs)
                if xs[0] in SUMS:
                    gather_up(s, range(xs[0], SUMS[xs[0]]), 2 * len(xs))
            dma("s", T.yt[:], T.ACC[:, L:384], "ACC3 ACC4 ACC5", "yt", "out1", 16)
            dma("s", T.yh[:], T.ACC[:, 0:L], "ACC0 ACC1 ACC2", "yh", "out0", 16)

    if "order" not in _ORDER:
        _ORDER["order"], _ORDER["time"] = _order(ops, raised)
        _ORDER["ops"] = (ops, raised)
    order = _ORDER["order"]
    on = dict(order)
    place = {i: k for k, (i, e) in enumerate(order)}
    need, seen = set(), {e: {} for e in Q}
    for i, e in order:
        last_of = {}
        for x in ops[i][2]:
            if x[0] == "e":
                last_of[on[x[1]]] = max(last_of.get(on[x[1]], -1), place[x[1]])
        for e2, k in last_of.items():
            if k > seen[e].get(e2, -1):
                seen[e][e2] = k
                need.add(order[k][0])
    num, tot = {}, {e: 0 for e in Q}
    for i, e in order:
        tot[e] += i in need
        num[i] = tot[e] if i in need else 0
    seen = {e: {} for e in Q}
    for i, e in order:
        f, deps, d = ops[i][1][e], ops[i][2], ops[i][3]
        want = {}
        for x in deps:
            sem, val = (CNT[on[x[1]]], num[x[1]]) if x[0] == "e" else (x[1], x[2])
            want[sem] = max(want.get(sem, 0), val)
        for sem in sorted(want):
            if want[sem] > seen[e].get(sem, 0):
                seen[e][sem] = want[sem]
                Q[e].wait_ge(T.sem[sem], want[sem])
        ins = f(Q[e])
        if d and d[1]:
            ins.then_inc(T.sem[d[0]], 16)
        elif i in need:
            ins.then_inc(T.sem[CNT[e]], 1)
    g.wait_ge(T.sem.sent, sent[0])
    g.wait_ge(T.sem.out1, 16)
    g.wait_ge(T.sem.out0, 16)
